import numpy as np
import ml_dtypes


def mxq(x, axis, fmt="e4m3"):
    dtype, down = {"e4m3": (ml_dtypes.float8_e4m3fn, 7), "e5m2": (ml_dtypes.float8_e5m2, 14)}[fmt]
    v = np.moveaxis(np.asarray(x, np.float32).astype(ml_dtypes.bfloat16).astype(np.float64), axis, -1)
    blocks = v.reshape(v.shape[:-1] + (-1, 32))
    amax = np.abs(blocks).max(-1, keepdims=True)
    byte = np.maximum(np.where(amax > 0, np.frexp(amax)[1] - 1 + 127, 0) - down, 1)
    scale = np.exp2(byte - 127.0)
    codes = (blocks / scale).astype(np.float32).astype(dtype).astype(np.float64)
    return np.moveaxis((codes * scale).reshape(v.shape), -1, axis)


WIDE = False


def mx_kscale(k):
    if not WIDE:
        return np.ones(k)
    levels = np.array([10, -10, 5, -5, 0])
    if k % 512:
        return np.exp2(np.random.permutation(np.resize(levels, k // 32))).repeat(32)
    a = np.empty((k // 512, 16))
    for p in range(k // 512):
        a[p, :8] = np.random.permutation(np.resize(levels, 8))
        for g in range(8):
            far = levels[np.abs(levels - a[p, g]) >= 10]
            a[p, g + 8] = far[np.random.randint(len(far))]
    return np.exp2(a.ravel()).repeat(32)


def f64(x):
    return np.asarray(x).astype(np.float64)


def striped(idx):
    return np.tile(idx.reshape(-1, 16).T, (8, 1)).astype(np.uint16)


def unstriped(offs):
    return offs[:16].T.reshape(-1).astype(np.int64)


E2M1 = np.array([0.0, 0.5, 1.0, 1.5, 2.0, 3.0, 4.0, 6.0, -0.0, -0.5, -1.0, -1.5, -2.0, -3.0, -4.0, -6.0])


def pack_weight(w, fmt):
    k, n = w.shape
    w = f64(np.asarray(w, np.float32).astype(ml_dtypes.bfloat16)).reshape(k // 32, 32, n)
    amax = np.abs(w).max(1)
    if fmt == "e4m3":
        byte = np.frexp(amax)[1] - 1 + 127 - 7
    else:
        mant, ex = np.frexp(amax / 6.0)
        byte = np.where(mant > 0.5, ex, ex - 1) + 127
    byte = np.clip(np.where(amax > 0, byte, 1), 1, 254)
    scaled = (w * np.exp2(127.0 - byte)[:, None, :]).reshape(k, n).astype(np.float32)
    by_word = np.ascontiguousarray(scaled.reshape(k // 512, 128, 4, n).transpose(0, 1, 3, 2))
    if fmt == "e4m3":
        words = by_word.astype(ml_dtypes.float8_e4m3fn).view(np.uint8)
    else:
        c = by_word.astype(ml_dtypes.float4_e2m1fn).view(np.uint8) & 0xF
        words = (c[..., 0::2] | (c[..., 1::2] << 4)).reshape(k // 512, 128, 2 * n)
    return np.ascontiguousarray(words), np.ascontiguousarray(byte.astype(np.uint8).reshape(k // 512, 16, n))


def unpack_weight(words, scales, fmt):
    g, _, n = scales.shape
    words = np.ascontiguousarray(words).reshape(g, 128, n, -1)
    if fmt == "e4m3":
        vals = words.view(ml_dtypes.float8_e4m3fn).astype(np.float64)
    else:
        nib = np.empty((g, 128, n, 4), np.uint8)
        nib[..., 0::2] = words & 0xF
        nib[..., 1::2] = words >> 4
        vals = E2M1[nib]
    vals = vals * np.repeat(np.exp2(scales.astype(np.float64) - 127.0), 8, axis=1)[..., None]
    return vals.transpose(0, 1, 3, 2).reshape(g * 512, n)


def gelu(v):
    return 0.5 * v * (1.0 + np.tanh(np.sqrt(2.0 / np.pi) * (v + 0.044715 * v**3)))


def striped8(idx):
    return np.concatenate([v.reshape(-1, 16).T for v in idx]).astype(np.uint16)


def unstriped8(offs):
    return np.stack([offs[16 * g:16 * g + 16].T.reshape(-1) for g in range(8)]).astype(np.int64)


def runs(v, idx8):
    k = np.arange(v.shape[0])
    return v[k[:, None], idx8[k % 512 // 64]]


K, K2, H, N, T, T2, S = 1024, 512, 1024, 512, 2048, 2048, 1024

def setup_inputs():
    n = np.random.standard_normal
    s = mx_kscale(K)[:, None]
    s2 = mx_kscale(K2)[:, None]
    u = mx_kscale(H)[:, None]
    tab_words, tab_scales = pack_weight(n((K, T)) * s, "e4m3")
    tab2_words, tab2_scales = pack_weight(n((K2, T2)) * s2, "e4m3")
    offs = striped8(np.stack([np.random.permutation(T)[:S] for _ in range(8)]))
    offs2 = striped(np.random.permutation(T2)[:S])
    w1_words, w1_scales = pack_weight(1.5 * n((K, H)) / np.sqrt(K) / s * u.T, "e2m1")
    w2 = (0.9 * n((K2, H)) / np.sqrt(K2) / s2).astype(np.float32)
    w3_words, w3_scales = pack_weight(1.5 * n((H, N)) / np.sqrt(H) / u, "e4m3")
    return {"tab_words": tab_words, "tab_scales": tab_scales, "offs": offs,
            "tab2_words": tab2_words, "tab2_scales": tab2_scales, "offs2": offs2,
            "w1_words": w1_words, "w1_scales": w1_scales, "w2": w2,
            "w3_words": w3_words, "w3_scales": w3_scales}

def reference(tab_words, tab_scales, offs, tab2_words, tab2_scales, offs2,
              w1_words, w1_scales, w2, w3_words, w3_scales):
    v = runs(unpack_weight(tab_words, tab_scales, "e4m3"), unstriped8(offs))
    v2 = unpack_weight(tab2_words, tab2_scales, "e4m3")[:, unstriped(offs2)]
    w1 = unpack_weight(w1_words, w1_scales, "e2m1")
    w3 = unpack_weight(w3_words, w3_scales, "e4m3")
    a = w1.T @ v
    b = mxq(f64(w2), 0, "e4m3").T @ v2
    e = np.exp(-np.square(b))
    h = a - a * e
    return w3.T @ mxq(h, 0, "e4m3")

@@ -1,0 +1,243 @@
+from contextlib import ExitStack
+
+import concourse.mybir as mybir
+
+K, K2, H, N, T, S = 1024, 512, 1024, 512, 2048, 1024
+FLOPS = 2 * S * (K * H + K2 * H + H * N)
+
+F32 = mybir.dt.float32
+BF16 = mybir.dt.bfloat16
+I32 = mybir.dt.int32
+U32 = mybir.dt.uint32
+U16 = mybir.dt.uint16
+U8 = mybir.dt.uint8
+FP8X4 = mybir.dt.float8_e4m3fn_x4
+FP4X4 = mybir.dt.float4_e2m1fn_x4
+ACT = mybir.ActivationFunctionType
+ALU = mybir.AluOpType
+
+P = 128
+PACK = 4
+PASS = P * PACK
+BLOCK = 256
+UNIT = 128
+BLOCKS = S // BLOCK
+COLS = BLOCK // 16
+LEAD = 4
+
+
+def tile_list_wake_correction_kernel(
+    tc, tab_words, tab_scales, offs, tab2_words, tab2_scales, offs2,
+    w1_words, w1_scales, w2, w3_words, w3_scales, out,
+):
+    nc = tc.nc
+    with ExitStack() as ctx:
+        keep = ctx.enter_context(tc.tile_pool(name="keep", bufs=1))
+        ring = ctx.enter_context(tc.tile_pool(name="ring", bufs=3))
+        psum = ctx.enter_context(tc.psum_pool(name="psum", bufs=1))
+
+        def held(shape, dtype, name, tag=""):
+            return keep.tile(shape, dtype, name=name, tag=tag or name, align_bytes=256)
+
+        list1 = keep.tile([P, S // 16], U16, name="list1")
+        list2 = keep.tile([P, S // 16], U16, name="list2")
+        v2_scale_rows = held([P, T], U8, "v2_scale_rows")
+        v_scale_rows = held([P, T], U8, "v_scale_rows")
+        w1_scale_rows = held([P, 2, H], U8, "w1_scale_rows")
+        w3_scale = held([P, 2, N], U8, "w3_scale")
+        v_scale1 = held([P, S], U8, "v_scale1")
+        for tile in (v2_scale_rows, w1_scale_rows, w3_scale, v_scale1):
+            nc.vector.memset(tile[:].bitcast(I32), 0)
+
+        nc.sync.dma_start(list2[:], offs2)
+        nc.sync.dma_start(list1[:], offs)
+        v2_rows = tab2_scales[0].rearrange("(d r) t -> r d t", r=4)
+        for r in range(4):
+            nc.scalar.dma_start(v2_scale_rows[r:P:32, :].bitcast(I32), v2_rows[r].bitcast(I32))
+        v_rows = tab_scales.rearrange("a q t -> q a t").bitcast(I32)
+        for a in range(2):
+            nc.sync.dma_start(
+                v_scale_rows[a:P:2, :].bitcast(I32), v_rows[:, a : a + 1, :].to_broadcast([16, 4, T // 4])
+            )
+        w1_rows = w1_scales.rearrange("a (d r) c -> r d a c", r=4)
+        for r in range(4):
+            nc.gpsimd.dma_start(w1_scale_rows[r:P:32, :, :].bitcast(I32), w1_rows[r].bitcast(I32))
+        w3_rows = w3_scales.rearrange("a (d r) c -> r d a c", r=4)
+        for r in range(4):
+            nc.gpsimd.dma_start(w3_scale[r:P:32, :, :].bitcast(I32), w3_rows[r].bitcast(I32))
+        w1_raw = held([P, 2, 2 * H], U8, "w1_raw")
+        w2_rows = w2.rearrange("(p j) c -> p j c", j=PACK)
+
+        def load_w2(c):
+            raw = ring.tile([P, PACK, 256], F32, name="w2_raw", bufs=2)
+            nc.sync.dma_start(raw[:], w2_rows[:, :, 256 * c : 256 * (c + 1)])
+            return raw
+
+        def load_table(words, name, tag):
+            window = held([P, T], I32, name, tag)
+            nc.sync.dma_start(window[:], words.rearrange("p t i -> p (t i)").bitcast(I32))
+            return window
+
+        w2_codes = [held([P, PASS], U32, f"w2_codes{g}") for g in range(2)]
+        w2_scale = [held([P, PASS], U8, f"w2_scale{g}") for g in range(2)]
+
+        def quantise_w2(g, raws):
+            grouped = held([P, PACK, P, PACK], BF16, f"w2_grouped{g}")
+            for c in range(2):
+                dst = grouped[:, :, 64 * c : 64 * (c + 1), :].rearrange("p t m j -> p m j t")
+                src = raws[c][:].rearrange("p j (m t) -> p m j t", t=PACK)
+                if g == 0:
+                    nc.scalar.activation(dst, src, ACT.Copy)
+                else:
+                    nc.vector.tensor_copy(dst, src)
+            nc.vector.quantize_mx(
+                out=w2_codes[g][:].bitcast(FP8X4),
+                scales=w2_scale[g][:],
+                in_=grouped[:].rearrange("p t m j -> p (t m j)"),
+            )
+
+        w1_codes = [held([P, 2, 2 * PASS], U8, f"w1_codes{g}") for g in range(2)]
+
+        def permute_w1_codes(g):
+            cols = slice(PASS * g, PASS * (g + 1))
+            nc.vector.tensor_copy(
+                w1_codes[g][:].bitcast(U16).rearrange("p a (t m) -> p a t m", t=PACK),
+                w1_raw[:].bitcast(U16)[:, :, cols].rearrange("p a (m t) -> p a t m", t=PACK),
+            )
+
+        def permute_w1_scale(g):
+            cols = slice(PASS * g, PASS * (g + 1))
+            nc.vector.tensor_copy(
+                w1_scale[:, g, :, :].rearrange("p a (t m) -> p a t m", t=PACK),
+                w1_scale_rows[:, :, cols].rearrange("p a (m t) -> p a t m", t=PACK),
+            )
+
+        def pick(window, offsets, block, name):
+            picked = held([P, BLOCK], U32, name)
+            nc.vector.tensor_copy(
+                picked[:], window[:].bitcast(U32).indirect(offsets[:, COLS * block : COLS * (block + 1)])
+            )
+            return picked
+
+        def gaussian(v2_codes, block, g):
+            squares = ring.tile([P, 2, UNIT, PACK], F32, name="squares")
+            for half in range(2):
+                bank = psum.tile([P, PACK, UNIT], F32, name="b_bank", tag="ab", bufs=6)
+                here = slice(UNIT * half, UNIT * (half + 1))
+                entries = slice(BLOCK * block + UNIT * half, BLOCK * block + UNIT * (half + 1))
+                for t in range(PACK):
+                    cols = slice(P * t, P * (t + 1))
+                    nc.tensor.matmul_mx(
+                        out=bank[:, t, :],
+                        lhsT=w2_codes[g][:, cols].bitcast(FP8X4),
+                        lhsT_scale=w2_scale[g][:, cols],
+                        rhs=v2_codes[:, here].bitcast(FP8X4),
+                        rhs_scale=v2_scale[:, entries],
+                        start=True,
+                        stop=True,
+                    )
+                nc.scalar.activation(squares[:, half, :, :], bank[:].rearrange("p t n -> p n t"), ACT.Square)
+            share = held([P, 2, UNIT, PACK], F32, f"share{block}_{g}")
+            nc.scalar.activation(share[:], squares[:], ACT.Exp, scale=-1.0)
+            return share
+
+        def corrected(v_codes, share, block, g):
+            minus_h = ring.tile([P, 2, UNIT, PACK], BF16, name="minus_h", align_bytes=256)
+            for half in range(2):
+                bank = psum.tile([P, PACK, UNIT], F32, name="a_bank", tag="ab", bufs=6)
+                here = slice(UNIT * half, UNIT * (half + 1))
+                entries = slice(BLOCK * block + UNIT * half, BLOCK * block + UNIT * (half + 1))
+                for t in range(PACK):
+                    for a in range(2):
+                        nc.tensor.matmul_mx(
+                            out=bank[:, t, :],
+                            lhsT=w1_codes[g][:, a, 2 * P * t : 2 * P * (t + 1)].bitcast(FP4X4),
+                            lhsT_scale=w1_scale[:, g, a, P * t : P * (t + 1)],
+                            rhs=v_codes[a][:, here].bitcast(FP8X4),
+                            rhs_scale=v_scale[a][:, entries],
+                            start=(a == 0),
+                            stop=(a == 1),
+                        )
+                nc.vector.scalar_tensor_tensor(
+                    out=minus_h[:, half, :, :],
+                    in0=share[:, half, :, :],
+                    scalar=1.0,
+                    in1=bank[:].rearrange("p t n -> p n t"),
+                    op0=ALU.subtract,
+                    op1=ALU.mult,
+                )
+            h_codes = ring.tile([P, BLOCK], U32, name="h_codes", align_bytes=256, bufs=4)
+            h_scale = ring.tile([P, BLOCK], U8, name="h_scale", align_bytes=256, bufs=4)
+            nc.vector.quantize_mx(
+                out=h_codes[:].bitcast(FP8X4),
+                scales=h_scale[:],
+                in_=minus_h[:].rearrange("p u n t -> p (u n t)"),
+            )
+            return h_codes, h_scale
+
+        def read_out(h, block):
+            for pair in range(2):
+                bank = psum.tile([P, 2, BLOCK], F32, name="out_bank", bufs=2)
+                for u in range(2):
+                    cols = slice(P * (2 * pair + u), P * (2 * pair + u + 1))
+                    for g in range(2):
+                        nc.tensor.matmul_mx(
+                            out=bank[:, u, :],
+                            lhsT=w3_codes[:, g, cols].bitcast(FP8X4),
+                            lhsT_scale=w3_scale[:, g, cols],
+                            rhs=h[g][0][:].bitcast(FP8X4),
+                            rhs_scale=h[g][1][:],
+                            start=(g == 0),
+                            stop=(g == 1),
+                        )
+                result = ring.tile([P, 2, BLOCK], F32, name="result")
+                if block == BLOCKS - 1 and pair == 1:
+                    nc.vector.tensor_scalar_mul(result[:], bank[:], -1.0)
+                else:
+                    nc.scalar.activation(result[:], bank[:], ACT.Copy, scale=-1.0)
+                rows = out[2 * P * pair : 2 * P * (pair + 1), BLOCK * block : BLOCK * (block + 1)]
+                nc.sync.dma_start(rows.rearrange("(u p) c -> p u c", p=P), result[:])
+
+        first_raws = [load_w2(c) for c in range(2)]
+        v2_words = load_table(tab2_words[0], "v2_words", "v2_words")
+        nc.sync.dma_start(w1_raw[:].bitcast(I32), w1_words.rearrange("a p c -> p a c").bitcast(I32))
+        v2_scale = held([P, S], U8, "v2_scale")
+        nc.vector.tensor_copy(v2_scale[:], v2_scale_rows[:].indirect(list2[:]))
+        quantise_w2(0, first_raws)
+        v2_codes = [pick(v2_words, list2, 0, "v2_codes0")]
+        v_scale_picked = held([P, S], U8, "v_scale_picked")
+        nc.vector.tensor_copy(v_scale_picked[:], v_scale_rows[:].indirect(list1[:]))
+        v_words = [load_table(tab_words[0], "v_words0", "v_scale_rows"), load_table(tab_words[1], "v_words1", "w2_grouped0")]
+
+        def place_v_scale(plane, a, rows):
+            for r in rows:
+                nc.sync.dma_start(plane[r:P:32, :].bitcast(I32), v_scale_picked[8 * r + a : P : 32, :].bitcast(I32))
+
+        place_v_scale(v_scale1, 1, range(4))
+        v2_codes.extend(pick(v2_words, list2, block, f"v2_codes{block}") for block in range(1, BLOCKS))
+        quantise_w2(1, [load_w2(c) for c in range(2, 4)])
+        for g in range(2):
+            permute_w1_codes(g)
+        v_scale0 = held([P, S], U8, "v_scale0", "w1_raw")
+        nc.vector.tensor_copy(v_scale0[:].bitcast(I32), v_scale_picked[:].bitcast(I32))
+        place_v_scale(v_scale0, 0, range(1, 4))
+        v_scale = [v_scale0, v_scale1]
+        w3_codes = held([P, 2, N], U32, "w3_codes", "w2_grouped1")
+        nc.sync.dma_start(w3_codes[:].bitcast(I32), w3_words.rearrange("a p c i -> p a (c i)").bitcast(I32))
+        w1_scale = held([P, 2, 2, PASS], U8, "w1_scale", "v2_words")
+        for g in range(2):
+            permute_w1_scale(g)
+        b_steps = [(block, g) for g in range(2) for block in range(BLOCKS)]
+        a_steps = [(0, 0), (1, 0), (0, 1), (1, 1), (2, 0), (2, 1), (3, 0), (3, 1)]
+        shares, v_codes, h = {}, {}, {}
+        for step in range(len(a_steps) + LEAD):
+            if step >= LEAD:
+                block, g = a_steps[step - LEAD]
+                if g == 0:
+                    v_codes[block] = [pick(v_words[a], list1, block, f"v_codes{block}_{a}") for a in range(2)]
+                h[block, g] = corrected(v_codes[block], shares[block, g], block, g)
+                if g == 1:
+                    read_out([h[block, 0], h[block, 1]], block)
+            if step < len(b_steps):
+                block, g = b_steps[step]
+                shares[block, g] = gaussian(v2_codes[block], block, g)

@@ -19,11 +19,12 @@ ALU = mybir.AluOpType
 P = 128
 PACK = 4
 PASS = P * PACK
+GROUPS = H // PASS
 BLOCK = 256
-UNIT = 128
 BLOCKS = S // BLOCK
-COLS = BLOCK // 16
-LEAD = 4
+UNIT = 128
+LIST_COLS = BLOCK // 16
+CHUNK = 256
 
 
 def tile_list_wake_correction_kernel(
@@ -39,205 +40,205 @@ def tile_list_wake_correction_kernel(
         def held(shape, dtype, name, tag=""):
             return keep.tile(shape, dtype, name=name, tag=tag or name, align_bytes=256)
 
+        def bank(shape, name, number):
+            return psum.tile(shape, F32, name=name, tag=f"bank{number}")
+
+        def load_table(words, name):
+            window = held([P, T], I32, name)
+            nc.sync.dma_start(window[:], words.rearrange("p t i -> p (t i)").bitcast(I32))
+            return window
+
+        def load_w2(first, width):
+            raw = held([P, PACK, width], F32, f"w2_raw{first}")
+            nc.sync.dma_start(raw[:], w2.rearrange("(p j) c -> p j c", j=PACK)[:, :, first : first + width])
+            return [raw[:, :, c : c + CHUNK] for c in range(0, width, CHUNK)]
+
+        def load_two_planes(tile, scales):
+            for d in range(4):
+                nc.sync.dma_start(
+                    tile[32 * d : 32 * d + 8, :].bitcast(I32), scales[:, 4 * d : 4 * d + 4, :].bitcast(I32)
+                )
+
+        def pick(windows, offsets, block, name, tag=""):
+            picked = held([P, len(windows), BLOCK], U32, name, tag)
+            entries = offsets[:, LIST_COLS * block : LIST_COLS * (block + 1)]
+            for a, window in enumerate(windows):
+                nc.vector.tensor_copy(picked[:, a, :], window[:].bitcast(U32).indirect(entries))
+            return picked
+
+        def quantise_w2(g, chunks, round_copy):
+            grouped = held([P, PACK, P, PACK], BF16, f"w2_grouped{g}")
+            for c, chunk in enumerate(chunks):
+                rows = slice(CHUNK // PACK * c, CHUNK // PACK * (c + 1))
+                round_copy(
+                    grouped[:, :, rows, :].rearrange("p t m j -> p m j t"),
+                    chunk.rearrange("p j (m t) -> p m j t", t=PACK),
+                )
+            codes = held([P, PASS], U32, f"w2_codes{g}")
+            scale = held([P, PASS], U8, f"w2_scale{g}")
+            nc.vector.quantize_mx(
+                out=codes[:].bitcast(FP8X4), scales=scale[:], in_=grouped[:].rearrange("p t m j -> p (t m j)")
+            )
+            return codes, scale
+
         list1 = keep.tile([P, S // 16], U16, name="list1")
         list2 = keep.tile([P, S // 16], U16, name="list2")
         v2_scale_rows = held([P, T], U8, "v2_scale_rows")
-        v_scale_rows = held([P, T], U8, "v_scale_rows")
-        w1_scale_rows = held([P, 2, H], U8, "w1_scale_rows")
-        w3_scale = held([P, 2, N], U8, "w3_scale")
-        v_scale1 = held([P, S], U8, "v_scale1")
-        for tile in (v2_scale_rows, w1_scale_rows, w3_scale, v_scale1):
+        w1_scale_rows = held([P, H], U8, "w1_scale_rows")
+        v_scale = [held([P, S], U8, f"v_scale{a}") for a in range(2)]
+        w1_scale = [held([P, H], U8, f"w1_scale{a}") for a in range(2)]
+        w3_scale = held([P, N], U8, "w3_scale")
+        for tile in (w1_scale_rows, v_scale[0], v_scale[1], w1_scale[1], w3_scale, v2_scale_rows):
             nc.vector.memset(tile[:].bitcast(I32), 0)
 
-        nc.sync.dma_start(list2[:], offs2)
         nc.sync.dma_start(list1[:], offs)
-        v2_rows = tab2_scales[0].rearrange("(d r) t -> r d t", r=4)
-        for r in range(4):
-            nc.scalar.dma_start(v2_scale_rows[r:P:32, :].bitcast(I32), v2_rows[r].bitcast(I32))
+        v_scale_rows = held([P, T], U8, "v_scale_rows")
         v_rows = tab_scales.rearrange("a q t -> q a t").bitcast(I32)
         for a in range(2):
             nc.sync.dma_start(
                 v_scale_rows[a:P:2, :].bitcast(I32), v_rows[:, a : a + 1, :].to_broadcast([16, 4, T // 4])
             )
-        w1_rows = w1_scales.rearrange("a (d r) c -> r d a c", r=4)
+        w2_first = load_w2(0, PASS)
+        nc.sync.dma_start(list2[:], offs2)
+        v2_rows = tab2_scales[0].rearrange("(d r) t -> r d t", r=4)
         for r in range(4):
-            nc.gpsimd.dma_start(w1_scale_rows[r:P:32, :, :].bitcast(I32), w1_rows[r].bitcast(I32))
-        w3_rows = w3_scales.rearrange("a (d r) c -> r d a c", r=4)
-        for r in range(4):
-            nc.gpsimd.dma_start(w3_scale[r:P:32, :, :].bitcast(I32), w3_rows[r].bitcast(I32))
+            nc.scalar.dma_start(v2_scale_rows[r:P:32, :].bitcast(I32), v2_rows[r].bitcast(I32))
+        v2_words = load_table(tab2_words[0], "v2_words")
+
+        v_scale_picked = held([P, S], U8, "v_scale_picked")
+        nc.vector.tensor_copy(v_scale_picked[:], v_scale_rows[:].indirect(list1[:]))
+        v2_scale = held([P, S], U8, "v2_scale")
+        nc.vector.tensor_copy(v2_scale[:], v2_scale_rows[:].indirect(list2[:]))
+        w2_mx = [quantise_w2(0, w2_first, lambda dst, src: nc.scalar.activation(dst, src, ACT.Copy))]
+
+        load_two_planes(w1_scale_rows, w1_scales)
         w1_raw = held([P, 2, 2 * H], U8, "w1_raw")
-        w2_rows = w2.rearrange("(p j) c -> p j c", j=PACK)
-
-        def load_w2(c):
-            raw = ring.tile([P, PACK, 256], F32, name="w2_raw", bufs=2)
-            nc.sync.dma_start(raw[:], w2_rows[:, :, 256 * c : 256 * (c + 1)])
-            return raw
-
-        def load_table(words, name, tag):
-            window = held([P, T], I32, name, tag)
-            nc.sync.dma_start(window[:], words.rearrange("p t i -> p (t i)").bitcast(I32))
-            return window
-
-        w2_codes = [held([P, PASS], U32, f"w2_codes{g}") for g in range(2)]
-        w2_scale = [held([P, PASS], U8, f"w2_scale{g}") for g in range(2)]
-
-        def quantise_w2(g, raws):
-            grouped = held([P, PACK, P, PACK], BF16, f"w2_grouped{g}")
-            for c in range(2):
-                dst = grouped[:, :, 64 * c : 64 * (c + 1), :].rearrange("p t m j -> p m j t")
-                src = raws[c][:].rearrange("p j (m t) -> p m j t", t=PACK)
-                if g == 0:
-                    nc.scalar.activation(dst, src, ACT.Copy)
-                else:
-                    nc.vector.tensor_copy(dst, src)
-            nc.vector.quantize_mx(
-                out=w2_codes[g][:].bitcast(FP8X4),
-                scales=w2_scale[g][:],
-                in_=grouped[:].rearrange("p t m j -> p (t m j)"),
-            )
-
-        w1_codes = [held([P, 2, 2 * PASS], U8, f"w1_codes{g}") for g in range(2)]
-
-        def permute_w1_codes(g):
-            cols = slice(PASS * g, PASS * (g + 1))
+        nc.sync.dma_start(w1_raw[:].bitcast(I32), w1_words.rearrange("a p c -> p a c").bitcast(I32))
+        v_words = []
+        for a in range(2):
+            v_words.append(load_table(tab_words[a], f"v_words{a}"))
+            for r in range(4):
+                nc.sync.dma_start(
+                    v_scale[a][r:P:32, :].bitcast(I32), v_scale_picked[8 * r + a : P : 32, :].bitcast(I32)
+                )
+        w2_second = load_w2(PASS, CHUNK)
+        nc.vector.tensor_copy(
+            w1_scale[0][:].rearrange("p (g t m) -> p g t m", g=GROUPS, t=PACK),
+            w1_scale_rows[:].rearrange("p (g m t) -> p g t m", g=GROUPS, t=PACK),
+        )
+        nc.sync.dma_start(w1_scale[1][0:112, :].bitcast(I32), w1_scale[0][4:116, :].bitcast(I32))
+        w2_second.extend(load_w2(PASS + CHUNK, CHUNK))
+        w2_mx.append(quantise_w2(1, w2_second, nc.vector.tensor_copy))
+        w1_codes = [held([P, 2, 2 * PASS], U8, f"w1_codes{g}") for g in range(GROUPS)]
+        for g in range(GROUPS):
             nc.vector.tensor_copy(
                 w1_codes[g][:].bitcast(U16).rearrange("p a (t m) -> p a t m", t=PACK),
-                w1_raw[:].bitcast(U16)[:, :, cols].rearrange("p a (m t) -> p a t m", t=PACK),
+                w1_raw[:].bitcast(U16)[:, :, PASS * g : PASS * (g + 1)].rearrange("p a (m t) -> p a t m", t=PACK),
             )
+        w3_codes = held([P, GROUPS, N], U32, "w3_codes")
+        nc.sync.dma_start(w3_codes[:].bitcast(I32), w3_words.rearrange("a p c i -> p a (c i)").bitcast(I32))
+        load_two_planes(w3_scale, w3_scales)
 
-        def permute_w1_scale(g):
-            cols = slice(PASS * g, PASS * (g + 1))
-            nc.vector.tensor_copy(
-                w1_scale[:, g, :, :].rearrange("p a (t m) -> p a t m", t=PACK),
-                w1_scale_rows[:, :, cols].rearrange("p a (m t) -> p a t m", t=PACK),
-            )
-
-        def pick(window, offsets, block, name):
-            picked = held([P, BLOCK], U32, name)
-            nc.vector.tensor_copy(
-                picked[:], window[:].bitcast(U32).indirect(offsets[:, COLS * block : COLS * (block + 1)])
-            )
-            return picked
-
-        def gaussian(v2_codes, block, g):
-            squares = ring.tile([P, 2, UNIT, PACK], F32, name="squares")
+        def gaussian(v2_codes, block, g, banks):
+            codes, scale = w2_mx[g]
+            squares = ring.tile([P, 2, UNIT, PACK], F32, name="squares", bufs=2)
             for half in range(2):
-                bank = psum.tile([P, PACK, UNIT], F32, name="b_bank", tag="ab", bufs=6)
-                here = slice(UNIT * half, UNIT * (half + 1))
-                entries = slice(BLOCK * block + UNIT * half, BLOCK * block + UNIT * (half + 1))
+                b = bank([P, PACK, UNIT], "b", banks[half])
+                first = BLOCK * block + UNIT * half
                 for t in range(PACK):
                     cols = slice(P * t, P * (t + 1))
                     nc.tensor.matmul_mx(
-                        out=bank[:, t, :],
-                        lhsT=w2_codes[g][:, cols].bitcast(FP8X4),
-                        lhsT_scale=w2_scale[g][:, cols],
-                        rhs=v2_codes[:, here].bitcast(FP8X4),
-                        rhs_scale=v2_scale[:, entries],
+                        out=b[:, t, :],
+                        lhsT=codes[:, cols].bitcast(FP8X4),
+                        lhsT_scale=scale[:, cols],
+                        rhs=v2_codes[:, 0, UNIT * half : UNIT * (half + 1)].bitcast(FP8X4),
+                        rhs_scale=v2_scale[:, first : first + UNIT],
                         start=True,
                         stop=True,
                     )
-                nc.scalar.activation(squares[:, half, :, :], bank[:].rearrange("p t n -> p n t"), ACT.Square)
+                nc.scalar.activation(squares[:, half, :, :], b[:].rearrange("p t n -> p n t"), ACT.Square)
             share = held([P, 2, UNIT, PACK], F32, f"share{block}_{g}")
             nc.scalar.activation(share[:], squares[:], ACT.Exp, scale=-1.0)
             return share
 
-        def corrected(v_codes, share, block, g):
-            minus_h = ring.tile([P, 2, UNIT, PACK], BF16, name="minus_h", align_bytes=256)
-            for half in range(2):
-                bank = psum.tile([P, PACK, UNIT], F32, name="a_bank", tag="ab", bufs=6)
-                here = slice(UNIT * half, UNIT * (half + 1))
-                entries = slice(BLOCK * block + UNIT * half, BLOCK * block + UNIT * (half + 1))
-                for t in range(PACK):
-                    for a in range(2):
-                        nc.tensor.matmul_mx(
-                            out=bank[:, t, :],
-                            lhsT=w1_codes[g][:, a, 2 * P * t : 2 * P * (t + 1)].bitcast(FP4X4),
-                            lhsT_scale=w1_scale[:, g, a, P * t : P * (t + 1)],
-                            rhs=v_codes[a][:, here].bitcast(FP8X4),
-                            rhs_scale=v_scale[a][:, entries],
-                            start=(a == 0),
-                            stop=(a == 1),
-                        )
-                nc.vector.scalar_tensor_tensor(
-                    out=minus_h[:, half, :, :],
-                    in0=share[:, half, :, :],
-                    scalar=1.0,
-                    in1=bank[:].rearrange("p t n -> p n t"),
-                    op0=ALU.subtract,
-                    op1=ALU.mult,
-                )
-            h_codes = ring.tile([P, BLOCK], U32, name="h_codes", align_bytes=256, bufs=4)
-            h_scale = ring.tile([P, BLOCK], U8, name="h_scale", align_bytes=256, bufs=4)
-            nc.vector.quantize_mx(
-                out=h_codes[:].bitcast(FP8X4),
-                scales=h_scale[:],
-                in_=minus_h[:].rearrange("p u n t -> p (u n t)"),
+        def corrected(v_codes, share, minus_h, block, g, half, number):
+            acc = bank([P, PACK, UNIT], "a", number)
+            first = BLOCK * block + UNIT * half
+            for t in range(PACK):
+                for a in range(2):
+                    nc.tensor.matmul_mx(
+                        out=acc[:, t, :],
+                        lhsT=w1_codes[g][:, a, 2 * P * t : 2 * P * (t + 1)].bitcast(FP4X4),
+                        lhsT_scale=w1_scale[a][:, PASS * g + P * t : PASS * g + P * (t + 1)],
+                        rhs=v_codes[:, a, UNIT * half : UNIT * (half + 1)].bitcast(FP8X4),
+                        rhs_scale=v_scale[a][:, first : first + UNIT],
+                        start=(a == 0),
+                        stop=(a == 1),
+                    )
+            nc.vector.scalar_tensor_tensor(
+                out=minus_h[:, half, :, :],
+                in0=share[:, half, :, :],
+                scalar=1.0,
+                in1=acc[:].rearrange("p t n -> p n t"),
+                op0=ALU.subtract,
+                op1=ALU.mult,
             )
-            return h_codes, h_scale
 
-        def read_out(h, block):
+        def quantise_h(minus_h, block, g):
+            codes = held([P, BLOCK], U32, f"h_codes{block}_{g}")
+            scale = held([P, BLOCK], U8, f"h_scale{block}_{g}")
+            nc.vector.quantize_mx(
+                out=codes[:].bitcast(FP8X4), scales=scale[:], in_=minus_h[:].rearrange("p u n t -> p (u n t)")
+            )
+            return codes, scale
+
+        def read_out(h_mx, block):
             for pair in range(2):
-                bank = psum.tile([P, 2, BLOCK], F32, name="out_bank", bufs=2)
+                acc = bank([P, 2, BLOCK], "out", pair if block % 2 else 6 + pair)
                 for u in range(2):
                     cols = slice(P * (2 * pair + u), P * (2 * pair + u + 1))
-                    for g in range(2):
+                    for g in range(GROUPS):
                         nc.tensor.matmul_mx(
-                            out=bank[:, u, :],
+                            out=acc[:, u, :],
                             lhsT=w3_codes[:, g, cols].bitcast(FP8X4),
-                            lhsT_scale=w3_scale[:, g, cols],
-                            rhs=h[g][0][:].bitcast(FP8X4),
-                            rhs_scale=h[g][1][:],
+                            lhsT_scale=w3_scale[4 * g : P, cols],
+                            rhs=h_mx[block, g][0][:].bitcast(FP8X4),
+                            rhs_scale=h_mx[block, g][1][:],
                             start=(g == 0),
-                            stop=(g == 1),
+                            stop=(g == GROUPS - 1),
                         )
-                result = ring.tile([P, 2, BLOCK], F32, name="result")
-                if block == BLOCKS - 1 and pair == 1:
-                    nc.vector.tensor_scalar_mul(result[:], bank[:], -1.0)
+                result = ring.tile([P, 2, BLOCK], F32, name="result", bufs=4)
+                if block >= BLOCKS - 2 and pair == 1:
+                    nc.vector.tensor_scalar_mul(result[:], acc[:], -1.0)
                 else:
-                    nc.scalar.activation(result[:], bank[:], ACT.Copy, scale=-1.0)
+                    nc.scalar.activation(result[:], acc[:], ACT.Copy, scale=-1.0)
                 rows = out[2 * P * pair : 2 * P * (pair + 1), BLOCK * block : BLOCK * (block + 1)]
                 nc.sync.dma_start(rows.rearrange("(u p) c -> p u c", p=P), result[:])
 
-        first_raws = [load_w2(c) for c in range(2)]
-        v2_words = load_table(tab2_words[0], "v2_words", "v2_words")
-        nc.sync.dma_start(w1_raw[:].bitcast(I32), w1_words.rearrange("a p c -> p a c").bitcast(I32))
-        v2_scale = held([P, S], U8, "v2_scale")
-        nc.vector.tensor_copy(v2_scale[:], v2_scale_rows[:].indirect(list2[:]))
-        quantise_w2(0, first_raws)
-        v2_codes = [pick(v2_words, list2, 0, "v2_codes0")]
-        v_scale_picked = held([P, S], U8, "v_scale_picked")
-        nc.vector.tensor_copy(v_scale_picked[:], v_scale_rows[:].indirect(list1[:]))
-        v_words = [load_table(tab_words[0], "v_words0", "v_scale_rows"), load_table(tab_words[1], "v_words1", "w2_grouped0")]
-
-        def place_v_scale(plane, a, rows):
-            for r in rows:
-                nc.sync.dma_start(plane[r:P:32, :].bitcast(I32), v_scale_picked[8 * r + a : P : 32, :].bitcast(I32))
-
-        place_v_scale(v_scale1, 1, range(4))
-        v2_codes.extend(pick(v2_words, list2, block, f"v2_codes{block}") for block in range(1, BLOCKS))
-        quantise_w2(1, [load_w2(c) for c in range(2, 4)])
-        for g in range(2):
-            permute_w1_codes(g)
-        v_scale0 = held([P, S], U8, "v_scale0", "w1_raw")
-        nc.vector.tensor_copy(v_scale0[:].bitcast(I32), v_scale_picked[:].bitcast(I32))
-        place_v_scale(v_scale0, 0, range(1, 4))
-        v_scale = [v_scale0, v_scale1]
-        w3_codes = held([P, 2, N], U32, "w3_codes", "w2_grouped1")
-        nc.sync.dma_start(w3_codes[:].bitcast(I32), w3_words.rearrange("a p c i -> p a (c i)").bitcast(I32))
-        w1_scale = held([P, 2, 2, PASS], U8, "w1_scale", "v2_words")
-        for g in range(2):
-            permute_w1_scale(g)
-        b_steps = [(block, g) for g in range(2) for block in range(BLOCKS)]
-        a_steps = [(0, 0), (1, 0), (0, 1), (1, 1), (2, 0), (2, 1), (3, 0), (3, 1)]
-        shares, v_codes, h = {}, {}, {}
-        for step in range(len(a_steps) + LEAD):
-            if step >= LEAD:
-                block, g = a_steps[step - LEAD]
+        v2_codes, shares = {}, {}
+        for g in range(GROUPS):
+            for block in range(BLOCKS):
                 if g == 0:
-                    v_codes[block] = [pick(v_words[a], list1, block, f"v_codes{block}_{a}") for a in range(2)]
-                h[block, g] = corrected(v_codes[block], shares[block, g], block, g)
-                if g == 1:
-                    read_out([h[block, 0], h[block, 1]], block)
-            if step < len(b_steps):
-                block, g = b_steps[step]
-                shares[block, g] = gaussian(v2_codes[block], block, g)
+                    v2_codes[block] = pick([v2_words], list2, block, f"v2_codes{block}")
+                banks = (6, 7) if g == 0 and block % 2 else (0, 1)
+                shares[block, g] = gaussian(v2_codes[block], block, g, banks)
+
+        last = BLOCKS - 1
+        steps = [(block, g) for g in range(GROUPS) for block in range(last)] + [(last, g) for g in range(GROUPS)]
+        units = [(block, g, half) for block, g in steps for half in range(2)]
+        v_codes, minus_h, h_mx = {}, {}, {}
+        for i in range(len(units) + 2):
+            if i < len(units):
+                block, g, half = units[i]
+                if block not in v_codes:
+                    v_codes[block] = pick(v_words, list1, block, f"v_codes{block}", "share0_0" if block == last else "")
+                if half == 0:
+                    minus_h[block, g] = ring.tile([P, 2, UNIT, PACK], BF16, name="minus_h", align_bytes=256)
+                corrected(v_codes[block], shares[block, g], minus_h[block, g], block, g, half, 2 + i % 4)
+            if i >= 2 and i % 2 == 0:
+                block, g = steps[i // 2 - 1]
+                h_mx[block, g] = quantise_h(minus_h[block, g], block, g)
+            if i >= 3 and i % 2 == 1:
+                block, g = steps[i // 2 - 1]
+                if g == GROUPS - 1:
+                    read_out(h_mx, block)

@@ -66,11 +66,11 @@ def tile_list_wake_correction_kernel(
                 nc.vector.tensor_copy(picked[:, a, :], window[:].bitcast(U32).indirect(entries))
             return picked
 
-        def quantise_w2(g, chunks, round_copy):
+        def quantise_w2(g, chunks, round_copies):
             grouped = held([P, PACK, P, PACK], BF16, f"w2_grouped{g}")
             for c, chunk in enumerate(chunks):
                 rows = slice(CHUNK // PACK * c, CHUNK // PACK * (c + 1))
-                round_copy(
+                round_copies[c](
                     grouped[:, :, rows, :].rearrange("p t m j -> p m j t"),
                     chunk.rearrange("p j (m t) -> p m j t", t=PACK),
                 )
@@ -81,6 +81,9 @@ def tile_list_wake_correction_kernel(
             )
             return codes, scale
 
+        def on_scalar(dst, src):
+            nc.scalar.activation(dst, src, ACT.Copy)
+
         list1 = keep.tile([P, S // 16], U16, name="list1")
         list2 = keep.tile([P, S // 16], U16, name="list2")
         v2_scale_rows = held([P, T], U8, "v2_scale_rows")
@@ -88,7 +91,7 @@ def tile_list_wake_correction_kernel(
         v_scale = [held([P, S], U8, f"v_scale{a}") for a in range(2)]
         w1_scale = [held([P, H], U8, f"w1_scale{a}") for a in range(2)]
         w3_scale = held([P, N], U8, "w3_scale")
-        for tile in (w1_scale_rows, v_scale[0], v_scale[1], w1_scale[1], w3_scale, v2_scale_rows):
+        for tile in (v2_scale_rows, w1_scale_rows, v_scale[0], v_scale[1], w1_scale[1], w3_scale):
             nc.vector.memset(tile[:].bitcast(I32), 0)
 
         nc.sync.dma_start(list1[:], offs)
@@ -103,13 +106,14 @@ def tile_list_wake_correction_kernel(
         v2_rows = tab2_scales[0].rearrange("(d r) t -> r d t", r=4)
         for r in range(4):
             nc.scalar.dma_start(v2_scale_rows[r:P:32, :].bitcast(I32), v2_rows[r].bitcast(I32))
+        w2_second = load_w2(PASS, CHUNK)
         v2_words = load_table(tab2_words[0], "v2_words")
 
         v_scale_picked = held([P, S], U8, "v_scale_picked")
         nc.vector.tensor_copy(v_scale_picked[:], v_scale_rows[:].indirect(list1[:]))
         v2_scale = held([P, S], U8, "v2_scale")
         nc.vector.tensor_copy(v2_scale[:], v2_scale_rows[:].indirect(list2[:]))
-        w2_mx = [quantise_w2(0, w2_first, lambda dst, src: nc.scalar.activation(dst, src, ACT.Copy))]
+        w2_mx = [quantise_w2(0, w2_first, [on_scalar, on_scalar])]
 
         load_two_planes(w1_scale_rows, w1_scales)
         w1_raw = held([P, 2, 2 * H], U8, "w1_raw")
@@ -121,14 +125,13 @@ def tile_list_wake_correction_kernel(
                 nc.sync.dma_start(
                     v_scale[a][r:P:32, :].bitcast(I32), v_scale_picked[8 * r + a : P : 32, :].bitcast(I32)
                 )
-        w2_second = load_w2(PASS, CHUNK)
         nc.vector.tensor_copy(
             w1_scale[0][:].rearrange("p (g t m) -> p g t m", g=GROUPS, t=PACK),
             w1_scale_rows[:].rearrange("p (g m t) -> p g t m", g=GROUPS, t=PACK),
         )
         nc.sync.dma_start(w1_scale[1][0:112, :].bitcast(I32), w1_scale[0][4:116, :].bitcast(I32))
         w2_second.extend(load_w2(PASS + CHUNK, CHUNK))
-        w2_mx.append(quantise_w2(1, w2_second, nc.vector.tensor_copy))
+        w2_mx.append(quantise_w2(1, w2_second, [on_scalar, nc.vector.tensor_copy]))
         w1_codes = [held([P, 2, 2 * PASS], U8, f"w1_codes{g}") for g in range(GROUPS)]
         for g in range(GROUPS):
             nc.vector.tensor_copy(
@@ -151,7 +154,7 @@ def tile_list_wake_correction_kernel(
                         out=b[:, t, :],
                         lhsT=codes[:, cols].bitcast(FP8X4),
                         lhsT_scale=scale[:, cols],
-                        rhs=v2_codes[:, 0, UNIT * half : UNIT * (half + 1)].bitcast(FP8X4),
+                        rhs=v2_codes[:, UNIT * half : UNIT * (half + 1)].bitcast(FP8X4),
                         rhs_scale=v2_scale[:, first : first + UNIT],
                         start=True,
                         stop=True,
@@ -194,7 +197,7 @@ def tile_list_wake_correction_kernel(
 
         def read_out(h_mx, block):
             for pair in range(2):
-                acc = bank([P, 2, BLOCK], "out", pair if block % 2 else 6 + pair)
+                acc = bank([P, 2, BLOCK], "out", pair if block == BLOCKS - 2 else 6 + pair)
                 for u in range(2):
                     cols = slice(P * (2 * pair + u), P * (2 * pair + u + 1))
                     for g in range(GROUPS):
@@ -208,20 +211,46 @@ def tile_list_wake_correction_kernel(
                             stop=(g == GROUPS - 1),
                         )
                 result = ring.tile([P, 2, BLOCK], F32, name="result", bufs=4)
-                if block >= BLOCKS - 2 and pair == 1:
+                if block == BLOCKS - 2 and pair == 1:
                     nc.vector.tensor_scalar_mul(result[:], acc[:], -1.0)
                 else:
                     nc.scalar.activation(result[:], acc[:], ACT.Copy, scale=-1.0)
                 rows = out[2 * P * pair : 2 * P * (pair + 1), BLOCK * block : BLOCK * (block + 1)]
                 nc.sync.dma_start(rows.rearrange("(u p) c -> p u c", p=P), result[:])
 
-        v2_codes, shares = {}, {}
+        def read_out_last(h_mx, block):
+            accs = [bank([P, BLOCK], "out_last", 2 + n) for n in range(N // P)]
+            for g in range(GROUPS):
+                for n, acc in enumerate(accs):
+                    cols = slice(P * n, P * (n + 1))
+                    nc.tensor.matmul_mx(
+                        out=acc[:],
+                        lhsT=w3_codes[:, g, cols].bitcast(FP8X4),
+                        lhsT_scale=w3_scale[4 * g : P, cols],
+                        rhs=h_mx[block, g][0][:].bitcast(FP8X4),
+                        rhs_scale=h_mx[block, g][1][:],
+                        start=(g == 0),
+                        stop=(g == GROUPS - 1),
+                    )
+            for n, acc in enumerate(accs):
+                result = held([P, BLOCK], F32, f"result_last{n}")
+                if n % 2:
+                    nc.vector.tensor_scalar_mul(result[:], acc[:], -1.0)
+                else:
+                    nc.scalar.activation(result[:], acc[:], ACT.Copy, scale=-1.0)
+                nc.sync.dma_start(out[P * n : P * (n + 1), BLOCK * block : BLOCK * (block + 1)], result[:])
+
+        v2_first = held([P, BLOCK], U32, "v2_first")
+        nc.vector.tensor_copy(v2_first[:], v2_words[:].bitcast(U32).indirect(list2[:, 0:LIST_COLS]))
+        v2_rest = held([P, S - BLOCK], U32, "v2_rest", "w2_grouped0")
+        nc.vector.tensor_copy(v2_rest[:], v2_words[:].bitcast(U32).indirect(list2[:, LIST_COLS : S // 16]))
+        v2_codes = [v2_first[:]] + [v2_rest[:, BLOCK * i : BLOCK * (i + 1)] for i in range(BLOCKS - 1)]
+        shares = {}
         for g in range(GROUPS):
             for block in range(BLOCKS):
-                if g == 0:
-                    v2_codes[block] = pick([v2_words], list2, block, f"v2_codes{block}")
                 banks = (6, 7) if g == 0 and block % 2 else (0, 1)
-                shares[block, g] = gaussian(v2_codes[block], block, g, banks)
+                if (block, g) != (BLOCKS - 1, GROUPS - 1):
+                    shares[block, g] = gaussian(v2_codes[block], block, g, banks)
 
         last = BLOCKS - 1
         steps = [(block, g) for g in range(GROUPS) for block in range(last)] + [(last, g) for g in range(GROUPS)]
@@ -240,5 +269,9 @@ def tile_list_wake_correction_kernel(
                 h_mx[block, g] = quantise_h(minus_h[block, g], block, g)
             if i >= 3 and i % 2 == 1:
                 block, g = steps[i // 2 - 1]
-                if g == GROUPS - 1:
+                if (block, g) == (0, GROUPS - 1):
                     read_out(h_mx, block)
+                    shares[last, g] = gaussian(v2_codes[last], last, g, (0, 1))
+        for block in range(1, last):
+            read_out(h_mx, block)
+        read_out_last(h_mx, last)

@@ -53,9 +53,9 @@ def tile_list_wake_correction_kernel(
             nc.sync.dma_start(raw[:], w2.rearrange("(p j) c -> p j c", j=PACK)[:, :, first : first + width])
             return [raw[:, :, c : c + CHUNK] for c in range(0, width, CHUNK)]
 
-        def load_two_planes(tile, scales):
+        def load_two_planes(queue, tile, scales):
             for d in range(4):
-                nc.sync.dma_start(
+                queue.dma_start(
                     tile[32 * d : 32 * d + 8, :].bitcast(I32), scales[:, 4 * d : 4 * d + 4, :].bitcast(I32)
                 )
 
@@ -86,65 +86,77 @@ def tile_list_wake_correction_kernel(
 
         list1 = keep.tile([P, S // 16], U16, name="list1")
         list2 = keep.tile([P, S // 16], U16, name="list2")
+        v_scale_rows = held([P, T], U8, "v_scale_rows")
         v2_scale_rows = held([P, T], U8, "v2_scale_rows")
         w1_scale_rows = held([P, H], U8, "w1_scale_rows")
         v_scale = [held([P, S], U8, f"v_scale{a}") for a in range(2)]
-        w1_scale = [held([P, H], U8, f"w1_scale{a}") for a in range(2)]
+        w1_scale_second = held([P, H], U8, "w1_scale1")
         w3_scale = held([P, N], U8, "w3_scale")
-        for tile in (v2_scale_rows, w1_scale_rows, v_scale[0], v_scale[1], w1_scale[1], w3_scale):
+        for tile in (v_scale_rows, v2_scale_rows, w1_scale_rows, v_scale[0], v_scale[1], w1_scale_second, w3_scale):
             nc.vector.memset(tile[:].bitcast(I32), 0)
 
-        nc.sync.dma_start(list1[:], offs)
-        v_scale_rows = held([P, T], U8, "v_scale_rows")
-        v_rows = tab_scales.rearrange("a q t -> q a t").bitcast(I32)
-        for a in range(2):
-            nc.sync.dma_start(
-                v_scale_rows[a:P:2, :].bitcast(I32), v_rows[:, a : a + 1, :].to_broadcast([16, 4, T // 4])
+        def move_v_scale(a):
+            for r in range(4):
+                nc.sync.dma_start(
+                    v_scale[a][r:P:32, :].bitcast(I32), v_scale_picked[8 * r + 4 * a : P : 32, :].bitcast(I32)
+                )
+
+        def load_w1(g):
+            raw = held([P, 2, 2 * PASS], U8, f"w1_raw{g}")
+            columns = w1_words.rearrange("a p c -> p a c")[:, :, 2 * PASS * g : 2 * PASS * (g + 1)]
+            nc.sync.dma_start(raw[:].bitcast(I32), columns.bitcast(I32))
+            return raw
+
+        def deal_w1(g, tag=""):
+            codes = held([P, 2, 2 * PASS], U8, f"w1_codes{g}", tag)
+            nc.vector.tensor_copy(
+                codes[:].bitcast(U16).rearrange("p a (t m) -> p a t m", t=PACK),
+                w1_raw[g][:].bitcast(U16).rearrange("p a (m t) -> p a t m", t=PACK),
             )
-        w2_first = load_w2(0, PASS)
-        nc.sync.dma_start(list2[:], offs2)
+            return codes
+
+        w2_raw, v_words = [], []
+        w3_codes = held([P, GROUPS, N], U32, "w3_codes")
         v2_rows = tab2_scales[0].rearrange("(d r) t -> r d t", r=4)
+        nc.sync.dma_start(list1[:], offs)
+        nc.sync.dma_start(list2[:], offs2)
+        nc.sync.dma_start(v_scale_rows[0:P:4, :].bitcast(I32), tab_scales.rearrange("a q t -> q a t").bitcast(I32))
+        w2_raw.extend(load_w2(0, CHUNK))
+        w2_raw.extend(load_w2(CHUNK, CHUNK))
         for r in range(4):
             nc.scalar.dma_start(v2_scale_rows[r:P:32, :].bitcast(I32), v2_rows[r].bitcast(I32))
-        w2_second = load_w2(PASS, CHUNK)
         v2_words = load_table(tab2_words[0], "v2_words")
+        load_two_planes(nc.sync, w1_scale_rows, w1_scales)
+        w1_raw = [load_w1(0)]
 
         v_scale_picked = held([P, S], U8, "v_scale_picked")
         nc.vector.tensor_copy(v_scale_picked[:], v_scale_rows[:].indirect(list1[:]))
         v2_scale = held([P, S], U8, "v2_scale")
         nc.vector.tensor_copy(v2_scale[:], v2_scale_rows[:].indirect(list2[:]))
-        w2_mx = [quantise_w2(0, w2_first, [on_scalar, on_scalar])]
-
-        load_two_planes(w1_scale_rows, w1_scales)
-        w1_raw = held([P, 2, 2 * H], U8, "w1_raw")
-        nc.sync.dma_start(w1_raw[:].bitcast(I32), w1_words.rearrange("a p c -> p a c").bitcast(I32))
-        v_words = []
-        for a in range(2):
-            v_words.append(load_table(tab_words[a], f"v_words{a}"))
-            for r in range(4):
-                nc.sync.dma_start(
-                    v_scale[a][r:P:32, :].bitcast(I32), v_scale_picked[8 * r + a : P : 32, :].bitcast(I32)
-                )
+        w2_mx = [quantise_w2(0, w2_raw[0:2], [on_scalar, on_scalar])]
+        v2_codes = [pick([v2_words], list2, block, f"v2_codes{block}", "w2_grouped0" if block else "")[:, 0, :] for block in range(2)]
+        w1_scale = [held([P, H], U8, "w1_scale0"), w1_scale_second]
         nc.vector.tensor_copy(
             w1_scale[0][:].rearrange("p (g t m) -> p g t m", g=GROUPS, t=PACK),
             w1_scale_rows[:].rearrange("p (g m t) -> p g t m", g=GROUPS, t=PACK),
         )
+        v2_rest = held([P, 2 * BLOCK], U32, "v2_rest", "w1_scale_rows")
+        nc.vector.tensor_copy(v2_rest[:], v2_words[:].bitcast(U32).indirect(list2[:, 2 * LIST_COLS : S // 16]))
+        v2_codes.extend(v2_rest[:, BLOCK * i : BLOCK * (i + 1)] for i in range(2))
+        v_words.append(load_table(tab_words[0], "v_words0"))
+        move_v_scale(0)
+        v_words.append(load_table(tab_words[1], "v_words1"))
+        move_v_scale(1)
         nc.sync.dma_start(w1_scale[1][0:112, :].bitcast(I32), w1_scale[0][4:116, :].bitcast(I32))
-        w2_second.extend(load_w2(PASS + CHUNK, CHUNK))
-        w2_mx.append(quantise_w2(1, w2_second, [on_scalar, nc.vector.tensor_copy]))
-        w1_codes = [held([P, 2, 2 * PASS], U8, f"w1_codes{g}") for g in range(GROUPS)]
-        for g in range(GROUPS):
-            nc.vector.tensor_copy(
-                w1_codes[g][:].bitcast(U16).rearrange("p a (t m) -> p a t m", t=PACK),
-                w1_raw[:].bitcast(U16)[:, :, PASS * g : PASS * (g + 1)].rearrange("p a (m t) -> p a t m", t=PACK),
-            )
-        w3_codes = held([P, GROUPS, N], U32, "w3_codes")
+        w2_raw.extend(load_w2(2 * CHUNK, CHUNK))
+        w2_raw.extend(load_w2(3 * CHUNK, CHUNK))
+        w1_raw.append(load_w1(1))
         nc.sync.dma_start(w3_codes[:].bitcast(I32), w3_words.rearrange("a p c i -> p a (c i)").bitcast(I32))
-        load_two_planes(w3_scale, w3_scales)
+        load_two_planes(nc.sync, w3_scale, w3_scales)
 
-        def gaussian(v2_codes, block, g, banks):
+        def gaussian(v2_codes, block, g, banks, tag=""):
             codes, scale = w2_mx[g]
-            squares = ring.tile([P, 2, UNIT, PACK], F32, name="squares", bufs=2)
+            squares = held([P, 2, UNIT, PACK], F32, f"squares{block}_{g}", tag)
             for half in range(2):
                 b = bank([P, PACK, UNIT], "b", banks[half])
                 first = BLOCK * block + UNIT * half
@@ -168,15 +180,15 @@ def tile_list_wake_correction_kernel(
             acc = bank([P, PACK, UNIT], "a", number)
             first = BLOCK * block + UNIT * half
             for t in range(PACK):
-                for a in range(2):
+                for a in (1, 0):
                     nc.tensor.matmul_mx(
                         out=acc[:, t, :],
                         lhsT=w1_codes[g][:, a, 2 * P * t : 2 * P * (t + 1)].bitcast(FP4X4),
                         lhsT_scale=w1_scale[a][:, PASS * g + P * t : PASS * g + P * (t + 1)],
                         rhs=v_codes[:, a, UNIT * half : UNIT * (half + 1)].bitcast(FP8X4),
                         rhs_scale=v_scale[a][:, first : first + UNIT],
-                        start=(a == 0),
-                        stop=(a == 1),
+                        start=(a == 1),
+                        stop=(a == 0),
                     )
             nc.vector.scalar_tensor_tensor(
                 out=minus_h[:, half, :, :],
@@ -197,21 +209,21 @@ def tile_list_wake_correction_kernel(
 
         def read_out(h_mx, block):
             for pair in range(2):
-                acc = bank([P, 2, BLOCK], "out", pair if block == BLOCKS - 2 else 6 + pair)
+                acc = bank([P, 2, BLOCK], "out", 4 + pair)
                 for u in range(2):
                     cols = slice(P * (2 * pair + u), P * (2 * pair + u + 1))
-                    for g in range(GROUPS):
+                    for g in (1, 0):
                         nc.tensor.matmul_mx(
                             out=acc[:, u, :],
                             lhsT=w3_codes[:, g, cols].bitcast(FP8X4),
                             lhsT_scale=w3_scale[4 * g : P, cols],
                             rhs=h_mx[block, g][0][:].bitcast(FP8X4),
                             rhs_scale=h_mx[block, g][1][:],
-                            start=(g == 0),
-                            stop=(g == GROUPS - 1),
+                            start=(g == 1),
+                            stop=(g == 0),
                         )
                 result = ring.tile([P, 2, BLOCK], F32, name="result", bufs=4)
-                if block == BLOCKS - 2 and pair == 1:
+                if (block, pair) in {(0, 0)}:
                     nc.vector.tensor_scalar_mul(result[:], acc[:], -1.0)
                 else:
                     nc.scalar.activation(result[:], acc[:], ACT.Copy, scale=-1.0)
@@ -219,7 +231,7 @@ def tile_list_wake_correction_kernel(
                 nc.sync.dma_start(rows.rearrange("(u p) c -> p u c", p=P), result[:])
 
         def read_out_last(h_mx, block):
-            accs = [bank([P, BLOCK], "out_last", 2 + n) for n in range(N // P)]
+            accs = [bank([P, BLOCK], "out_last", (0, 1, 6, 7)[n]) for n in range(N // P)]
             for g in range(GROUPS):
                 for n, acc in enumerate(accs):
                     cols = slice(P * n, P * (n + 1))
@@ -240,38 +252,34 @@ def tile_list_wake_correction_kernel(
                     nc.scalar.activation(result[:], acc[:], ACT.Copy, scale=-1.0)
                 nc.sync.dma_start(out[P * n : P * (n + 1), BLOCK * block : BLOCK * (block + 1)], result[:])
 
-        v2_first = held([P, BLOCK], U32, "v2_first")
-        nc.vector.tensor_copy(v2_first[:], v2_words[:].bitcast(U32).indirect(list2[:, 0:LIST_COLS]))
-        v2_rest = held([P, S - BLOCK], U32, "v2_rest", "w2_grouped0")
-        nc.vector.tensor_copy(v2_rest[:], v2_words[:].bitcast(U32).indirect(list2[:, LIST_COLS : S // 16]))
-        v2_codes = [v2_first[:]] + [v2_rest[:, BLOCK * i : BLOCK * (i + 1)] for i in range(BLOCKS - 1)]
-        shares = {}
-        for g in range(GROUPS):
-            for block in range(BLOCKS):
-                banks = (6, 7) if g == 0 and block % 2 else (0, 1)
-                if (block, g) != (BLOCKS - 1, GROUPS - 1):
-                    shares[block, g] = gaussian(v2_codes[block], block, g, banks)
-
         last = BLOCKS - 1
-        steps = [(block, g) for g in range(GROUPS) for block in range(last)] + [(last, g) for g in range(GROUPS)]
+        first_banks = {0: (0, 1), 1: (6, 7), 2: (4, 5), 3: (0, 1)}
+        shares = {}
+        for block in range(last):
+            shares[block, 0] = gaussian(v2_codes[block], block, 0, first_banks[block])
+        w1_codes = [deal_w1(g) for g in range(GROUPS)]
+        w2_mx.append(quantise_w2(1, w2_raw[2:], [on_scalar, nc.vector.tensor_copy]))
+        shares[last, 0] = gaussian(v2_codes[last], last, 0, first_banks[last], "w2_raw512")
+        for block in range(BLOCKS):
+            shares[block, 1] = gaussian(v2_codes[block], block, 1, (0, 1))
+
+        steps = [(block, g) for g in range(GROUPS) for block in range(BLOCKS)]
         units = [(block, g, half) for block, g in steps for half in range(2)]
-        v_codes, minus_h, h_mx = {}, {}, {}
+        minus_h, h_mx = {}, {}
+        v_codes = {block: pick(v_words, list1, block, f"v_codes{block}", "v_scale_picked" if block == 2 else "") for block in range(last)}
         for i in range(len(units) + 2):
             if i < len(units):
                 block, g, half = units[i]
-                if block not in v_codes:
-                    v_codes[block] = pick(v_words, list1, block, f"v_codes{block}", "share0_0" if block == last else "")
+                if i == 2:
+                    v_codes[last] = pick(v_words, list1, last, "v_codes_last", "share0_0")
                 if half == 0:
                     minus_h[block, g] = ring.tile([P, 2, UNIT, PACK], BF16, name="minus_h", align_bytes=256)
-                corrected(v_codes[block], shares[block, g], minus_h[block, g], block, g, half, 2 + i % 4)
+                corrected(v_codes[block], shares[block, g], minus_h[block, g], block, g, half, (2, 3, 6, 7, 4, 5, 2, 3)[i] if i < 8 else (6, 7, 2, 3)[i % 4])
             if i >= 2 and i % 2 == 0:
                 block, g = steps[i // 2 - 1]
                 h_mx[block, g] = quantise_h(minus_h[block, g], block, g)
             if i >= 3 and i % 2 == 1:
                 block, g = steps[i // 2 - 1]
-                if (block, g) == (0, GROUPS - 1):
+                if g == GROUPS - 1 and block < last:
                     read_out(h_mx, block)
-                    shares[last, g] = gaussian(v2_codes[last], last, g, (0, 1))
-        for block in range(1, last):
-            read_out(h_mx, block)
         read_out_last(h_mx, last)

@@ -24,6 +24,7 @@ BLOCK = 256
 BLOCKS = S // BLOCK
 UNIT = 128
 LIST_COLS = BLOCK // 16
+EARLY = 768
 CHUNK = 256
 
 
@@ -88,11 +89,11 @@ def tile_list_wake_correction_kernel(
         list2 = keep.tile([P, S // 16], U16, name="list2")
         v_scale_rows = held([P, T], U8, "v_scale_rows")
         v2_scale_rows = held([P, T], U8, "v2_scale_rows")
-        w1_scale_rows = held([P, H], U8, "w1_scale_rows")
+        w1_scale_rows = held([P, 2, H], U8, "w1_scale_rows")
         v_scale = [held([P, S], U8, f"v_scale{a}") for a in range(2)]
-        w1_scale_second = held([P, H], U8, "w1_scale1")
         w3_scale = held([P, N], U8, "w3_scale")
-        for tile in (v_scale_rows, v2_scale_rows, w1_scale_rows, v_scale[0], v_scale[1], w1_scale_second, w3_scale):
+        nc.gpsimd.memset(v2_scale_rows[:].bitcast(I32), 0)
+        for tile in (v_scale_rows, w1_scale_rows, v_scale[0], v_scale[1], w3_scale):
             nc.vector.memset(tile[:].bitcast(I32), 0)
 
         def move_v_scale(a):
@@ -108,14 +109,20 @@ def tile_list_wake_correction_kernel(
             return raw
 
         def deal_w1(g, tag=""):
+            scale = held([P, 2, PASS], U8, f"w1_scale{g}")
+            nc.gpsimd.tensor_copy(
+                scale[:].rearrange("p a (t m) -> p a t m", t=PACK),
+                w1_scale_rows[:, :, PASS * g : PASS * (g + 1)].rearrange("p a (m t) -> p a t m", t=PACK),
+            )
+            w1_scale.append(scale)
             codes = held([P, 2, 2 * PASS], U8, f"w1_codes{g}", tag)
-            nc.vector.tensor_copy(
+            nc.gpsimd.tensor_copy(
                 codes[:].bitcast(U16).rearrange("p a (t m) -> p a t m", t=PACK),
                 w1_raw[g][:].bitcast(U16).rearrange("p a (m t) -> p a t m", t=PACK),
             )
             return codes
 
-        w2_raw, v_words = [], []
+        w2_raw, v_words, w1_scale = [], [], []
         w3_codes = held([P, GROUPS, N], U32, "w3_codes")
         v2_rows = tab2_scales[0].rearrange("(d r) t -> r d t", r=4)
         nc.sync.dma_start(list1[:], offs)
@@ -126,28 +133,35 @@ def tile_list_wake_correction_kernel(
         for r in range(4):
             nc.scalar.dma_start(v2_scale_rows[r:P:32, :].bitcast(I32), v2_rows[r].bitcast(I32))
         v2_words = load_table(tab2_words[0], "v2_words")
-        load_two_planes(nc.sync, w1_scale_rows, w1_scales)
-        w1_raw = [load_w1(0)]
 
         v_scale_picked = held([P, S], U8, "v_scale_picked")
         nc.vector.tensor_copy(v_scale_picked[:], v_scale_rows[:].indirect(list1[:]))
-        v2_scale = held([P, S], U8, "v2_scale")
-        nc.vector.tensor_copy(v2_scale[:], v2_scale_rows[:].indirect(list2[:]))
+        v2_scale_first = held([P, EARLY], U8, "v2_scale_first")
+        nc.vector.tensor_copy(v2_scale_first[:], v2_scale_rows[:].indirect(list2[:, 0 : EARLY // 16]))
         w2_mx = [quantise_w2(0, w2_raw[0:2], [on_scalar, on_scalar])]
-        v2_codes = [pick([v2_words], list2, block, f"v2_codes{block}", "w2_grouped0" if block else "")[:, 0, :] for block in range(2)]
-        w1_scale = [held([P, H], U8, "w1_scale0"), w1_scale_second]
-        nc.vector.tensor_copy(
-            w1_scale[0][:].rearrange("p (g t m) -> p g t m", g=GROUPS, t=PACK),
-            w1_scale_rows[:].rearrange("p (g m t) -> p g t m", g=GROUPS, t=PACK),
-        )
-        v2_rest = held([P, 2 * BLOCK], U32, "v2_rest", "w1_scale_rows")
+        v2_first = held([P, 2, BLOCK], U32, "v2_first", "w2_raw256")
+        for block in range(2):
+            entries = list2[:, LIST_COLS * block : LIST_COLS * (block + 1)]
+            nc.vector.tensor_copy(v2_first[:, block, :], v2_words[:].bitcast(U32).indirect(entries))
+        v2_scale_rest = held([P, S - EARLY], U8, "v2_scale_rest", "w2_grouped0")
+        nc.vector.tensor_copy(v2_scale_rest[:], v2_scale_rows[:].indirect(list2[:, EARLY // 16 : S // 16]))
+        v2_rest = held([P, 2 * BLOCK], U32, "v2_rest", "v2_scale_rows")
         nc.vector.tensor_copy(v2_rest[:], v2_words[:].bitcast(U32).indirect(list2[:, 2 * LIST_COLS : S // 16]))
-        v2_codes.extend(v2_rest[:, BLOCK * i : BLOCK * (i + 1)] for i in range(2))
-        v_words.append(load_table(tab_words[0], "v_words0"))
+        v2_codes = [v2_first[:, 0, :], v2_first[:, 1, :], v2_rest[:, 0:BLOCK], v2_rest[:, BLOCK : 2 * BLOCK]]
+
+        def v2_scale(first):
+            if first < EARLY:
+                return v2_scale_first[:, first : first + UNIT]
+            return v2_scale_rest[:, first - EARLY : first - EARLY + UNIT]
+
         move_v_scale(0)
+        v_words.append(load_table(tab_words[0], "v_words0"))
+        for d in range(4):
+            rows = w1_scales[:, 4 * d : 4 * d + 4, :].rearrange("a r c -> r a c")
+            nc.sync.dma_start(w1_scale_rows[32 * d : 32 * d + 4, :, :].bitcast(I32), rows.bitcast(I32))
+        w1_raw = [load_w1(0)]
         v_words.append(load_table(tab_words[1], "v_words1"))
         move_v_scale(1)
-        nc.sync.dma_start(w1_scale[1][0:112, :].bitcast(I32), w1_scale[0][4:116, :].bitcast(I32))
         w2_raw.extend(load_w2(2 * CHUNK, CHUNK))
         w2_raw.extend(load_w2(3 * CHUNK, CHUNK))
         w1_raw.append(load_w1(1))
@@ -167,7 +181,7 @@ def tile_list_wake_correction_kernel(
                         lhsT=codes[:, cols].bitcast(FP8X4),
                         lhsT_scale=scale[:, cols],
                         rhs=v2_codes[:, UNIT * half : UNIT * (half + 1)].bitcast(FP8X4),
-                        rhs_scale=v2_scale[:, first : first + UNIT],
+                        rhs_scale=v2_scale(first),
                         start=True,
                         stop=True,
                     )
@@ -184,7 +198,7 @@ def tile_list_wake_correction_kernel(
                     nc.tensor.matmul_mx(
                         out=acc[:, t, :],
                         lhsT=w1_codes[g][:, a, 2 * P * t : 2 * P * (t + 1)].bitcast(FP4X4),
-                        lhsT_scale=w1_scale[a][:, PASS * g + P * t : PASS * g + P * (t + 1)],
+                        lhsT_scale=w1_scale[g][:, a, P * t : P * (t + 1)],
                         rhs=v_codes[:, a, UNIT * half : UNIT * (half + 1)].bitcast(FP8X4),
                         rhs_scale=v_scale[a][:, first : first + UNIT],
                         start=(a == 1),
@@ -207,31 +221,30 @@ def tile_list_wake_correction_kernel(
             )
             return codes, scale
 
-        def read_out(h_mx, block):
-            for pair in range(2):
-                acc = bank([P, 2, BLOCK], "out", 4 + pair)
-                for u in range(2):
-                    cols = slice(P * (2 * pair + u), P * (2 * pair + u + 1))
-                    for g in (1, 0):
-                        nc.tensor.matmul_mx(
-                            out=acc[:, u, :],
-                            lhsT=w3_codes[:, g, cols].bitcast(FP8X4),
-                            lhsT_scale=w3_scale[4 * g : P, cols],
-                            rhs=h_mx[block, g][0][:].bitcast(FP8X4),
-                            rhs_scale=h_mx[block, g][1][:],
-                            start=(g == 1),
-                            stop=(g == 0),
-                        )
-                result = ring.tile([P, 2, BLOCK], F32, name="result", bufs=4)
-                if (block, pair) in {(0, 0)}:
-                    nc.vector.tensor_scalar_mul(result[:], acc[:], -1.0)
-                else:
-                    nc.scalar.activation(result[:], acc[:], ACT.Copy, scale=-1.0)
-                rows = out[2 * P * pair : 2 * P * (pair + 1), BLOCK * block : BLOCK * (block + 1)]
-                nc.sync.dma_start(rows.rearrange("(u p) c -> p u c", p=P), result[:])
+        def read_out(h_mx, block, pair, number, on_vector):
+            acc = bank([P, 2, BLOCK], "out", number)
+            for u in range(2):
+                cols = slice(P * (2 * pair + u), P * (2 * pair + u + 1))
+                for g in (1, 0):
+                    nc.tensor.matmul_mx(
+                        out=acc[:, u, :],
+                        lhsT=w3_codes[:, g, cols].bitcast(FP8X4),
+                        lhsT_scale=w3_scale[4 * g : P, cols],
+                        rhs=h_mx[block, g][0][:].bitcast(FP8X4),
+                        rhs_scale=h_mx[block, g][1][:],
+                        start=(g == 1),
+                        stop=(g == 0),
+                    )
+            result = ring.tile([P, 2, BLOCK], F32, name="result", bufs=4)
+            if on_vector:
+                nc.vector.tensor_scalar_mul(result[:], acc[:], -1.0)
+            else:
+                nc.scalar.activation(result[:], acc[:], ACT.Copy, scale=-1.0)
+            rows = out[2 * P * pair : 2 * P * (pair + 1), BLOCK * block : BLOCK * (block + 1)]
+            nc.sync.dma_start(rows.rearrange("(u p) c -> p u c", p=P), result[:])
 
         def read_out_last(h_mx, block):
-            accs = [bank([P, BLOCK], "out_last", (0, 1, 6, 7)[n]) for n in range(N // P)]
+            accs = [bank([P, BLOCK], "out_last", (4, 5, 0, 1)[n]) for n in range(N // P)]
             for g in range(GROUPS):
                 for n, acc in enumerate(accs):
                     cols = slice(P * n, P * (n + 1))
@@ -261,25 +274,25 @@ def tile_list_wake_correction_kernel(
         w2_mx.append(quantise_w2(1, w2_raw[2:], [on_scalar, nc.vector.tensor_copy]))
         shares[last, 0] = gaussian(v2_codes[last], last, 0, first_banks[last], "w2_raw512")
         for block in range(BLOCKS):
-            shares[block, 1] = gaussian(v2_codes[block], block, 1, (0, 1))
+            shares[block, 1] = gaussian(v2_codes[block], block, 1, (0, 1) if block % 2 else (4, 5))
 
         steps = [(block, g) for g in range(GROUPS) for block in range(BLOCKS)]
         units = [(block, g, half) for block, g in steps for half in range(2)]
         minus_h, h_mx = {}, {}
-        v_codes = {block: pick(v_words, list1, block, f"v_codes{block}", "v_scale_picked" if block == 2 else "") for block in range(last)}
-        for i in range(len(units) + 2):
-            if i < len(units):
-                block, g, half = units[i]
-                if i == 2:
-                    v_codes[last] = pick(v_words, list1, last, "v_codes_last", "share0_0")
-                if half == 0:
-                    minus_h[block, g] = ring.tile([P, 2, UNIT, PACK], BF16, name="minus_h", align_bytes=256)
-                corrected(v_codes[block], shares[block, g], minus_h[block, g], block, g, half, (2, 3, 6, 7, 4, 5, 2, 3)[i] if i < 8 else (6, 7, 2, 3)[i % 4])
-            if i >= 2 and i % 2 == 0:
-                block, g = steps[i // 2 - 1]
+        v_codes = {block: pick(v_words, list1, block, f"v_codes{block}", "") for block in range(BLOCKS)}
+        a_banks = [(2, 3), (6, 7), (2, 3), (6, 7), (2, 3), (6, 7), (4, 5), (6, 7)]
+        out_banks = [(2, 3), (0, 1), (2, 3)]
+        on_vector = {(0, 0), (0, 1), (2, 1)}
+        for k, (block, g) in enumerate(steps):
+            minus_h[block, g] = ring.tile([P, 2, UNIT, PACK], BF16, name="minus_h", align_bytes=256)
+            corrected(v_codes[block], shares[block, g], minus_h[block, g], block, g, 0, a_banks[k][0])
+            if 1 <= k <= 4:
+                h_mx[steps[k - 1]] = quantise_h(minus_h[steps[k - 1]], *steps[k - 1])
+            corrected(v_codes[block], shares[block, g], minus_h[block, g], block, g, 1, a_banks[k][1])
+            if g == 1 and block >= 1:
+                read_out(h_mx, block - 1, 0, out_banks[block - 1][0], (block - 1, 0) in on_vector)
+            if k >= 4:
                 h_mx[block, g] = quantise_h(minus_h[block, g], block, g)
-            if i >= 3 and i % 2 == 1:
-                block, g = steps[i // 2 - 1]
-                if g == GROUPS - 1 and block < last:
-                    read_out(h_mx, block)
+            if g == 1 and block >= 1:
+                read_out(h_mx, block - 1, 1, out_banks[block - 1][1], (block - 1, 1) in on_vector)
         read_out_last(h_mx, last)

@@ -23,9 +23,11 @@ GROUPS = H // PASS
 BLOCK = 256
 BLOCKS = S // BLOCK
 UNIT = 128
-LIST_COLS = BLOCK // 16
-EARLY = 768
 CHUNK = 256
+SCALAR_SHARE = 384
+MAST_BANKS = (0, 0, 6, 0, 0, 4, 0, 4)
+V2_ROW = 8
+W3_ROW = 4
 
 
 def tile_list_wake_correction_kernel(
@@ -35,7 +37,6 @@ def tile_list_wake_correction_kernel(
     nc = tc.nc
     with ExitStack() as ctx:
         keep = ctx.enter_context(tc.tile_pool(name="keep", bufs=1))
-        ring = ctx.enter_context(tc.tile_pool(name="ring", bufs=3))
         psum = ctx.enter_context(tc.psum_pool(name="psum", bufs=1))
 
         def held(shape, dtype, name, tag=""):
@@ -43,6 +44,9 @@ def tile_list_wake_correction_kernel(
 
         def bank(shape, name, number):
             return psum.tile(shape, F32, name=name, tag=f"bank{number}")
+
+        def entries(offsets, first, count):
+            return offsets[:, first // 16 : (first + count) // 16]
 
         def load_table(words, name):
             window = held([P, T], I32, name)
@@ -52,55 +56,38 @@ def tile_list_wake_correction_kernel(
         def load_w2(first, width):
             raw = held([P, PACK, width], F32, f"w2_raw{first}")
             nc.sync.dma_start(raw[:], w2.rearrange("(p j) c -> p j c", j=PACK)[:, :, first : first + width])
-            return [raw[:, :, c : c + CHUNK] for c in range(0, width, CHUNK)]
+            return raw
 
-        def load_two_planes(queue, tile, scales):
-            for d in range(4):
-                queue.dma_start(
-                    tile[32 * d : 32 * d + 8, :].bitcast(I32), scales[:, 4 * d : 4 * d + 4, :].bitcast(I32)
-                )
-
-        def pick(windows, offsets, block, name, tag=""):
-            picked = held([P, len(windows), BLOCK], U32, name, tag)
-            entries = offsets[:, LIST_COLS * block : LIST_COLS * (block + 1)]
-            for a, window in enumerate(windows):
-                nc.vector.tensor_copy(picked[:, a, :], window[:].bitcast(U32).indirect(entries))
+        def pick_bytes(window, offsets, first, count, name, tag=""):
+            picked = held([P, count], U8, name, tag)
+            nc.vector.tensor_copy(picked[:], window[:].indirect(entries(offsets, first, count)))
             return picked
 
-        def quantise_w2(g, chunks, round_copies):
-            grouped = held([P, PACK, P, PACK], BF16, f"w2_grouped{g}")
-            for c, chunk in enumerate(chunks):
-                rows = slice(CHUNK // PACK * c, CHUNK // PACK * (c + 1))
-                round_copies[c](
-                    grouped[:, :, rows, :].rearrange("p t m j -> p m j t"),
-                    chunk.rearrange("p j (m t) -> p m j t", t=PACK),
-                )
-            codes = held([P, PASS], U32, f"w2_codes{g}")
-            scale = held([P, PASS], U8, f"w2_scale{g}")
-            nc.vector.quantize_mx(
-                out=codes[:].bitcast(FP8X4), scales=scale[:], in_=grouped[:].rearrange("p t m j -> p (t m j)")
-            )
+        def round_w2(g, first, columns, engine):
+            dst = w2_grouped[g][:, :, first // PACK : (first + columns.shape[2]) // PACK, :]
+            src = columns.rearrange("p j (m t) -> p t m j", t=PACK)
+            if engine == "gpsimd":
+                nc.gpsimd.tensor_copy(dst, src)
+                return
+            dst, src = dst.rearrange("p t m j -> p m j t"), src.rearrange("p t m j -> p m j t")
+            if engine == "scalar":
+                nc.scalar.activation(dst, src, ACT.Copy)
+            else:
+                nc.vector.tensor_copy(dst, src)
+
+        def quantise(values, width, name, tag=""):
+            codes = held([P, width], U32, f"{name}_codes", tag)
+            scale = held([P, width], U8, f"{name}_scale")
+            nc.vector.quantize_mx(out=codes[:].bitcast(FP8X4), scales=scale[:], in_=values)
             return codes, scale
 
-        def on_scalar(dst, src):
-            nc.scalar.activation(dst, src, ACT.Copy)
-
-        list1 = keep.tile([P, S // 16], U16, name="list1")
-        list2 = keep.tile([P, S // 16], U16, name="list2")
-        v_scale_rows = held([P, T], U8, "v_scale_rows")
-        v2_scale_rows = held([P, T], U8, "v2_scale_rows")
-        w1_scale_rows = held([P, 2, H], U8, "w1_scale_rows")
-        v_scale = [held([P, S], U8, f"v_scale{a}") for a in range(2)]
-        w3_scale = held([P, N], U8, "w3_scale")
-        nc.gpsimd.memset(v2_scale_rows[:].bitcast(I32), 0)
-        for tile in (v_scale_rows, w1_scale_rows, v_scale[0], v_scale[1], w3_scale):
-            nc.vector.memset(tile[:].bitcast(I32), 0)
-
-        def move_v_scale(a):
-            for r in range(4):
-                nc.sync.dma_start(
-                    v_scale[a][r:P:32, :].bitcast(I32), v_scale_picked[8 * r + 4 * a : P : 32, :].bitcast(I32)
-                )
+        def deal_w1_scale(g):
+            scale = held([P, 2, PASS], U8, f"w1_scale{g}")
+            nc.gpsimd.tensor_copy(
+                scale[:].rearrange("p a (t m) -> p a t m", t=PACK),
+                w1_scale_rows[:, :, PASS * g : PASS * (g + 1)].rearrange("p a (m t) -> p a t m", t=PACK),
+            )
+            return scale
 
         def load_w1(g):
             raw = held([P, 2, 2 * PASS], U8, f"w1_raw{g}")
@@ -108,191 +95,259 @@ def tile_list_wake_correction_kernel(
             nc.sync.dma_start(raw[:].bitcast(I32), columns.bitcast(I32))
             return raw
 
-        def deal_w1(g, tag=""):
-            scale = held([P, 2, PASS], U8, f"w1_scale{g}")
-            nc.gpsimd.tensor_copy(
-                scale[:].rearrange("p a (t m) -> p a t m", t=PACK),
-                w1_scale_rows[:, :, PASS * g : PASS * (g + 1)].rearrange("p a (m t) -> p a t m", t=PACK),
-            )
-            w1_scale.append(scale)
-            codes = held([P, 2, 2 * PASS], U8, f"w1_codes{g}", tag)
-            nc.gpsimd.tensor_copy(
+        def deal_w1_codes(g, copy):
+            codes = held([P, 2, 2 * PASS], U8, f"w1_codes{g}")
+            copy(
                 codes[:].bitcast(U16).rearrange("p a (t m) -> p a t m", t=PACK),
                 w1_raw[g][:].bitcast(U16).rearrange("p a (m t) -> p a t m", t=PACK),
             )
             return codes
 
-        w2_raw, v_words, w1_scale = [], [], []
-        w3_codes = held([P, GROUPS, N], U32, "w3_codes")
-        v2_rows = tab2_scales[0].rearrange("(d r) t -> r d t", r=4)
-        nc.sync.dma_start(list1[:], offs)
+        list1 = keep.tile([P, S // 16], U16, name="list1")
+        list2 = keep.tile([P, S // 16], U16, name="list2")
+        v_scale_rows = held([P, T], U8, "v_scale_rows")
+        v2_scale_rows = held([P, T], U8, "v2_scale_rows")
+        w1_scale_rows = held([P, 2, H], U8, "w1_scale_rows")
+        w3_scale = held([P, N], U8, "w3_scale")
+        v_scale = held([P, 2, S], U8, "v_scale")
+        nc.gpsimd.memset(v_scale_rows[:].bitcast(I32), 0)
+        nc.vector.memset(v2_scale_rows[:].bitcast(I32), 0)
+        nc.vector.memset(w1_scale_rows[:].bitcast(I32), 0)
+        nc.vector.memset(v_scale[:].bitcast(I32), 0)
+        nc.gpsimd.memset(w3_scale[:].bitcast(I32), 0)
+
         nc.sync.dma_start(list2[:], offs2)
+        nc.sync.dma_start(list1[:], offs)
         nc.sync.dma_start(v_scale_rows[0:P:4, :].bitcast(I32), tab_scales.rearrange("a q t -> q a t").bitcast(I32))
-        w2_raw.extend(load_w2(0, CHUNK))
-        w2_raw.extend(load_w2(CHUNK, CHUNK))
-        for r in range(4):
-            nc.scalar.dma_start(v2_scale_rows[r:P:32, :].bitcast(I32), v2_rows[r].bitcast(I32))
+        for d in range(4):
+            rows = slice(32 * d + V2_ROW, 32 * d + V2_ROW + 4)
+            nc.scalar.dma_start(v2_scale_rows[rows, :].bitcast(I32), tab2_scales[0, 4 * d : 4 * d + 4, :].bitcast(I32))
+        w2_raw = [load_w2(0, PASS)]
         v2_words = load_table(tab2_words[0], "v2_words")
-
-        v_scale_picked = held([P, S], U8, "v_scale_picked")
-        nc.vector.tensor_copy(v_scale_picked[:], v_scale_rows[:].indirect(list1[:]))
-        v2_scale_first = held([P, EARLY], U8, "v2_scale_first")
-        nc.vector.tensor_copy(v2_scale_first[:], v2_scale_rows[:].indirect(list2[:, 0 : EARLY // 16]))
-        w2_mx = [quantise_w2(0, w2_raw[0:2], [on_scalar, on_scalar])]
-        v2_first = held([P, 2, BLOCK], U32, "v2_first", "w2_raw256")
-        for block in range(2):
-            entries = list2[:, LIST_COLS * block : LIST_COLS * (block + 1)]
-            nc.vector.tensor_copy(v2_first[:, block, :], v2_words[:].bitcast(U32).indirect(entries))
-        v2_scale_rest = held([P, S - EARLY], U8, "v2_scale_rest", "w2_grouped0")
-        nc.vector.tensor_copy(v2_scale_rest[:], v2_scale_rows[:].indirect(list2[:, EARLY // 16 : S // 16]))
-        v2_rest = held([P, 2 * BLOCK], U32, "v2_rest", "v2_scale_rows")
-        nc.vector.tensor_copy(v2_rest[:], v2_words[:].bitcast(U32).indirect(list2[:, 2 * LIST_COLS : S // 16]))
-        v2_codes = [v2_first[:, 0, :], v2_first[:, 1, :], v2_rest[:, 0:BLOCK], v2_rest[:, BLOCK : 2 * BLOCK]]
-
-        def v2_scale(first):
-            if first < EARLY:
-                return v2_scale_first[:, first : first + UNIT]
-            return v2_scale_rest[:, first - EARLY : first - EARLY + UNIT]
-
-        move_v_scale(0)
-        v_words.append(load_table(tab_words[0], "v_words0"))
         for d in range(4):
             rows = w1_scales[:, 4 * d : 4 * d + 4, :].rearrange("a r c -> r a c")
             nc.sync.dma_start(w1_scale_rows[32 * d : 32 * d + 4, :, :].bitcast(I32), rows.bitcast(I32))
         w1_raw = [load_w1(0)]
+        v_words = [load_table(tab_words[0], "v_words0")]
+        v_scale_picked = pick_bytes(v_scale_rows, list1, 0, S, "v_scale_picked")
+        for d in range(4):
+            nc.sync.dma_start(
+                v_scale[32 * d : 32 * d + 4, :, :].bitcast(I32),
+                v_scale_picked[32 * d : 32 * d + 32 : 4, :].bitcast(I32),
+            )
         v_words.append(load_table(tab_words[1], "v_words1"))
-        move_v_scale(1)
-        w2_raw.extend(load_w2(2 * CHUNK, CHUNK))
-        w2_raw.extend(load_w2(3 * CHUNK, CHUNK))
+        w2_raw.append(load_w2(2 * CHUNK, CHUNK))
+        w2_raw.append(load_w2(3 * CHUNK, CHUNK))
         w1_raw.append(load_w1(1))
+        w3_codes = held([P, GROUPS, N], U32, "w3_codes")
         nc.sync.dma_start(w3_codes[:].bitcast(I32), w3_words.rearrange("a p c i -> p a (c i)").bitcast(I32))
-        load_two_planes(nc.sync, w3_scale, w3_scales)
+        for d in range(4):
+            rows = slice(32 * d + W3_ROW, 32 * d + W3_ROW + 8)
+            nc.sync.dma_start(w3_scale[rows, :].bitcast(I32), w3_scales[:, 4 * d : 4 * d + 4, :].bitcast(I32))
 
-        def gaussian(v2_codes, block, g, banks, tag=""):
+        w2_grouped = [held([P, PACK, P, PACK], BF16, f"w2_grouped{g}") for g in range(GROUPS)]
+        round_w2(0, 0, w2_raw[0][:, :, 0:SCALAR_SHARE], "scalar")
+        round_w2(0, SCALAR_SHARE, w2_raw[0][:, :, SCALAR_SHARE:PASS], "gpsimd")
+        v2_scale = [pick_bytes(v2_scale_rows, list2, 0, S - BLOCK, "v2_scale0")]
+        w2_mx = [quantise(w2_grouped[0][:].rearrange("p t m j -> p (t m j)"), PASS, "w2_0")]
+        v2_codes = held([P, S], U32, "v2_codes", "w2_grouped0")
+        for first, stop in ((0, UNIT), (UNIT, S // 2), (S // 2, S)):
+            picked = v2_words[:].bitcast(U32).indirect(entries(list2, first, stop - first))
+            nc.vector.tensor_copy(v2_codes[:, first:stop], picked)
+
+        def v2_operand(first, width):
+            codes = v2_codes[:, first : first + width]
+            part, at = divmod(first, S - BLOCK)
+            return codes.bitcast(FP8X4), v2_scale[part][V2_ROW:P, at : at + width]
+
+        w1_scale = [deal_w1_scale(0)]
+        w1_codes = [deal_w1_codes(0, nc.gpsimd.tensor_copy)]
+        w1_scale.append(deal_w1_scale(1))
+
+        def gaussian_by_units(step):
+            g, block = divmod(step, BLOCKS)
             codes, scale = w2_mx[g]
-            squares = held([P, 2, UNIT, PACK], F32, f"squares{block}_{g}", tag)
+            share = held([P, BLOCK, 2, 2], F32, f"share{step}")
             for half in range(2):
-                b = bank([P, PACK, UNIT], "b", banks[half])
-                first = BLOCK * block + UNIT * half
+                squares = held([P, UNIT, PACK], F32, f"squares{step}_{half}")
+                b = bank([P, PACK, UNIT], "b", MAST_BANKS[step] + half)
+                rhs, rhs_scale = v2_operand(BLOCK * block + UNIT * half, UNIT)
                 for t in range(PACK):
                     cols = slice(P * t, P * (t + 1))
                     nc.tensor.matmul_mx(
                         out=b[:, t, :],
                         lhsT=codes[:, cols].bitcast(FP8X4),
                         lhsT_scale=scale[:, cols],
-                        rhs=v2_codes[:, UNIT * half : UNIT * (half + 1)].bitcast(FP8X4),
-                        rhs_scale=v2_scale(first),
+                        rhs=rhs,
+                        rhs_scale=rhs_scale,
                         start=True,
                         stop=True,
                     )
-                nc.scalar.activation(squares[:, half, :, :], b[:].rearrange("p t n -> p n t"), ACT.Square)
-            share = held([P, 2, UNIT, PACK], F32, f"share{block}_{g}")
-            nc.scalar.activation(share[:], squares[:], ACT.Exp, scale=-1.0)
+                rows = slice(UNIT * half, UNIT * (half + 1))
+                nc.scalar.activation(squares[:], b[:].rearrange("p t n -> p n t"), ACT.Square)
+                nc.scalar.activation(
+                    share[:, rows, :, :].rearrange("p n h u -> p n (h u)"), squares[:], ACT.Exp, scale=-1.0
+                )
             return share
 
-        def corrected(v_codes, share, minus_h, block, g, half, number):
-            acc = bank([P, PACK, UNIT], "a", number)
-            first = BLOCK * block + UNIT * half
-            for t in range(PACK):
-                for a in (1, 0):
+        def gaussian(step):
+            g, block = divmod(step, BLOCKS)
+            codes, scale = w2_mx[g]
+            if step in (0, 2 * BLOCKS - 1):
+                return gaussian_by_units(step)
+            squares = held([P, 2, BLOCK, 2], F32, f"squares{step}")
+            rhs, rhs_scale = v2_operand(BLOCK * block, BLOCK)
+            for pair in range(2):
+                b = bank([P, 2, BLOCK], "b", MAST_BANKS[step] + pair)
+                for u in range(2):
+                    cols = slice(P * (2 * pair + u), P * (2 * pair + u + 1))
                     nc.tensor.matmul_mx(
-                        out=acc[:, t, :],
-                        lhsT=w1_codes[g][:, a, 2 * P * t : 2 * P * (t + 1)].bitcast(FP4X4),
-                        lhsT_scale=w1_scale[g][:, a, P * t : P * (t + 1)],
-                        rhs=v_codes[:, a, UNIT * half : UNIT * (half + 1)].bitcast(FP8X4),
-                        rhs_scale=v_scale[a][:, first : first + UNIT],
-                        start=(a == 1),
-                        stop=(a == 0),
+                        out=b[:, u, :],
+                        lhsT=codes[:, cols].bitcast(FP8X4),
+                        lhsT_scale=scale[:, cols],
+                        rhs=rhs,
+                        rhs_scale=rhs_scale,
+                        start=True,
+                        stop=True,
                     )
+                nc.scalar.activation(squares[:, pair, :, :], b[:].rearrange("p u n -> p n u"), ACT.Square)
+            share = held([P, BLOCK, 2, 2], F32, f"share{step}")
+            nc.scalar.activation(share[:], squares[:].rearrange("p h n u -> p n h u"), ACT.Exp, scale=-1.0)
+            return share
+
+        def rotor_pass(unit, a):
+            g, first = unit // 8, UNIT * (unit % 8)
+            for t in range(PACK):
+                nc.tensor.matmul_mx(
+                    out=rotor[unit][:, t, :],
+                    lhsT=w1_codes[g][:, a, 2 * P * t : 2 * P * (t + 1)].bitcast(FP4X4),
+                    lhsT_scale=w1_scale[g][:, a, P * t : P * (t + 1)],
+                    rhs=v_codes[a][:, first : first + UNIT].bitcast(FP8X4),
+                    rhs_scale=v_scale[:, a, first : first + UNIT],
+                    start=(a == 0 and t == 0),
+                    stop=(a == 1 and t == PACK - 1),
+                )
+
+        def correct(unit):
+            step, half = divmod(unit, 2)
             nc.vector.scalar_tensor_tensor(
-                out=minus_h[:, half, :, :],
-                in0=share[:, half, :, :],
+                out=minus_h[step][:, UNIT * half : UNIT * (half + 1), :],
+                in0=shares[step][:, UNIT * half : UNIT * (half + 1), :, :].rearrange("p n h u -> p n (h u)"),
                 scalar=1.0,
-                in1=acc[:].rearrange("p t n -> p n t"),
+                in1=rotor[unit][:].rearrange("p t n -> p n t"),
                 op0=ALU.subtract,
                 op1=ALU.mult,
             )
 
-        def quantise_h(minus_h, block, g):
-            codes = held([P, BLOCK], U32, f"h_codes{block}_{g}")
-            scale = held([P, BLOCK], U8, f"h_scale{block}_{g}")
-            nc.vector.quantize_mx(
-                out=codes[:].bitcast(FP8X4), scales=scale[:], in_=minus_h[:].rearrange("p u n t -> p (u n t)")
-            )
-            return codes, scale
+        def leave(result, acc, engine):
+            if engine == "vector":
+                nc.vector.tensor_scalar_mul(result, acc, -1.0)
+            else:
+                nc.scalar.activation(result, acc, ACT.Copy, scale=-1.0)
 
-        def read_out(h_mx, block, pair, number, on_vector):
-            acc = bank([P, 2, BLOCK], "out", number)
+        def out_pass(acc, pair, g, operand, width, start, stop):
             for u in range(2):
                 cols = slice(P * (2 * pair + u), P * (2 * pair + u + 1))
-                for g in (1, 0):
-                    nc.tensor.matmul_mx(
-                        out=acc[:, u, :],
-                        lhsT=w3_codes[:, g, cols].bitcast(FP8X4),
-                        lhsT_scale=w3_scale[4 * g : P, cols],
-                        rhs=h_mx[block, g][0][:].bitcast(FP8X4),
-                        rhs_scale=h_mx[block, g][1][:],
-                        start=(g == 1),
-                        stop=(g == 0),
-                    )
-            result = ring.tile([P, 2, BLOCK], F32, name="result", bufs=4)
-            if on_vector:
-                nc.vector.tensor_scalar_mul(result[:], acc[:], -1.0)
-            else:
-                nc.scalar.activation(result[:], acc[:], ACT.Copy, scale=-1.0)
-            rows = out[2 * P * pair : 2 * P * (pair + 1), BLOCK * block : BLOCK * (block + 1)]
+                nc.tensor.matmul_mx(
+                    out=acc[:, u, :],
+                    lhsT=w3_codes[:, g, cols].bitcast(FP8X4),
+                    lhsT_scale=w3_scale[W3_ROW + 4 * g : P, cols],
+                    rhs=operand[0].bitcast(FP8X4),
+                    rhs_scale=operand[1],
+                    start=(start and u == 0),
+                    stop=(stop and u == 1),
+                )
+
+        def store(acc, pair, first, width, engine):
+            result = held([P, 2, width], F32, f"result{first}_{pair}")
+            leave(result[:], acc[:], engine)
+            rows = out[2 * P * pair : 2 * P * (pair + 1), first : first + width]
             nc.sync.dma_start(rows.rearrange("(u p) c -> p u c", p=P), result[:])
 
-        def read_out_last(h_mx, block):
-            accs = [bank([P, BLOCK], "out_last", (4, 5, 0, 1)[n]) for n in range(N // P)]
+        def read_out(block, pair, number, engine):
+            acc = bank([P, 2, BLOCK], "out", number)
             for g in range(GROUPS):
-                for n, acc in enumerate(accs):
-                    cols = slice(P * n, P * (n + 1))
-                    nc.tensor.matmul_mx(
-                        out=acc[:],
-                        lhsT=w3_codes[:, g, cols].bitcast(FP8X4),
-                        lhsT_scale=w3_scale[4 * g : P, cols],
-                        rhs=h_mx[block, g][0][:].bitcast(FP8X4),
-                        rhs_scale=h_mx[block, g][1][:],
-                        start=(g == 0),
-                        stop=(g == GROUPS - 1),
-                    )
-            for n, acc in enumerate(accs):
-                result = held([P, BLOCK], F32, f"result_last{n}")
-                if n % 2:
-                    nc.vector.tensor_scalar_mul(result[:], acc[:], -1.0)
-                else:
-                    nc.scalar.activation(result[:], acc[:], ACT.Copy, scale=-1.0)
-                nc.sync.dma_start(out[P * n : P * (n + 1), BLOCK * block : BLOCK * (block + 1)], result[:])
+                codes, scale = h_mx[BLOCKS * g + block]
+                out_pass(acc, pair, g, (codes, scale), BLOCK, g == 0, g == 1)
+            store(acc, pair, BLOCK * block, BLOCK, engine)
 
-        last = BLOCKS - 1
-        first_banks = {0: (0, 1), 1: (6, 7), 2: (4, 5), 3: (0, 1)}
-        shares = {}
-        for block in range(last):
-            shares[block, 0] = gaussian(v2_codes[block], block, 0, first_banks[block])
-        w1_codes = [deal_w1(g) for g in range(GROUPS)]
-        w2_mx.append(quantise_w2(1, w2_raw[2:], [on_scalar, nc.vector.tensor_copy]))
-        shares[last, 0] = gaussian(v2_codes[last], last, 0, first_banks[last], "w2_raw512")
-        for block in range(BLOCKS):
-            shares[block, 1] = gaussian(v2_codes[block], block, 1, (0, 1) if block % 2 else (4, 5))
+        early = 6
+        last = 2 * BLOCKS - 1
+        rotor_banks = [2, 3, 4, 5, 6, 7, 2, 3, 6, 7, 2, 3, 6, 7, 2, 3]
+        shares = {0: gaussian(0)}
+        v2_scale.append(pick_bytes(v2_scale_rows, list2, S - BLOCK, BLOCK, "v2_scale1", "v2_words"))
+        for step in range(1, BLOCKS):
+            shares[step] = gaussian(step)
+        v_codes = [held([P, S], U32, f"v_codes{a}") for a in range(2)]
+        for a, cuts in enumerate(((0, S // 2, S), (0, BLOCK, S // 2, S))):
+            for first, stop in zip(cuts, cuts[1:]):
+                picked = v_words[a][:].bitcast(U32).indirect(entries(list1, first, stop - first))
+                nc.vector.tensor_copy(v_codes[a][:, first:stop], picked)
+        rotor = {}
+        for unit in range(early):
+            rotor[unit] = bank([P, PACK, UNIT], "a", rotor_banks[unit])
+            rotor_pass(unit, 0)
+        round_w2(1, 0, w2_raw[1][:], "gpsimd")
+        round_w2(1, CHUNK, w2_raw[2][:], "scalar")
+        w2_mx.append(quantise(w2_grouped[1][:].rearrange("p t m j -> p (t m j)"), PASS, "w2_1"))
+        w1_codes.append(deal_w1_codes(1, nc.scalar.copy))
+        shares[BLOCKS] = gaussian(BLOCKS)
+        pairs_h = [held([P, 2, BLOCK, PACK], BF16, f"pair_h{pair}") for pair in range(2)]
+        minus_h = {step: pairs_h[step // 2][:, step % 2, :, :] for step in range(BLOCKS)}
+        h_mx = {}
 
-        steps = [(block, g) for g in range(GROUPS) for block in range(BLOCKS)]
-        units = [(block, g, half) for block, g in steps for half in range(2)]
-        minus_h, h_mx = {}, {}
-        v_codes = {block: pick(v_words, list1, block, f"v_codes{block}", "") for block in range(BLOCKS)}
-        a_banks = [(2, 3), (6, 7), (2, 3), (6, 7), (2, 3), (6, 7), (4, 5), (6, 7)]
-        out_banks = [(2, 3), (0, 1), (2, 3)]
-        on_vector = {(0, 0), (0, 1), (2, 1)}
-        for k, (block, g) in enumerate(steps):
-            minus_h[block, g] = ring.tile([P, 2, UNIT, PACK], BF16, name="minus_h", align_bytes=256)
-            corrected(v_codes[block], shares[block, g], minus_h[block, g], block, g, 0, a_banks[k][0])
-            if 1 <= k <= 4:
-                h_mx[steps[k - 1]] = quantise_h(minus_h[steps[k - 1]], *steps[k - 1])
-            corrected(v_codes[block], shares[block, g], minus_h[block, g], block, g, 1, a_banks[k][1])
-            if g == 1 and block >= 1:
-                read_out(h_mx, block - 1, 0, out_banks[block - 1][0], (block - 1, 0) in on_vector)
-            if k >= 4:
-                h_mx[block, g] = quantise_h(minus_h[block, g], block, g)
-            if g == 1 and block >= 1:
-                read_out(h_mx, block - 1, 1, out_banks[block - 1][1], (block - 1, 1) in on_vector)
-        read_out_last(h_mx, last)
+        def quantise_h(step):
+            if step < BLOCKS:
+                if step % 2:
+                    values = pairs_h[step // 2][:].rearrange("p s n t -> p (s n t)")
+                    codes, scale = quantise(values, 2 * BLOCK, f"h{step}")
+                    for s in range(2):
+                        cols = slice(BLOCK * s, BLOCK * (s + 1))
+                        h_mx[step - 1 + s] = (codes[:, cols], scale[:, cols])
+                return
+            codes, scale = quantise(minus_h[step].rearrange("p n t -> p (n t)"), BLOCK, f"h{step}")
+            h_mx[step] = (codes[:], scale[:])
+
+        def rotor_unit(unit):
+            if unit not in rotor:
+                rotor[unit] = bank([P, PACK, UNIT], "a", rotor_banks[unit])
+                rotor_pass(unit, 0)
+            rotor_pass(unit, 1)
+            correct(unit)
+
+        for step in range(last):
+            if step not in minus_h:
+                tile = held([P, BLOCK, PACK], BF16, f"minus_h{step}")
+                minus_h[step] = tile[:]
+            if step in (2, 3, 5):
+                later = {2: 5, 3: 6, 5: 7}[step]
+                shares[later] = gaussian(later)
+            rotor_unit(2 * step)
+            if step >= 1:
+                quantise_h(step - 1)
+            rotor_unit(2 * step + 1)
+            if step >= 5:
+                for pair in range(2):
+                    read_out(step - 5, pair, (0, 4)[step - 5] + pair, "scalar")
+
+        first = BLOCK * (BLOCKS - 1)
+        last_h = held([P, BLOCK, PACK], BF16, "last_h")
+        minus_h[last] = last_h[:]
+        halves = [minus_h[last][:, UNIT * half : UNIT * (half + 1), :].rearrange("p n t -> p (n t)") for half in range(2)]
+        rotor_unit(2 * last)
+        quantise_h(last - 1)
+        rotor_unit(2 * last + 1)
+        tail_mx = [quantise(halves[0], UNIT, "h_tail0")]
+        tail_mx.append(quantise(halves[1], UNIT, "h_tail1"))
+        read_out(2, 0, 6, "vector")
+        read_out(2, 1, 7, "vector")
+        codes, scale = h_mx[BLOCKS - 1]
+        tail_banks = [(0, 1), (2, 3)]
+        for half in range(2):
+            cols = slice(UNIT * half, UNIT * (half + 1))
+            accs = [bank([P, 2, UNIT], "out_tail", tail_banks[half][pair]) for pair in range(2)]
+            for pair in range(2):
+                out_pass(accs[pair], pair, 0, (codes[:, cols], scale[:, cols]), UNIT, True, False)
+            for pair in range(2):
+                out_pass(accs[pair], pair, 1, (tail_mx[half][0][:], tail_mx[half][1][:]), UNIT, False, True)
+                store(accs[pair], pair, first + UNIT * half, UNIT, ("scalar", "vector")[pair])

@@ -24,8 +24,8 @@ BLOCK = 256
 BLOCKS = S // BLOCK
 UNIT = 128
 CHUNK = 256
-SCALAR_SHARE = 384
-MAST_BANKS = (0, 0, 6, 0, 0, 4, 0, 4)
+EARLY = 512
+AHEAD = 4
 V2_ROW = 8
 W3_ROW = 4
 
@@ -53,41 +53,10 @@ def tile_list_wake_correction_kernel(
             nc.sync.dma_start(window[:], words.rearrange("p t i -> p (t i)").bitcast(I32))
             return window
 
-        def load_w2(first, width):
-            raw = held([P, PACK, width], F32, f"w2_raw{first}")
-            nc.sync.dma_start(raw[:], w2.rearrange("(p j) c -> p j c", j=PACK)[:, :, first : first + width])
+        def load_w2(chunk, raw):
+            columns = w2.rearrange("(p j) c -> p j c", j=PACK)[:, :, CHUNK * chunk : CHUNK * (chunk + 1)]
+            nc.sync.dma_start(raw[:], columns)
             return raw
-
-        def pick_bytes(window, offsets, first, count, name, tag=""):
-            picked = held([P, count], U8, name, tag)
-            nc.vector.tensor_copy(picked[:], window[:].indirect(entries(offsets, first, count)))
-            return picked
-
-        def round_w2(g, first, columns, engine):
-            dst = w2_grouped[g][:, :, first // PACK : (first + columns.shape[2]) // PACK, :]
-            src = columns.rearrange("p j (m t) -> p t m j", t=PACK)
-            if engine == "gpsimd":
-                nc.gpsimd.tensor_copy(dst, src)
-                return
-            dst, src = dst.rearrange("p t m j -> p m j t"), src.rearrange("p t m j -> p m j t")
-            if engine == "scalar":
-                nc.scalar.activation(dst, src, ACT.Copy)
-            else:
-                nc.vector.tensor_copy(dst, src)
-
-        def quantise(values, width, name, tag=""):
-            codes = held([P, width], U32, f"{name}_codes", tag)
-            scale = held([P, width], U8, f"{name}_scale")
-            nc.vector.quantize_mx(out=codes[:].bitcast(FP8X4), scales=scale[:], in_=values)
-            return codes, scale
-
-        def deal_w1_scale(g):
-            scale = held([P, 2, PASS], U8, f"w1_scale{g}")
-            nc.gpsimd.tensor_copy(
-                scale[:].rearrange("p a (t m) -> p a t m", t=PACK),
-                w1_scale_rows[:, :, PASS * g : PASS * (g + 1)].rearrange("p a (m t) -> p a t m", t=PACK),
-            )
-            return scale
 
         def load_w1(g):
             raw = held([P, 2, 2 * PASS], U8, f"w1_raw{g}")
@@ -95,9 +64,41 @@ def tile_list_wake_correction_kernel(
             nc.sync.dma_start(raw[:].bitcast(I32), columns.bitcast(I32))
             return raw
 
-        def deal_w1_codes(g, copy):
-            codes = held([P, 2, 2 * PASS], U8, f"w1_codes{g}")
+        def pick_bytes(window, offsets, first, count, name, tag=""):
+            picked = held([P, count], U8, name, tag)
+            nc.vector.tensor_copy(picked[:], window[:].indirect(entries(offsets, first, count)))
+            return picked
+
+        def pick_words(window, offsets, cuts, name, tag=""):
+            picked = held([P, S], U32, name, tag)
+            for first, stop in zip(cuts, cuts[1:]):
+                looked_up = window[:].bitcast(U32).indirect(entries(offsets, first, stop - first))
+                nc.vector.tensor_copy(picked[:, first:stop], looked_up)
+            return picked
+
+        def on_scalar(dst, src):
+            nc.scalar.activation(dst, src, ACT.Copy)
+
+        def round_w2(chunk, copy):
+            g, half = divmod(chunk, 2)
+            rows = slice(CHUNK // PACK * half, CHUNK // PACK * (half + 1))
             copy(
+                w2_grouped[g][:, :, rows, :].rearrange("p t m j -> p m j t"),
+                w2_raw[chunk][:].rearrange("p j (m t) -> p m j t", t=PACK),
+            )
+
+        def quantise(values, codes, name):
+            scale = held(list(codes.shape), U8, f"{name}_scale")
+            nc.vector.quantize_mx(out=codes[:].bitcast(FP8X4), scales=scale[:], in_=values)
+            return codes, scale
+
+        def quantise_w2(g):
+            codes = held([P, PASS], U32, f"w2_codes{g}")
+            return quantise(w2_grouped[g][:].rearrange("p t m j -> p (t m j)"), codes, f"w2_{g}")
+
+        def deal_w1_codes(g, tag=""):
+            codes = held([P, 2, 2 * PASS], U8, f"w1_codes{g}", tag)
+            nc.gpsimd.tensor_copy(
                 codes[:].bitcast(U16).rearrange("p a (t m) -> p a t m", t=PACK),
                 w1_raw[g][:].bitcast(U16).rearrange("p a (m t) -> p a t m", t=PACK),
             )
@@ -107,37 +108,46 @@ def tile_list_wake_correction_kernel(
         list2 = keep.tile([P, S // 16], U16, name="list2")
         v_scale_rows = held([P, T], U8, "v_scale_rows")
         v2_scale_rows = held([P, T], U8, "v2_scale_rows")
-        w1_scale_rows = held([P, 2, H], U8, "w1_scale_rows")
+        w1_scale_rows = held([P, H], U8, "w1_scale_rows")
         w3_scale = held([P, N], U8, "w3_scale")
-        v_scale = held([P, 2, S], U8, "v_scale")
-        nc.gpsimd.memset(v_scale_rows[:].bitcast(I32), 0)
-        nc.vector.memset(v2_scale_rows[:].bitcast(I32), 0)
-        nc.vector.memset(w1_scale_rows[:].bitcast(I32), 0)
-        nc.vector.memset(v_scale[:].bitcast(I32), 0)
-        nc.gpsimd.memset(w3_scale[:].bitcast(I32), 0)
+        planes = [held([P, S + H], U8, f"planes{a}") for a in range(2)]
+        for tile in (v_scale_rows, w1_scale_rows):
+            nc.gpsimd.memset(tile[:].bitcast(I32), 0)
+        for tile in (v2_scale_rows, planes[0], planes[1], w3_scale):
+            nc.vector.memset(tile[:].bitcast(I32), 0)
 
-        nc.sync.dma_start(list2[:], offs2)
+        def move_planes(a):
+            for r in range(4):
+                nc.sync.dma_start(planes[a][r:P:32, :].bitcast(I32), staged[8 * r + 4 * a : P : 32, :].bitcast(I32))
+
+        w2_raw = [held([P, PACK, CHUNK], F32, f"w2_raw{chunk}") for chunk in range(4)]
         nc.sync.dma_start(list1[:], offs)
+        nc.sync.dma_start(list2[:], offs2)
         nc.sync.dma_start(v_scale_rows[0:P:4, :].bitcast(I32), tab_scales.rearrange("a q t -> q a t").bitcast(I32))
-        for d in range(4):
-            rows = slice(32 * d + V2_ROW, 32 * d + V2_ROW + 4)
-            nc.scalar.dma_start(v2_scale_rows[rows, :].bitcast(I32), tab2_scales[0, 4 * d : 4 * d + 4, :].bitcast(I32))
-        w2_raw = [load_w2(0, PASS)]
+        load_w2(0, w2_raw[0])
+        load_w2(1, w2_raw[1])
+        v2_rows = tab2_scales[0].rearrange("(d r) t -> r d t", r=4)
+        for r in range(4):
+            nc.scalar.dma_start(v2_scale_rows[V2_ROW + r : P : 32, :].bitcast(I32), v2_rows[r].bitcast(I32))
+        nc.gpsimd.dma_start(w1_scale_rows[0:P:4, :].bitcast(I32), w1_scales.rearrange("a q c -> q a c").bitcast(I32))
         v2_words = load_table(tab2_words[0], "v2_words")
-        for d in range(4):
-            rows = w1_scales[:, 4 * d : 4 * d + 4, :].rearrange("a r c -> r a c")
-            nc.sync.dma_start(w1_scale_rows[32 * d : 32 * d + 4, :, :].bitcast(I32), rows.bitcast(I32))
         w1_raw = [load_w1(0)]
         v_words = [load_table(tab_words[0], "v_words0")]
+
         v_scale_picked = pick_bytes(v_scale_rows, list1, 0, S, "v_scale_picked")
-        for d in range(4):
-            nc.sync.dma_start(
-                v_scale[32 * d : 32 * d + 4, :, :].bitcast(I32),
-                v_scale_picked[32 * d : 32 * d + 32 : 4, :].bitcast(I32),
-            )
+        staged = held([P, S + H], U8, "staged")
+        nc.gpsimd.tensor_copy(
+            staged[:, S : S + H].rearrange("p (g t m) -> p g t m", g=GROUPS, t=PACK),
+            w1_scale_rows[:].rearrange("p (g m t) -> p g t m", g=GROUPS, t=PACK),
+        )
+        nc.vector.tensor_copy(staged[:, 0:S].bitcast(I32), v_scale_picked[:].bitcast(I32))
+        v2_scale = [pick_bytes(v2_scale_rows, list2, 0, EARLY, "v2_scale0")]
+
+        move_planes(0)
         v_words.append(load_table(tab_words[1], "v_words1"))
-        w2_raw.append(load_w2(2 * CHUNK, CHUNK))
-        w2_raw.append(load_w2(3 * CHUNK, CHUNK))
+        move_planes(1)
+        load_w2(2, w2_raw[2])
+        load_w2(3, w2_raw[3])
         w1_raw.append(load_w1(1))
         w3_codes = held([P, GROUPS, N], U32, "w3_codes")
         nc.sync.dma_start(w3_codes[:].bitcast(I32), w3_words.rearrange("a p c i -> p a (c i)").bitcast(I32))
@@ -146,208 +156,196 @@ def tile_list_wake_correction_kernel(
             nc.sync.dma_start(w3_scale[rows, :].bitcast(I32), w3_scales[:, 4 * d : 4 * d + 4, :].bitcast(I32))
 
         w2_grouped = [held([P, PACK, P, PACK], BF16, f"w2_grouped{g}") for g in range(GROUPS)]
-        round_w2(0, 0, w2_raw[0][:, :, 0:SCALAR_SHARE], "scalar")
-        round_w2(0, SCALAR_SHARE, w2_raw[0][:, :, SCALAR_SHARE:PASS], "gpsimd")
-        v2_scale = [pick_bytes(v2_scale_rows, list2, 0, S - BLOCK, "v2_scale0")]
-        w2_mx = [quantise(w2_grouped[0][:].rearrange("p t m j -> p (t m j)"), PASS, "w2_0")]
-        v2_codes = held([P, S], U32, "v2_codes", "w2_grouped0")
-        for first, stop in ((0, UNIT), (UNIT, S // 2), (S // 2, S)):
-            picked = v2_words[:].bitcast(U32).indirect(entries(list2, first, stop - first))
-            nc.vector.tensor_copy(v2_codes[:, first:stop], picked)
+        round_w2(0, on_scalar)
+        round_w2(1, on_scalar)
+        w2_mx = [quantise_w2(0)]
+        w1_codes = [deal_w1_codes(0)]
+        v2_codes = pick_words(v2_words, list2, (0, UNIT, S // 2, S), "v2_codes", "w2_grouped0")
+        v2_scale.append(pick_bytes(v2_scale_rows, list2, EARLY, S - EARLY, "v2_scale1", "v2_words"))
 
-        def v2_operand(first, width):
-            codes = v2_codes[:, first : first + width]
-            part, at = divmod(first, S - BLOCK)
-            return codes.bitcast(FP8X4), v2_scale[part][V2_ROW:P, at : at + width]
-
-        w1_scale = [deal_w1_scale(0)]
-        w1_codes = [deal_w1_codes(0, nc.gpsimd.tensor_copy)]
-        w1_scale.append(deal_w1_scale(1))
-
-        def gaussian_by_units(step):
-            g, block = divmod(step, BLOCKS)
+        def mast_pass(acc, g, t, first, width):
             codes, scale = w2_mx[g]
-            share = held([P, BLOCK, 2, 2], F32, f"share{step}")
+            cols = slice(P * t, P * (t + 1))
+            part, at = divmod(first, EARLY)
+            nc.tensor.matmul_mx(
+                out=acc,
+                lhsT=codes[:, cols].bitcast(FP8X4),
+                lhsT_scale=scale[:, cols],
+                rhs=v2_codes[:, first : first + width].bitcast(FP8X4),
+                rhs_scale=v2_scale[part][V2_ROW:P, at : at + width],
+                start=True,
+                stop=True,
+            )
+
+        def gaussian_by_units(step, number):
+            g, block = divmod(step, BLOCKS)
             for half in range(2):
-                squares = held([P, UNIT, PACK], F32, f"squares{step}_{half}")
-                b = bank([P, PACK, UNIT], "b", MAST_BANKS[step] + half)
-                rhs, rhs_scale = v2_operand(BLOCK * block + UNIT * half, UNIT)
+                unit = 2 * step + half
+                b = bank([P, PACK, UNIT], "b", number + half)
                 for t in range(PACK):
-                    cols = slice(P * t, P * (t + 1))
-                    nc.tensor.matmul_mx(
-                        out=b[:, t, :],
-                        lhsT=codes[:, cols].bitcast(FP8X4),
-                        lhsT_scale=scale[:, cols],
-                        rhs=rhs,
-                        rhs_scale=rhs_scale,
-                        start=True,
-                        stop=True,
-                    )
-                rows = slice(UNIT * half, UNIT * (half + 1))
+                    mast_pass(b[:, t, :], g, t, BLOCK * block + UNIT * half, UNIT)
+                squares = held([P, UNIT, PACK], F32, f"squares_unit{unit}")
                 nc.scalar.activation(squares[:], b[:].rearrange("p t n -> p n t"), ACT.Square)
-                nc.scalar.activation(
-                    share[:, rows, :, :].rearrange("p n h u -> p n (h u)"), squares[:], ACT.Exp, scale=-1.0
-                )
-            return share
+                share = held([P, UNIT, PACK], F32, f"share_unit{unit}")
+                nc.scalar.activation(share[:], squares[:], ACT.Exp, scale=-1.0)
+                shares[unit] = share[:]
 
-        def gaussian(step):
+        def gaussian(step, number, tag=""):
             g, block = divmod(step, BLOCKS)
-            codes, scale = w2_mx[g]
-            if step in (0, 2 * BLOCKS - 1):
-                return gaussian_by_units(step)
-            squares = held([P, 2, BLOCK, 2], F32, f"squares{step}")
-            rhs, rhs_scale = v2_operand(BLOCK * block, BLOCK)
+            squares = held([P, 2, BLOCK, 2], F32, f"squares{step}", tag)
             for pair in range(2):
-                b = bank([P, 2, BLOCK], "b", MAST_BANKS[step] + pair)
+                b = bank([P, 2, BLOCK], "b", number + pair)
                 for u in range(2):
-                    cols = slice(P * (2 * pair + u), P * (2 * pair + u + 1))
-                    nc.tensor.matmul_mx(
-                        out=b[:, u, :],
-                        lhsT=codes[:, cols].bitcast(FP8X4),
-                        lhsT_scale=scale[:, cols],
-                        rhs=rhs,
-                        rhs_scale=rhs_scale,
-                        start=True,
-                        stop=True,
-                    )
+                    mast_pass(b[:, u, :], g, 2 * pair + u, BLOCK * block, BLOCK)
                 nc.scalar.activation(squares[:, pair, :, :], b[:].rearrange("p u n -> p n u"), ACT.Square)
             share = held([P, BLOCK, 2, 2], F32, f"share{step}")
             nc.scalar.activation(share[:], squares[:].rearrange("p h n u -> p n h u"), ACT.Exp, scale=-1.0)
-            return share
+            for half in range(2):
+                shares[2 * step + half] = share[:, UNIT * half : UNIT * (half + 1), :, :].rearrange("p n h u -> p n (h u)")
 
-        def rotor_pass(unit, a):
+        def rotor_pass(unit, a, start, stop):
             g, first = unit // 8, UNIT * (unit % 8)
             for t in range(PACK):
                 nc.tensor.matmul_mx(
                     out=rotor[unit][:, t, :],
                     lhsT=w1_codes[g][:, a, 2 * P * t : 2 * P * (t + 1)].bitcast(FP4X4),
-                    lhsT_scale=w1_scale[g][:, a, P * t : P * (t + 1)],
+                    lhsT_scale=planes[a][:, S + PASS * g + P * t : S + PASS * g + P * (t + 1)],
                     rhs=v_codes[a][:, first : first + UNIT].bitcast(FP8X4),
-                    rhs_scale=v_scale[:, a, first : first + UNIT],
-                    start=(a == 0 and t == 0),
-                    stop=(a == 1 and t == PACK - 1),
+                    rhs_scale=planes[a][:, first : first + UNIT],
+                    start=(start and t == 0),
+                    stop=(stop and t == PACK - 1),
                 )
 
+        def rotor_unit(unit, number):
+            rotor[unit] = bank([P, PACK, UNIT], "a", number)
+            rotor_pass(unit, 1, True, False)
+            rotor_pass(unit, 0, False, True)
+
         def correct(unit):
-            step, half = divmod(unit, 2)
             nc.vector.scalar_tensor_tensor(
-                out=minus_h[step][:, UNIT * half : UNIT * (half + 1), :],
-                in0=shares[step][:, UNIT * half : UNIT * (half + 1), :, :].rearrange("p n h u -> p n (h u)"),
+                out=minus_h[unit],
+                in0=shares[unit],
                 scalar=1.0,
                 in1=rotor[unit][:].rearrange("p t n -> p n t"),
                 op0=ALU.subtract,
                 op1=ALU.mult,
             )
 
-        def leave(result, acc, engine):
-            if engine == "vector":
-                nc.vector.tensor_scalar_mul(result, acc, -1.0)
-            else:
-                nc.scalar.activation(result, acc, ACT.Copy, scale=-1.0)
+        def quantise_h(tile, first, count):
+            g, at = divmod(first, 2 * BLOCKS)
+            cols = slice(UNIT * at, UNIT * (at + count))
+            nc.vector.quantize_mx(
+                out=h_codes[g][:, cols].bitcast(FP8X4),
+                scales=h_scale[g][:, cols],
+                in_=tile.rearrange("p u n t -> p (u n t)"),
+            )
 
-        def out_pass(acc, pair, g, operand, width, start, stop):
-            for u in range(2):
-                cols = slice(P * (2 * pair + u), P * (2 * pair + u + 1))
-                nc.tensor.matmul_mx(
-                    out=acc[:, u, :],
-                    lhsT=w3_codes[:, g, cols].bitcast(FP8X4),
-                    lhsT_scale=w3_scale[W3_ROW + 4 * g : P, cols],
-                    rhs=operand[0].bitcast(FP8X4),
-                    rhs_scale=operand[1],
-                    start=(start and u == 0),
-                    stop=(stop and u == 1),
-                )
+        def out_pass(acc, row_tile, g, first, width, start, stop):
+            cols = slice(P * row_tile, P * (row_tile + 1))
+            nc.tensor.matmul_mx(
+                out=acc,
+                lhsT=w3_codes[:, g, cols].bitcast(FP8X4),
+                lhsT_scale=w3_scale[W3_ROW + 4 * g : P, cols],
+                rhs=h_codes[g][:, first : first + width].bitcast(FP8X4),
+                rhs_scale=h_scale[g][:, first : first + width],
+                start=start,
+                stop=stop,
+            )
 
-        def store(acc, pair, first, width, engine):
+        def store(acc, pair, first, width, on_vector):
             result = held([P, 2, width], F32, f"result{first}_{pair}")
-            leave(result[:], acc[:], engine)
+            if on_vector:
+                nc.vector.tensor_scalar_mul(result[:], acc[:], -1.0)
+            else:
+                nc.scalar.activation(result[:], acc[:], ACT.Copy, scale=-1.0)
             rows = out[2 * P * pair : 2 * P * (pair + 1), first : first + width]
             nc.sync.dma_start(rows.rearrange("(u p) c -> p u c", p=P), result[:])
 
-        def read_out(block, pair, number, engine):
+        def multiply_out(block, pair, number):
             acc = bank([P, 2, BLOCK], "out", number)
             for g in range(GROUPS):
-                codes, scale = h_mx[BLOCKS * g + block]
-                out_pass(acc, pair, g, (codes, scale), BLOCK, g == 0, g == 1)
-            store(acc, pair, BLOCK * block, BLOCK, engine)
+                for u in range(2):
+                    out_pass(acc[:, u, :], 2 * pair + u, g, BLOCK * block, BLOCK, g + u == 0, g + u == 2)
+            return acc
 
-        early = 6
-        last = 2 * BLOCKS - 1
-        rotor_banks = [2, 3, 4, 5, 6, 7, 2, 3, 6, 7, 2, 3, 6, 7, 2, 3]
-        shares = {0: gaussian(0)}
-        v2_scale.append(pick_bytes(v2_scale_rows, list2, S - BLOCK, BLOCK, "v2_scale1", "v2_words"))
-        for step in range(1, BLOCKS):
-            shares[step] = gaussian(step)
-        v_codes = [held([P, S], U32, f"v_codes{a}") for a in range(2)]
-        for a, cuts in enumerate(((0, S // 2, S), (0, BLOCK, S // 2, S))):
-            for first, stop in zip(cuts, cuts[1:]):
-                picked = v_words[a][:].bitcast(U32).indirect(entries(list1, first, stop - first))
-                nc.vector.tensor_copy(v_codes[a][:, first:stop], picked)
-        rotor = {}
-        for unit in range(early):
-            rotor[unit] = bank([P, PACK, UNIT], "a", rotor_banks[unit])
-            rotor_pass(unit, 0)
-        round_w2(1, 0, w2_raw[1][:], "gpsimd")
-        round_w2(1, CHUNK, w2_raw[2][:], "scalar")
-        w2_mx.append(quantise(w2_grouped[1][:].rearrange("p t m j -> p (t m j)"), PASS, "w2_1"))
-        w1_codes.append(deal_w1_codes(1, nc.scalar.copy))
-        shares[BLOCKS] = gaussian(BLOCKS)
-        pairs_h = [held([P, 2, BLOCK, PACK], BF16, f"pair_h{pair}") for pair in range(2)]
-        minus_h = {step: pairs_h[step // 2][:, step % 2, :, :] for step in range(BLOCKS)}
-        h_mx = {}
-
-        def quantise_h(step):
-            if step < BLOCKS:
-                if step % 2:
-                    values = pairs_h[step // 2][:].rearrange("p s n t -> p (s n t)")
-                    codes, scale = quantise(values, 2 * BLOCK, f"h{step}")
-                    for s in range(2):
-                        cols = slice(BLOCK * s, BLOCK * (s + 1))
-                        h_mx[step - 1 + s] = (codes[:, cols], scale[:, cols])
-                return
-            codes, scale = quantise(minus_h[step].rearrange("p n t -> p (n t)"), BLOCK, f"h{step}")
-            h_mx[step] = (codes[:], scale[:])
-
-        def rotor_unit(unit):
-            if unit not in rotor:
-                rotor[unit] = bank([P, PACK, UNIT], "a", rotor_banks[unit])
-                rotor_pass(unit, 0)
-            rotor_pass(unit, 1)
-            correct(unit)
-
-        for step in range(last):
-            if step not in minus_h:
-                tile = held([P, BLOCK, PACK], BF16, f"minus_h{step}")
-                minus_h[step] = tile[:]
-            if step in (2, 3, 5):
-                later = {2: 5, 3: 6, 5: 7}[step]
-                shares[later] = gaussian(later)
-            rotor_unit(2 * step)
-            if step >= 1:
-                quantise_h(step - 1)
-            rotor_unit(2 * step + 1)
-            if step >= 5:
-                for pair in range(2):
-                    read_out(step - 5, pair, (0, 4)[step - 5] + pair, "scalar")
-
-        first = BLOCK * (BLOCKS - 1)
-        last_h = held([P, BLOCK, PACK], BF16, "last_h")
-        minus_h[last] = last_h[:]
-        halves = [minus_h[last][:, UNIT * half : UNIT * (half + 1), :].rearrange("p n t -> p (n t)") for half in range(2)]
-        rotor_unit(2 * last)
-        quantise_h(last - 1)
-        rotor_unit(2 * last + 1)
-        tail_mx = [quantise(halves[0], UNIT, "h_tail0")]
-        tail_mx.append(quantise(halves[1], UNIT, "h_tail1"))
-        read_out(2, 0, 6, "vector")
-        read_out(2, 1, 7, "vector")
-        codes, scale = h_mx[BLOCKS - 1]
-        tail_banks = [(0, 1), (2, 3)]
+        shares, rotor = {}, {}
+        h_codes = [held([P, S], U32, f"h_codes{g}") for g in range(GROUPS)]
+        h_first = held([P, 1, UNIT, PACK], BF16, "h_first")
+        h_rest = held([P, 2 * BLOCKS - 1, UNIT, PACK], BF16, "h_rest", "w2_raw3")
+        h_second = [held([P, 2, UNIT, PACK], BF16, f"h_second{block}") for block in range(BLOCKS)]
+        minus_h = [h_first[:, 0, :, :]] + [h_rest[:, u, :, :] for u in range(2 * BLOCKS - 1)]
+        minus_h.extend(h_second[u // 2][:, u % 2, :, :] for u in range(2 * BLOCKS))
+        gaussian_by_units(0, 0)
+        h_scale = [held([P, S], U8, f"h_scale{g}", ("share_unit1", "")[g]) for g in range(GROUPS)]
+        gaussian(1, 2)
+        gaussian(2, 0)
+        round_w2(2, on_scalar)
+        gaussian(3, 2, "w2_raw2")
+        v_codes = [pick_words(v_words[0], list1, (0, S // 2, S), "v_codes0")]
+        for unit in range(AHEAD):
+            rotor[unit] = bank([P, PACK, UNIT], "a", 4 + unit)
+            rotor_pass(unit, 0, True, False)
+        v_codes.append(pick_words(v_words[1], list1, (0, BLOCK, S // 2, S), "v_codes1"))
+        for unit in range(AHEAD):
+            rotor_pass(unit, 1, False, True)
+        rotor_unit(4, 0)
+        rotor_unit(5, 1)
+        correct(0)
+        round_w2(3, nc.vector.tensor_copy)
+        correct(1)
+        w2_mx.append(quantise_w2(1))
+        w1_codes.append(deal_w1_codes(1, "w2_grouped1"))
+        rotor_unit(6, 4)
+        gaussian(4, 2)
+        rotor_unit(7, 5)
+        correct(2)
+        correct(3)
+        rotor_unit(8, 6)
+        rotor_unit(9, 7)
+        quantise_h(h_first[:], 0, 1)
+        correct(4)
+        quantise_h(h_rest[:, 0:3, :, :], 1, 3)
+        correct(5)
+        gaussian(5, 2)
+        rotor_unit(10, 0)
+        rotor_unit(11, 1)
+        correct(6)
+        correct(7)
+        gaussian(6, 2)
+        rotor_unit(12, 4)
+        rotor_unit(13, 5)
+        correct(8)
+        quantise_h(h_rest[:, 3:7, :, :], 4, 4)
+        correct(9)
+        gaussian_by_units(7, 2)
+        correct(10)
+        quantise_h(h_second[0][:], 8, 2)
+        correct(11)
+        accs = [multiply_out(0, pair, 6 + pair) for pair in range(2)]
+        rotor_unit(14, 0)
+        rotor_unit(15, 1)
+        store(accs[0], 0, 0, BLOCK, True)
+        quantise_h(h_second[1][:], 10, 2)
+        correct(12)
+        store(accs[1], 1, 0, BLOCK, False)
+        correct(13)
+        accs = [multiply_out(1, pair, 4 + pair) for pair in range(2)]
+        correct(14)
+        quantise_h(h_second[2][:], 12, 2)
+        correct(15)
+        for pair in range(2):
+            store(accs[pair], pair, BLOCK, BLOCK, False)
+        accs = [multiply_out(2, pair, 6 + pair) for pair in range(2)]
         for half in range(2):
-            cols = slice(UNIT * half, UNIT * (half + 1))
-            accs = [bank([P, 2, UNIT], "out_tail", tail_banks[half][pair]) for pair in range(2)]
+            quantise_h(h_second[3][:, half : half + 1, :, :], 14 + half, 1)
+        for pair in range(2):
+            store(accs[pair], pair, 2 * BLOCK, BLOCK, False)
+        for half in range(2):
+            first = S - BLOCK + UNIT * half
+            accs = [bank([P, 2, UNIT], "out_tail", (2, 0)[half] + pair) for pair in range(2)]
+            for g in range(GROUPS):
+                for pair in range(2):
+                    for u in range(2):
+                        out_pass(accs[pair][:, u, :], 2 * pair + u, g, first, UNIT, g + u == 0, g + u == 2)
             for pair in range(2):
-                out_pass(accs[pair], pair, 0, (codes[:, cols], scale[:, cols]), UNIT, True, False)
-            for pair in range(2):
-                out_pass(accs[pair], pair, 1, (tail_mx[half][0][:], tail_mx[half][1][:]), UNIT, False, True)
-                store(accs[pair], pair, first + UNIT * half, UNIT, ("scalar", "vector")[pair])
+                store(accs[pair], pair, first, UNIT, half + pair < 2)

@@ -53,9 +53,9 @@ def tile_list_wake_correction_kernel(
             nc.sync.dma_start(window[:], words.rearrange("p t i -> p (t i)").bitcast(I32))
             return window
 
-        def load_w2(chunk, raw):
-            columns = w2.rearrange("(p j) c -> p j c", j=PACK)[:, :, CHUNK * chunk : CHUNK * (chunk + 1)]
-            nc.sync.dma_start(raw[:], columns)
+        def load_w2(first, width):
+            raw = held([P, PACK, width], F32, f"w2_raw{first}")
+            nc.sync.dma_start(raw[:], w2.rearrange("(p j) c -> p j c", j=PACK)[:, :, first : first + width])
             return raw
 
         def load_w1(g):
@@ -79,12 +79,12 @@ def tile_list_wake_correction_kernel(
         def on_scalar(dst, src):
             nc.scalar.activation(dst, src, ACT.Copy)
 
-        def round_w2(chunk, copy):
-            g, half = divmod(chunk, 2)
-            rows = slice(CHUNK // PACK * half, CHUNK // PACK * (half + 1))
+        def round_w2(raw, first, copy):
+            g, at = divmod(first, PASS)
+            rows = slice(at // PACK, (at + raw.shape[2]) // PACK)
             copy(
                 w2_grouped[g][:, :, rows, :].rearrange("p t m j -> p m j t"),
-                w2_raw[chunk][:].rearrange("p j (m t) -> p m j t", t=PACK),
+                raw[:].rearrange("p j (m t) -> p m j t", t=PACK),
             )
 
         def quantise(values, codes, name):
@@ -96,9 +96,9 @@ def tile_list_wake_correction_kernel(
             codes = held([P, PASS], U32, f"w2_codes{g}")
             return quantise(w2_grouped[g][:].rearrange("p t m j -> p (t m j)"), codes, f"w2_{g}")
 
-        def deal_w1_codes(g, tag=""):
+        def deal_w1_codes(g, copy, tag=""):
             codes = held([P, 2, 2 * PASS], U8, f"w1_codes{g}", tag)
-            nc.gpsimd.tensor_copy(
+            copy(
                 codes[:].bitcast(U16).rearrange("p a (t m) -> p a t m", t=PACK),
                 w1_raw[g][:].bitcast(U16).rearrange("p a (m t) -> p a t m", t=PACK),
             )
@@ -120,23 +120,21 @@ def tile_list_wake_correction_kernel(
             for r in range(4):
                 nc.sync.dma_start(planes[a][r:P:32, :].bitcast(I32), staged[8 * r + 4 * a : P : 32, :].bitcast(I32))
 
-        w2_raw = [held([P, PACK, CHUNK], F32, f"w2_raw{chunk}") for chunk in range(4)]
         nc.sync.dma_start(list1[:], offs)
         nc.sync.dma_start(list2[:], offs2)
         nc.sync.dma_start(v_scale_rows[0:P:4, :].bitcast(I32), tab_scales.rearrange("a q t -> q a t").bitcast(I32))
-        load_w2(0, w2_raw[0])
-        load_w2(1, w2_raw[1])
+        w2_raw = [load_w2(0, PASS)]
         v2_rows = tab2_scales[0].rearrange("(d r) t -> r d t", r=4)
         for r in range(4):
             nc.scalar.dma_start(v2_scale_rows[V2_ROW + r : P : 32, :].bitcast(I32), v2_rows[r].bitcast(I32))
-        nc.gpsimd.dma_start(w1_scale_rows[0:P:4, :].bitcast(I32), w1_scales.rearrange("a q c -> q a c").bitcast(I32))
+        nc.sync.dma_start(w1_scale_rows[0:P:4, :].bitcast(I32), w1_scales.rearrange("a q c -> q a c").bitcast(I32))
         v2_words = load_table(tab2_words[0], "v2_words")
         w1_raw = [load_w1(0)]
         v_words = [load_table(tab_words[0], "v_words0")]
 
         v_scale_picked = pick_bytes(v_scale_rows, list1, 0, S, "v_scale_picked")
         staged = held([P, S + H], U8, "staged")
-        nc.gpsimd.tensor_copy(
+        nc.vector.tensor_copy(
             staged[:, S : S + H].rearrange("p (g t m) -> p g t m", g=GROUPS, t=PACK),
             w1_scale_rows[:].rearrange("p (g m t) -> p g t m", g=GROUPS, t=PACK),
         )
@@ -146,8 +144,7 @@ def tile_list_wake_correction_kernel(
         move_planes(0)
         v_words.append(load_table(tab_words[1], "v_words1"))
         move_planes(1)
-        load_w2(2, w2_raw[2])
-        load_w2(3, w2_raw[3])
+        w2_raw.extend(load_w2(first, CHUNK) for first in (PASS, PASS + CHUNK))
         w1_raw.append(load_w1(1))
         w3_codes = held([P, GROUPS, N], U32, "w3_codes")
         nc.sync.dma_start(w3_codes[:].bitcast(I32), w3_words.rearrange("a p c i -> p a (c i)").bitcast(I32))
@@ -156,10 +153,9 @@ def tile_list_wake_correction_kernel(
             nc.sync.dma_start(w3_scale[rows, :].bitcast(I32), w3_scales[:, 4 * d : 4 * d + 4, :].bitcast(I32))
 
         w2_grouped = [held([P, PACK, P, PACK], BF16, f"w2_grouped{g}") for g in range(GROUPS)]
-        round_w2(0, on_scalar)
-        round_w2(1, on_scalar)
+        round_w2(w2_raw[0], 0, on_scalar)
         w2_mx = [quantise_w2(0)]
-        w1_codes = [deal_w1_codes(0)]
+        w1_codes = [deal_w1_codes(0, nc.gpsimd.tensor_copy)]
         v2_codes = pick_words(v2_words, list2, (0, UNIT, S // 2, S), "v2_codes", "w2_grouped0")
         v2_scale.append(pick_bytes(v2_scale_rows, list2, EARLY, S - EARLY, "v2_scale1", "v2_words"))
 
@@ -270,17 +266,17 @@ def tile_list_wake_correction_kernel(
 
         shares, rotor = {}, {}
         h_codes = [held([P, S], U32, f"h_codes{g}") for g in range(GROUPS)]
-        h_first = held([P, 1, UNIT, PACK], BF16, "h_first")
-        h_rest = held([P, 2 * BLOCKS - 1, UNIT, PACK], BF16, "h_rest", "w2_raw3")
+        h_first = held([P, 2, UNIT, PACK], BF16, "h_first")
+        h_rest = held([P, 2 * BLOCKS - 2, UNIT, PACK], BF16, "h_rest", f"w2_raw{PASS + CHUNK}")
         h_second = [held([P, 2, UNIT, PACK], BF16, f"h_second{block}") for block in range(BLOCKS)]
-        minus_h = [h_first[:, 0, :, :]] + [h_rest[:, u, :, :] for u in range(2 * BLOCKS - 1)]
+        minus_h = [h_first[:, u, :, :] for u in range(2)] + [h_rest[:, u, :, :] for u in range(2 * BLOCKS - 2)]
         minus_h.extend(h_second[u // 2][:, u % 2, :, :] for u in range(2 * BLOCKS))
         gaussian_by_units(0, 0)
-        h_scale = [held([P, S], U8, f"h_scale{g}", ("share_unit1", "")[g]) for g in range(GROUPS)]
         gaussian(1, 2)
+        h_scale = [held([P, S], U8, f"h_scale{g}", ("share1", "")[g]) for g in range(GROUPS)]
         gaussian(2, 0)
-        round_w2(2, on_scalar)
-        gaussian(3, 2, "w2_raw2")
+        round_w2(w2_raw[1], PASS, on_scalar)
+        gaussian(3, 2, f"w2_raw{PASS}")
         v_codes = [pick_words(v_words[0], list1, (0, S // 2, S), "v_codes0")]
         for unit in range(AHEAD):
             rotor[unit] = bank([P, PACK, UNIT], "a", 4 + unit)
@@ -291,31 +287,31 @@ def tile_list_wake_correction_kernel(
         rotor_unit(4, 0)
         rotor_unit(5, 1)
         correct(0)
-        round_w2(3, nc.vector.tensor_copy)
         correct(1)
-        w2_mx.append(quantise_w2(1))
-        w1_codes.append(deal_w1_codes(1, "w2_grouped1"))
         rotor_unit(6, 4)
-        gaussian(4, 2)
         rotor_unit(7, 5)
+        round_w2(w2_raw[2], PASS + CHUNK, nc.vector.tensor_copy)
         correct(2)
+        w2_mx.append(quantise_w2(1))
+        w1_codes.append(deal_w1_codes(1, nc.gpsimd.tensor_copy, "w2_grouped1"))
+        gaussian(4, 2)
         correct(3)
         rotor_unit(8, 6)
         rotor_unit(9, 7)
-        quantise_h(h_first[:], 0, 1)
         correct(4)
-        quantise_h(h_rest[:, 0:3, :, :], 1, 3)
+        quantise_h(h_first[:], 0, 2)
         correct(5)
         gaussian(5, 2)
         rotor_unit(10, 0)
         rotor_unit(11, 1)
+        quantise_h(h_rest[:, 0:2, :, :], 2, 2)
         correct(6)
         correct(7)
         gaussian(6, 2)
         rotor_unit(12, 4)
         rotor_unit(13, 5)
         correct(8)
-        quantise_h(h_rest[:, 3:7, :, :], 4, 4)
+        quantise_h(h_rest[:, 2:6, :, :], 4, 4)
         correct(9)
         gaussian_by_units(7, 2)
         correct(10)

@@ -96,11 +96,11 @@ def tile_list_wake_correction_kernel(
             codes = held([P, PASS], U32, f"w2_codes{g}")
             return quantise(w2_grouped[g][:].rearrange("p t m j -> p (t m j)"), codes, f"w2_{g}")
 
-        def deal_w1_codes(g, copy, tag=""):
-            codes = held([P, 2, 2 * PASS], U8, f"w1_codes{g}", tag)
-            copy(
-                codes[:].bitcast(U16).rearrange("p a (t m) -> p a t m", t=PACK),
-                w1_raw[g][:].bitcast(U16).rearrange("p a (m t) -> p a t m", t=PACK),
+        def deal_w1_codes(g, a):
+            codes = held([P, 2 * PASS], U8, f"w1_codes{g}_{a}")
+            nc.gpsimd.tensor_copy(
+                codes[:].bitcast(U16).rearrange("p (t m) -> p t m", t=PACK),
+                w1_raw[g][:, a, :].bitcast(U16).rearrange("p (m t) -> p t m", t=PACK),
             )
             return codes
 
@@ -111,9 +111,8 @@ def tile_list_wake_correction_kernel(
         w1_scale_rows = held([P, H], U8, "w1_scale_rows")
         w3_scale = held([P, N], U8, "w3_scale")
         planes = [held([P, S + H], U8, f"planes{a}") for a in range(2)]
-        for tile in (v_scale_rows, w1_scale_rows):
-            nc.gpsimd.memset(tile[:].bitcast(I32), 0)
-        for tile in (v2_scale_rows, planes[0], planes[1], w3_scale):
+        nc.gpsimd.memset(v2_scale_rows[:].bitcast(I32), 0)
+        for tile in (v_scale_rows, w1_scale_rows, planes[0], planes[1], w3_scale):
             nc.vector.memset(tile[:].bitcast(I32), 0)
 
         def move_planes(a):
@@ -142,10 +141,10 @@ def tile_list_wake_correction_kernel(
         v2_scale = [pick_bytes(v2_scale_rows, list2, 0, EARLY, "v2_scale0")]
 
         move_planes(0)
+        w1_raw.append(load_w1(1))
         v_words.append(load_table(tab_words[1], "v_words1"))
         move_planes(1)
         w2_raw.extend(load_w2(first, CHUNK) for first in (PASS, PASS + CHUNK))
-        w1_raw.append(load_w1(1))
         w3_codes = held([P, GROUPS, N], U32, "w3_codes")
         nc.sync.dma_start(w3_codes[:].bitcast(I32), w3_words.rearrange("a p c i -> p a (c i)").bitcast(I32))
         for d in range(4):
@@ -155,7 +154,7 @@ def tile_list_wake_correction_kernel(
         w2_grouped = [held([P, PACK, P, PACK], BF16, f"w2_grouped{g}") for g in range(GROUPS)]
         round_w2(w2_raw[0], 0, on_scalar)
         w2_mx = [quantise_w2(0)]
-        w1_codes = [deal_w1_codes(0, nc.gpsimd.tensor_copy)]
+        w1_codes = {(g, a): deal_w1_codes(g, a) for g in range(GROUPS) for a in range(2)}
         v2_codes = pick_words(v2_words, list2, (0, UNIT, S // 2, S), "v2_codes", "w2_grouped0")
         v2_scale.append(pick_bytes(v2_scale_rows, list2, EARLY, S - EARLY, "v2_scale1", "v2_words"))
 
@@ -204,7 +203,7 @@ def tile_list_wake_correction_kernel(
             for t in range(PACK):
                 nc.tensor.matmul_mx(
                     out=rotor[unit][:, t, :],
-                    lhsT=w1_codes[g][:, a, 2 * P * t : 2 * P * (t + 1)].bitcast(FP4X4),
+                    lhsT=w1_codes[g, a][:, 2 * P * t : 2 * P * (t + 1)].bitcast(FP4X4),
                     lhsT_scale=planes[a][:, S + PASS * g + P * t : S + PASS * g + P * (t + 1)],
                     rhs=v_codes[a][:, first : first + UNIT].bitcast(FP8X4),
                     rhs_scale=planes[a][:, first : first + UNIT],
@@ -293,7 +292,6 @@ def tile_list_wake_correction_kernel(
         round_w2(w2_raw[2], PASS + CHUNK, nc.vector.tensor_copy)
         correct(2)
         w2_mx.append(quantise_w2(1))
-        w1_codes.append(deal_w1_codes(1, nc.gpsimd.tensor_copy, "w2_grouped1"))
         gaussian(4, 2)
         correct(3)
         rotor_unit(8, 6)

@@ -287,49 +287,49 @@ def tile_list_wake_correction_kernel(
         rotor_unit(5, 1)
         correct(0)
         correct(1)
-        rotor_unit(6, 4)
-        rotor_unit(7, 5)
         round_w2(w2_raw[2], PASS + CHUNK, nc.vector.tensor_copy)
         correct(2)
         w2_mx.append(quantise_w2(1))
         gaussian(4, 2)
+        rotor_unit(8, 4)
+        rotor_unit(9, 5)
         correct(3)
-        rotor_unit(8, 6)
-        rotor_unit(9, 7)
         correct(4)
         quantise_h(h_first[:], 0, 2)
+        rotor_unit(6, 6)
+        rotor_unit(7, 7)
         correct(5)
+        quantise_h(h_rest[:, 0:2, :, :], 2, 2)
         gaussian(5, 2)
         rotor_unit(10, 0)
         rotor_unit(11, 1)
-        quantise_h(h_rest[:, 0:2, :, :], 2, 2)
-        correct(6)
-        correct(7)
-        gaussian(6, 2)
-        rotor_unit(12, 4)
-        rotor_unit(13, 5)
         correct(8)
-        quantise_h(h_rest[:, 2:6, :, :], 4, 4)
         correct(9)
-        gaussian_by_units(7, 2)
-        correct(10)
+        correct(6)
         quantise_h(h_second[0][:], 8, 2)
+        correct(7)
+        accs = [multiply_out(0, pair, 4 + pair) for pair in range(2)]
+        store(accs[1], 1, 0, BLOCK, False)
+        gaussian(6, 2)
+        rotor_unit(12, 6)
+        rotor_unit(13, 7)
+        correct(10)
+        quantise_h(h_rest[:, 2:6, :, :], 4, 4)
         correct(11)
-        accs = [multiply_out(0, pair, 6 + pair) for pair in range(2)]
-        rotor_unit(14, 0)
-        rotor_unit(15, 1)
         store(accs[0], 0, 0, BLOCK, True)
         quantise_h(h_second[1][:], 10, 2)
+        accs = [multiply_out(1, pair, pair) for pair in range(2)]
+        store(accs[1], 1, BLOCK, BLOCK, False)
+        gaussian_by_units(7, 2)
+        rotor_unit(14, 4)
+        rotor_unit(15, 5)
         correct(12)
-        store(accs[1], 1, 0, BLOCK, False)
         correct(13)
-        accs = [multiply_out(1, pair, 4 + pair) for pair in range(2)]
-        correct(14)
+        store(accs[0], 0, BLOCK, BLOCK, True)
         quantise_h(h_second[2][:], 12, 2)
-        correct(15)
-        for pair in range(2):
-            store(accs[pair], pair, BLOCK, BLOCK, False)
         accs = [multiply_out(2, pair, 6 + pair) for pair in range(2)]
+        correct(14)
+        correct(15)
         for half in range(2):
             quantise_h(h_second[3][:, half : half + 1, :, :], 14 + half, 1)
         for pair in range(2):
@@ -342,4 +342,4 @@ def tile_list_wake_correction_kernel(
                     for u in range(2):
                         out_pass(accs[pair][:, u, :], 2 * pair + u, g, first, UNIT, g + u == 0, g + u == 2)
             for pair in range(2):
-                store(accs[pair], pair, first, UNIT, half + pair < 2)
+                store(accs[pair], pair, first, UNIT, pair == 0)

@@ -37,10 +37,14 @@ def tile_list_wake_correction_kernel(
     nc = tc.nc
     with ExitStack() as ctx:
         keep = ctx.enter_context(tc.tile_pool(name="keep", bufs=1))
+        head = ctx.enter_context(tc.tile_pool(name="head", bufs=1))
         psum = ctx.enter_context(tc.psum_pool(name="psum", bufs=1))
 
         def held(shape, dtype, name, tag=""):
             return keep.tile(shape, dtype, name=name, tag=tag or name, align_bytes=256)
+
+        def placed(shape, dtype, name, offset):
+            return head.tile(shape, dtype, name=name, tag=name, align_bytes=256, offset=offset)
 
         def bank(shape, name, number):
             return psum.tile(shape, F32, name=name, tag=f"bank{number}")
@@ -69,8 +73,7 @@ def tile_list_wake_correction_kernel(
             nc.vector.tensor_copy(picked[:], window[:].indirect(entries(offsets, first, count)))
             return picked
 
-        def pick_words(window, offsets, cuts, name, tag=""):
-            picked = held([P, S], U32, name, tag)
+        def pick_words(picked, window, offsets, cuts):
             for first, stop in zip(cuts, cuts[1:]):
                 looked_up = window[:].bitcast(U32).indirect(entries(offsets, first, stop - first))
                 nc.vector.tensor_copy(picked[:, first:stop], looked_up)
@@ -110,38 +113,46 @@ def tile_list_wake_correction_kernel(
         v2_scale_rows = held([P, T], U8, "v2_scale_rows")
         w1_scale_rows = held([P, H], U8, "w1_scale_rows")
         w3_scale = held([P, N], U8, "w3_scale")
-        planes = [held([P, S + H], U8, f"planes{a}") for a in range(2)]
-        nc.gpsimd.memset(v2_scale_rows[:].bitcast(I32), 0)
-        for tile in (v_scale_rows, w1_scale_rows, planes[0], planes[1], w3_scale):
+        plane1 = held([P, S + H], U8, "plane1")
+        nc.gpsimd.memset(v_scale_rows[:].bitcast(I32), 0)
+        for tile in (v2_scale_rows, w1_scale_rows, plane1, w3_scale):
             nc.vector.memset(tile[:].bitcast(I32), 0)
 
         def move_planes(a):
-            for r in range(4):
+            for r in range(1 - a, 4):
                 nc.sync.dma_start(planes[a][r:P:32, :].bitcast(I32), staged[8 * r + 4 * a : P : 32, :].bitcast(I32))
 
         nc.sync.dma_start(list1[:], offs)
         nc.sync.dma_start(list2[:], offs2)
         nc.sync.dma_start(v_scale_rows[0:P:4, :].bitcast(I32), tab_scales.rearrange("a q t -> q a t").bitcast(I32))
-        w2_raw = [load_w2(0, PASS)]
+        w2_raw = [load_w2(first, CHUNK) for first in (0, CHUNK)]
         v2_rows = tab2_scales[0].rearrange("(d r) t -> r d t", r=4)
         for r in range(4):
             nc.scalar.dma_start(v2_scale_rows[V2_ROW + r : P : 32, :].bitcast(I32), v2_rows[r].bitcast(I32))
-        nc.sync.dma_start(w1_scale_rows[0:P:4, :].bitcast(I32), w1_scales.rearrange("a q c -> q a c").bitcast(I32))
         v2_words = load_table(tab2_words[0], "v2_words")
+        nc.sync.dma_start(w1_scale_rows[0:P:4, :].bitcast(I32), w1_scales.rearrange("a q c -> q a c").bitcast(I32))
         w1_raw = [load_w1(0)]
         v_words = [load_table(tab_words[0], "v_words0")]
+        w1_raw.append(load_w1(1))
 
         v_scale_picked = pick_bytes(v_scale_rows, list1, 0, S, "v_scale_picked")
-        staged = held([P, S + H], U8, "staged")
+        v2_scale = [pick_bytes(v2_scale_rows, list2, 0, EARLY, "v2_scale0")]
+
+        w2_grouped = [placed([P, PACK, P, PACK], BF16, "w2_grouped0", S + H - 256), held([P, PACK, P, PACK], BF16, "w2_grouped1")]
+        for chunk in range(2):
+            round_w2(w2_raw[chunk], CHUNK * chunk, on_scalar)
+        w2_mx = [quantise_w2(0)]
+        v2_codes = placed([P, S], U32, "v2_codes", S + H + 4 * S - 512)
+        pick_words(v2_codes, v2_words, list2, (0, UNIT))
+        staged = placed([P, S + H], U8, "staged", 0)
+        planes = [staged, plane1]
         nc.vector.tensor_copy(
             staged[:, S : S + H].rearrange("p (g t m) -> p g t m", g=GROUPS, t=PACK),
             w1_scale_rows[:].rearrange("p (g m t) -> p g t m", g=GROUPS, t=PACK),
         )
         nc.vector.tensor_copy(staged[:, 0:S].bitcast(I32), v_scale_picked[:].bitcast(I32))
-        v2_scale = [pick_bytes(v2_scale_rows, list2, 0, EARLY, "v2_scale0")]
-
+        pick_words(v2_codes, v2_words, list2, (UNIT, S // 2, S))
         move_planes(0)
-        w1_raw.append(load_w1(1))
         v_words.append(load_table(tab_words[1], "v_words1"))
         move_planes(1)
         w2_raw.extend(load_w2(first, CHUNK) for first in (PASS, PASS + CHUNK))
@@ -151,11 +162,7 @@ def tile_list_wake_correction_kernel(
             rows = slice(32 * d + W3_ROW, 32 * d + W3_ROW + 8)
             nc.sync.dma_start(w3_scale[rows, :].bitcast(I32), w3_scales[:, 4 * d : 4 * d + 4, :].bitcast(I32))
 
-        w2_grouped = [held([P, PACK, P, PACK], BF16, f"w2_grouped{g}") for g in range(GROUPS)]
-        round_w2(w2_raw[0], 0, on_scalar)
-        w2_mx = [quantise_w2(0)]
         w1_codes = {(g, a): deal_w1_codes(g, a) for g in range(GROUPS) for a in range(2)}
-        v2_codes = pick_words(v2_words, list2, (0, UNIT, S // 2, S), "v2_codes", "w2_grouped0")
         v2_scale.append(pick_bytes(v2_scale_rows, list2, EARLY, S - EARLY, "v2_scale1", "v2_words"))
 
         def mast_pass(acc, g, t, first, width):
@@ -265,41 +272,41 @@ def tile_list_wake_correction_kernel(
 
         shares, rotor = {}, {}
         h_codes = [held([P, S], U32, f"h_codes{g}") for g in range(GROUPS)]
-        h_first = held([P, 2, UNIT, PACK], BF16, "h_first")
-        h_rest = held([P, 2 * BLOCKS - 2, UNIT, PACK], BF16, "h_rest", f"w2_raw{PASS + CHUNK}")
+        h_first = held([P, 1, UNIT, PACK], BF16, "h_first")
+        h_rest = held([P, 2 * BLOCKS - 1, UNIT, PACK], BF16, "h_rest", f"w2_raw{PASS + CHUNK}")
         h_second = [held([P, 2, UNIT, PACK], BF16, f"h_second{block}") for block in range(BLOCKS)]
-        minus_h = [h_first[:, u, :, :] for u in range(2)] + [h_rest[:, u, :, :] for u in range(2 * BLOCKS - 2)]
+        minus_h = [h_first[:, 0, :, :]] + [h_rest[:, u, :, :] for u in range(2 * BLOCKS - 1)]
         minus_h.extend(h_second[u // 2][:, u % 2, :, :] for u in range(2 * BLOCKS))
         gaussian_by_units(0, 0)
         gaussian(1, 2)
         h_scale = [held([P, S], U8, f"h_scale{g}", ("share1", "")[g]) for g in range(GROUPS)]
         gaussian(2, 0)
-        round_w2(w2_raw[1], PASS, on_scalar)
+        round_w2(w2_raw[2], PASS, on_scalar)
         gaussian(3, 2, f"w2_raw{PASS}")
-        v_codes = [pick_words(v_words[0], list1, (0, S // 2, S), "v_codes0")]
+        v_codes = [pick_words(held([P, S], U32, "v_codes0"), v_words[0], list1, (0, S // 2, S))]
         for unit in range(AHEAD):
             rotor[unit] = bank([P, PACK, UNIT], "a", 4 + unit)
             rotor_pass(unit, 0, True, False)
-        v_codes.append(pick_words(v_words[1], list1, (0, BLOCK, S // 2, S), "v_codes1"))
+        v_codes.append(pick_words(held([P, S], U32, "v_codes1"), v_words[1], list1, (0, BLOCK, S // 2, S)))
         for unit in range(AHEAD):
             rotor_pass(unit, 1, False, True)
         rotor_unit(4, 0)
         rotor_unit(5, 1)
         correct(0)
+        round_w2(w2_raw[3], PASS + CHUNK, nc.vector.tensor_copy)
         correct(1)
-        round_w2(w2_raw[2], PASS + CHUNK, nc.vector.tensor_copy)
-        correct(2)
         w2_mx.append(quantise_w2(1))
         gaussian(4, 2)
         rotor_unit(8, 4)
         rotor_unit(9, 5)
+        correct(2)
         correct(3)
-        correct(4)
-        quantise_h(h_first[:], 0, 2)
         rotor_unit(6, 6)
         rotor_unit(7, 7)
+        quantise_h(h_first[:], 0, 1)
+        correct(4)
+        quantise_h(h_rest[:, 0:3, :, :], 1, 3)
         correct(5)
-        quantise_h(h_rest[:, 0:2, :, :], 2, 2)
         gaussian(5, 2)
         rotor_unit(10, 0)
         rotor_unit(11, 1)
@@ -309,14 +316,14 @@ def tile_list_wake_correction_kernel(
         quantise_h(h_second[0][:], 8, 2)
         correct(7)
         accs = [multiply_out(0, pair, 4 + pair) for pair in range(2)]
-        store(accs[1], 1, 0, BLOCK, False)
         gaussian(6, 2)
         rotor_unit(12, 6)
         rotor_unit(13, 7)
+        quantise_h(h_rest[:, 3:7, :, :], 4, 4)
         correct(10)
-        quantise_h(h_rest[:, 2:6, :, :], 4, 4)
-        correct(11)
         store(accs[0], 0, 0, BLOCK, True)
+        correct(11)
+        store(accs[1], 1, 0, BLOCK, True)
         quantise_h(h_second[1][:], 10, 2)
         accs = [multiply_out(1, pair, pair) for pair in range(2)]
         store(accs[1], 1, BLOCK, BLOCK, False)

@@ -24,7 +24,7 @@ BLOCK = 256
 BLOCKS = S // BLOCK
 UNIT = 128
 CHUNK = 256
-EARLY = 512
+EARLY = 768
 AHEAD = 4
 V2_ROW = 8
 W3_ROW = 4
@@ -179,31 +179,33 @@ def tile_list_wake_correction_kernel(
                 stop=True,
             )
 
-        def gaussian_by_units(step, number):
+        def square(step, pair, number):
             g, block = divmod(step, BLOCKS)
-            for half in range(2):
-                unit = 2 * step + half
-                b = bank([P, PACK, UNIT], "b", number + half)
-                for t in range(PACK):
-                    mast_pass(b[:, t, :], g, t, BLOCK * block + UNIT * half, UNIT)
-                squares = held([P, UNIT, PACK], F32, f"squares_unit{unit}")
-                nc.scalar.activation(squares[:], b[:].rearrange("p t n -> p n t"), ACT.Square)
-                share = held([P, UNIT, PACK], F32, f"share_unit{unit}")
-                nc.scalar.activation(share[:], squares[:], ACT.Exp, scale=-1.0)
-                shares[unit] = share[:]
+            if pair == 0:
+                step_squares[step] = held([P, 2, BLOCK, 2], F32, f"squares{step}")
+            b = bank([P, 2, BLOCK], "b", number)
+            for u in range(2):
+                mast_pass(b[:, u, :], g, 2 * pair + u, BLOCK * block, BLOCK)
+            nc.scalar.activation(step_squares[step][:, pair, :, :], b[:].rearrange("p u n -> p n u"), ACT.Square)
 
-        def gaussian(step, number, tag=""):
-            g, block = divmod(step, BLOCKS)
-            squares = held([P, 2, BLOCK, 2], F32, f"squares{step}", tag)
-            for pair in range(2):
-                b = bank([P, 2, BLOCK], "b", number + pair)
-                for u in range(2):
-                    mast_pass(b[:, u, :], g, 2 * pair + u, BLOCK * block, BLOCK)
-                nc.scalar.activation(squares[:, pair, :, :], b[:].rearrange("p u n -> p n u"), ACT.Square)
-            share = held([P, BLOCK, 2, 2], F32, f"share{step}")
-            nc.scalar.activation(share[:], squares[:].rearrange("p h n u -> p n h u"), ACT.Exp, scale=-1.0)
+        def exponential(step, tag=""):
+            share = held([P, BLOCK, 2, 2], F32, f"share{step}", tag)
+            nc.scalar.activation(share[:], step_squares[step][:].rearrange("p h n u -> p n h u"), ACT.Exp, scale=-1.0)
             for half in range(2):
                 shares[2 * step + half] = share[:, UNIT * half : UNIT * (half + 1), :, :].rearrange("p n h u -> p n (h u)")
+
+        def square_unit(unit, number):
+            g, at = divmod(unit, 2 * BLOCKS)
+            b = bank([P, PACK, UNIT], "b", number)
+            for t in range(PACK):
+                mast_pass(b[:, t, :], g, t, UNIT * at, UNIT)
+            unit_squares[unit] = held([P, UNIT, PACK], F32, f"squares_unit{unit}")
+            nc.scalar.activation(unit_squares[unit][:], b[:].rearrange("p t n -> p n t"), ACT.Square)
+
+        def exponential_unit(unit):
+            share = held([P, UNIT, PACK], F32, f"share_unit{unit}")
+            nc.scalar.activation(share[:], unit_squares[unit][:], ACT.Exp, scale=-1.0)
+            shares[unit] = share[:]
 
         def rotor_pass(unit, a, start, stop):
             g, first = unit // 8, UNIT * (unit % 8)
@@ -270,19 +272,28 @@ def tile_list_wake_correction_kernel(
                     out_pass(acc[:, u, :], 2 * pair + u, g, BLOCK * block, BLOCK, g + u == 0, g + u == 2)
             return acc
 
-        shares, rotor = {}, {}
+        shares, rotor, step_squares, unit_squares = {}, {}, {}, {}
         h_codes = [held([P, S], U32, f"h_codes{g}") for g in range(GROUPS)]
         h_first = held([P, 1, UNIT, PACK], BF16, "h_first")
         h_rest = held([P, 2 * BLOCKS - 1, UNIT, PACK], BF16, "h_rest", f"w2_raw{PASS + CHUNK}")
         h_second = [held([P, 2, UNIT, PACK], BF16, f"h_second{block}") for block in range(BLOCKS)]
         minus_h = [h_first[:, 0, :, :]] + [h_rest[:, u, :, :] for u in range(2 * BLOCKS - 1)]
         minus_h.extend(h_second[u // 2][:, u % 2, :, :] for u in range(2 * BLOCKS))
-        gaussian_by_units(0, 0)
-        gaussian(1, 2)
+        square_unit(0, 0)
+        square_unit(1, 1)
+        exponential_unit(0)
+        square(1, 0, 2)
+        exponential_unit(1)
+        square(1, 1, 3)
+        square(2, 0, 0)
+        exponential(1)
         h_scale = [held([P, S], U8, f"h_scale{g}", ("share1", "")[g]) for g in range(GROUPS)]
-        gaussian(2, 0)
+        square(2, 1, 1)
+        square(3, 0, 2)
+        square(3, 1, 3)
         round_w2(w2_raw[2], PASS, on_scalar)
-        gaussian(3, 2, f"w2_raw{PASS}")
+        exponential(2, f"w2_raw{PASS}")
+        exponential(3)
         v_codes = [pick_words(held([P, S], U32, "v_codes0"), v_words[0], list1, (0, S // 2, S))]
         for unit in range(AHEAD):
             rotor[unit] = bank([P, PACK, UNIT], "a", 4 + unit)
@@ -296,7 +307,13 @@ def tile_list_wake_correction_kernel(
         round_w2(w2_raw[3], PASS + CHUNK, nc.vector.tensor_copy)
         correct(1)
         w2_mx.append(quantise_w2(1))
-        gaussian(4, 2)
+        square(4, 0, 2)
+        square(4, 1, 3)
+        square(5, 0, 2)
+        exponential(4)
+        square(5, 1, 3)
+        square(6, 0, 2)
+        exponential(5)
         rotor_unit(8, 4)
         rotor_unit(9, 5)
         correct(2)
@@ -307,7 +324,6 @@ def tile_list_wake_correction_kernel(
         correct(4)
         quantise_h(h_rest[:, 0:3, :, :], 1, 3)
         correct(5)
-        gaussian(5, 2)
         rotor_unit(10, 0)
         rotor_unit(11, 1)
         correct(8)
@@ -316,18 +332,22 @@ def tile_list_wake_correction_kernel(
         quantise_h(h_second[0][:], 8, 2)
         correct(7)
         accs = [multiply_out(0, pair, 4 + pair) for pair in range(2)]
-        gaussian(6, 2)
+        square(6, 1, 3)
+        store(accs[1], 1, 0, BLOCK, False)
+        square_unit(14, 2)
+        exponential(6)
         rotor_unit(12, 6)
         rotor_unit(13, 7)
         quantise_h(h_rest[:, 3:7, :, :], 4, 4)
         correct(10)
         store(accs[0], 0, 0, BLOCK, True)
         correct(11)
-        store(accs[1], 1, 0, BLOCK, True)
         quantise_h(h_second[1][:], 10, 2)
         accs = [multiply_out(1, pair, pair) for pair in range(2)]
+        square_unit(15, 3)
+        exponential_unit(14)
         store(accs[1], 1, BLOCK, BLOCK, False)
-        gaussian_by_units(7, 2)
+        exponential_unit(15)
         rotor_unit(14, 4)
         rotor_unit(15, 5)
         correct(12)

@@ -27,6 +27,7 @@ CHUNK = 256
 EARLY = 768
 AHEAD = 4
 V2_ROW = 8
+DEALT = 9 * S + H - 512
 W3_ROW = 4
 
 
@@ -100,7 +101,8 @@ def tile_list_wake_correction_kernel(
             return quantise(w2_grouped[g][:].rearrange("p t m j -> p (t m j)"), codes, f"w2_{g}")
 
         def deal_w1_codes(g, a):
-            codes = held([P, 2 * PASS], U8, f"w1_codes{g}_{a}")
+            name = f"w1_codes{g}_{a}"
+            codes = held([P, 2 * PASS], U8, name) if g else placed([P, 2 * PASS], U8, name, DEALT + a * (2 * H - 512))
             nc.gpsimd.tensor_copy(
                 codes[:].bitcast(U16).rearrange("p (t m) -> p t m", t=PACK),
                 w1_raw[g][:, a, :].bitcast(U16).rearrange("p (m t) -> p t m", t=PACK),
@@ -111,7 +113,7 @@ def tile_list_wake_correction_kernel(
         list2 = keep.tile([P, S // 16], U16, name="list2")
         v_scale_rows = held([P, T], U8, "v_scale_rows")
         v2_scale_rows = held([P, T], U8, "v2_scale_rows")
-        w1_scale_rows = held([P, H], U8, "w1_scale_rows")
+        w1_scale_rows = placed([P, H], U8, "w1_scale_rows", DEALT + H - 256)
         w3_scale = held([P, N], U8, "w3_scale")
         plane1 = held([P, S + H], U8, "plane1")
         nc.gpsimd.memset(v_scale_rows[:].bitcast(I32), 0)

@@ -278,9 +278,9 @@ def tile_list_wake_correction_kernel(
         h_codes = [held([P, S], U32, f"h_codes{g}") for g in range(GROUPS)]
         h_first = held([P, 1, UNIT, PACK], BF16, "h_first")
         h_rest = held([P, 2 * BLOCKS - 1, UNIT, PACK], BF16, "h_rest", f"w2_raw{PASS + CHUNK}")
-        h_second = [held([P, 2, UNIT, PACK], BF16, f"h_second{block}") for block in range(BLOCKS)]
+        h_second = [held([P, 2, UNIT, PACK], BF16, f"h_second{block}") for block in range(BLOCKS - 1)]
         minus_h = [h_first[:, 0, :, :]] + [h_rest[:, u, :, :] for u in range(2 * BLOCKS - 1)]
-        minus_h.extend(h_second[u // 2][:, u % 2, :, :] for u in range(2 * BLOCKS))
+        minus_h.extend(h_second[u // 2][:, u % 2, :, :] for u in range(2 * BLOCKS - 2))
         square_unit(0, 0)
         square_unit(1, 1)
         exponential_unit(0)
@@ -309,13 +309,18 @@ def tile_list_wake_correction_kernel(
         round_w2(w2_raw[3], PASS + CHUNK, nc.vector.tensor_copy)
         correct(1)
         w2_mx.append(quantise_w2(1))
-        square(4, 0, 2)
-        square(4, 1, 3)
+        square_unit(8, 2)
+        square_unit(9, 3)
+        exponential_unit(8)
         square(5, 0, 2)
-        exponential(4)
+        exponential_unit(9)
         square(5, 1, 3)
         square(6, 0, 2)
         exponential(5)
+        square(6, 1, 3)
+        square_unit(14, 2)
+        exponential(6)
+        square_unit(15, 3)
         rotor_unit(8, 4)
         rotor_unit(9, 5)
         correct(2)
@@ -329,43 +334,41 @@ def tile_list_wake_correction_kernel(
         rotor_unit(10, 0)
         rotor_unit(11, 1)
         correct(8)
+        quantise_h(h_rest[:, 3:5, :, :], 4, 2)
         correct(9)
         correct(6)
         quantise_h(h_second[0][:], 8, 2)
-        correct(7)
-        accs = [multiply_out(0, pair, 4 + pair) for pair in range(2)]
-        square(6, 1, 3)
-        store(accs[1], 1, 0, BLOCK, False)
-        square_unit(14, 2)
-        exponential(6)
         rotor_unit(12, 6)
-        rotor_unit(13, 7)
-        quantise_h(h_rest[:, 3:7, :, :], 4, 4)
-        correct(10)
-        store(accs[0], 0, 0, BLOCK, True)
-        correct(11)
-        quantise_h(h_second[1][:], 10, 2)
-        accs = [multiply_out(1, pair, pair) for pair in range(2)]
-        square_unit(15, 3)
+        first_block = [multiply_out(0, pair, 4 + pair) for pair in range(2)]
         exponential_unit(14)
-        store(accs[1], 1, BLOCK, BLOCK, False)
+        store(first_block[1], 1, 0, BLOCK, False)
         exponential_unit(15)
-        rotor_unit(14, 4)
-        rotor_unit(15, 5)
+        correct(10)
+        rotor_unit(13, 0)
+        correct(11)
+        store(first_block[0], 0, 0, BLOCK, True)
+        quantise_h(h_second[1][:], 10, 2)
+        second_block = [multiply_out(1, pair, (1, 4)[pair]) for pair in range(2)]
+        store(second_block[1], 1, BLOCK, BLOCK, False)
         correct(12)
+        rotor_unit(14, 6)
+        store(second_block[0], 0, BLOCK, BLOCK, True)
         correct(13)
-        store(accs[0], 0, BLOCK, BLOCK, True)
+        rotor_unit(15, 0)
+        correct(7)
         quantise_h(h_second[2][:], 12, 2)
-        accs = [multiply_out(2, pair, 6 + pair) for pair in range(2)]
-        correct(14)
-        correct(15)
-        for half in range(2):
-            quantise_h(h_second[3][:, half : half + 1, :, :], 14 + half, 1)
+        accs = [multiply_out(2, pair, (2, 3)[pair]) for pair in range(2)]
+        quantise_h(h_rest[:, 5:7, :, :], 6, 2)
+        for unit in (14, 15):
+            last = held([P, 1, UNIT, PACK], BF16, f"h_last{unit}", "h_last")
+            minus_h.append(last[:, 0, :, :])
+            correct(unit)
+            quantise_h(last[:], unit, 1)
         for pair in range(2):
             store(accs[pair], pair, 2 * BLOCK, BLOCK, False)
         for half in range(2):
             first = S - BLOCK + UNIT * half
-            accs = [bank([P, 2, UNIT], "out_tail", (2, 0)[half] + pair) for pair in range(2)]
+            accs = [bank([P, 2, UNIT], "out_tail", ((5, 7), (1, 4))[half][pair]) for pair in range(2)]
             for g in range(GROUPS):
                 for pair in range(2):
                     for u in range(2):

@@ -102,8 +102,9 @@ def tile_list_wake_correction_kernel(
 
         def deal_w1_codes(g, a):
             name = f"w1_codes{g}_{a}"
-            codes = held([P, 2 * PASS], U8, name) if g else placed([P, 2 * PASS], U8, name, DEALT + a * (2 * H - 512))
-            nc.gpsimd.tensor_copy(
+            codes = placed([P, 2 * PASS], U8, name, DEALT) if (g, a) == (0, 1) else held([P, 2 * PASS], U8, name)
+            copy = nc.gpsimd.tensor_copy if g + a else nc.scalar.copy
+            copy(
                 codes[:].bitcast(U16).rearrange("p (t m) -> p t m", t=PACK),
                 w1_raw[g][:, a, :].bitcast(U16).rearrange("p (m t) -> p t m", t=PACK),
             )

@@ -60,7 +60,8 @@ def tile_list_wake_correction_kernel(
 
         def load_w2(first, width):
             raw = held([P, PACK, width], F32, f"w2_raw{first}")
-            nc.sync.dma_start(raw[:], w2.rearrange("(p j) c -> p j c", j=PACK)[:, :, first : first + width])
+            queue = nc.sync if first else nc.scalar
+            queue.dma_start(raw[:], w2.rearrange("(p j) c -> p j c", j=PACK)[:, :, first : first + width])
             return raw
 
         def load_w1(g):

@@ -24,7 +24,7 @@ BLOCK = 256
 BLOCKS = S // BLOCK
 UNIT = 128
 CHUNK = 256
-EARLY = 768
+EARLY = 512
 AHEAD = 4
 V2_ROW = 8
 DEALT = 9 * S + H - 512
@@ -103,9 +103,8 @@ def tile_list_wake_correction_kernel(
 
         def deal_w1_codes(g, a):
             name = f"w1_codes{g}_{a}"
-            codes = placed([P, 2 * PASS], U8, name, DEALT) if (g, a) == (0, 1) else held([P, 2 * PASS], U8, name)
-            copy = nc.gpsimd.tensor_copy if g + a else nc.scalar.copy
-            copy(
+            codes = held([P, 2 * PASS], U8, name) if g else placed([P, 2 * PASS], U8, name, DEALT + a * (2 * H - 512))
+            nc.gpsimd.tensor_copy(
                 codes[:].bitcast(U16).rearrange("p (t m) -> p t m", t=PACK),
                 w1_raw[g][:, a, :].bitcast(U16).rearrange("p (m t) -> p t m", t=PACK),
             )
@@ -132,7 +131,8 @@ def tile_list_wake_correction_kernel(
         w2_raw = [load_w2(first, CHUNK) for first in (0, CHUNK)]
         v2_rows = tab2_scales[0].rearrange("(d r) t -> r d t", r=4)
         for r in range(4):
-            nc.scalar.dma_start(v2_scale_rows[V2_ROW + r : P : 32, :].bitcast(I32), v2_rows[r].bitcast(I32))
+            queue = nc.scalar if r else nc.gpsimd
+            queue.dma_start(v2_scale_rows[V2_ROW + r : P : 32, :].bitcast(I32), v2_rows[r].bitcast(I32))
         v2_words = load_table(tab2_words[0], "v2_words")
         nc.sync.dma_start(w1_scale_rows[0:P:4, :].bitcast(I32), w1_scales.rearrange("a q c -> q a c").bitcast(I32))
         w1_raw = [load_w1(0)]

@@ -22,12 +22,13 @@ PASS = P * PACK
 GROUPS = H // PASS
 BLOCK = 256
 BLOCKS = S // BLOCK
+HALF = S // 2
 UNIT = 128
 CHUNK = 256
-EARLY = 512
 AHEAD = 4
 V2_ROW = 8
-DEALT = 9 * S + H - 512
+W1_ROWS = 1024
+GROUPED = 4096
 W3_ROW = 4
 
 
@@ -45,7 +46,7 @@ def tile_list_wake_correction_kernel(
             return keep.tile(shape, dtype, name=name, tag=tag or name, align_bytes=256)
 
         def placed(shape, dtype, name, offset):
-            return head.tile(shape, dtype, name=name, tag=name, align_bytes=256, offset=offset)
+            return head.tile(shape, dtype, name=name, tag=name, align_bytes=64, offset=offset)
 
         def bank(shape, name, number):
             return psum.tile(shape, F32, name=name, tag=f"bank{number}")
@@ -64,22 +65,19 @@ def tile_list_wake_correction_kernel(
             queue.dma_start(raw[:], w2.rearrange("(p j) c -> p j c", j=PACK)[:, :, first : first + width])
             return raw
 
-        def load_w1(g):
-            raw = held([P, 2, 2 * PASS], U8, f"w1_raw{g}")
+        def load_w1(g, raw):
             columns = w1_words.rearrange("a p c -> p a c")[:, :, 2 * PASS * g : 2 * PASS * (g + 1)]
             nc.sync.dma_start(raw[:].bitcast(I32), columns.bitcast(I32))
             return raw
 
-        def pick_bytes(window, offsets, first, count, name, tag=""):
-            picked = held([P, count], U8, name, tag)
+        def pick_bytes(picked, window, offsets, first):
+            count = picked.shape[1]
             nc.vector.tensor_copy(picked[:], window[:].indirect(entries(offsets, first, count)))
             return picked
 
-        def pick_words(picked, window, offsets, cuts):
-            for first, stop in zip(cuts, cuts[1:]):
-                looked_up = window[:].bitcast(U32).indirect(entries(offsets, first, stop - first))
-                nc.vector.tensor_copy(picked[:, first:stop], looked_up)
-            return picked
+        def pick_words(picked, window, offsets, first):
+            looked_up = window[:].bitcast(U32).indirect(entries(offsets, first, picked.shape[1]))
+            nc.vector.tensor_copy(picked, looked_up)
 
         def on_scalar(dst, src):
             nc.scalar.activation(dst, src, ACT.Copy)
@@ -101,29 +99,30 @@ def tile_list_wake_correction_kernel(
             codes = held([P, PASS], U32, f"w2_codes{g}")
             return quantise(w2_grouped[g][:].rearrange("p t m j -> p (t m j)"), codes, f"w2_{g}")
 
-        def deal_w1_codes(g, a):
-            name = f"w1_codes{g}_{a}"
-            codes = held([P, 2 * PASS], U8, name) if g else placed([P, 2 * PASS], U8, name, DEALT + a * (2 * H - 512))
-            nc.gpsimd.tensor_copy(
+        def deal_w1_codes(g, a, copy, codes):
+            copy(
                 codes[:].bitcast(U16).rearrange("p (t m) -> p t m", t=PACK),
                 w1_raw[g][:, a, :].bitcast(U16).rearrange("p (m t) -> p t m", t=PACK),
             )
-            return codes
+            w1_codes[g, a] = codes
+
+        def move_rows(plane, rows, step):
+            for d in range(4):
+                source = rows[32 * d : 32 * (d + 1) : step, :].bitcast(I32)
+                target = plane[32 * d : 32 * d + 4, :].bitcast(I32).rearrange("p (x c) -> p x c", x=8 // step)
+                nc.sync.dma_start(target, source)
 
         list1 = keep.tile([P, S // 16], U16, name="list1")
         list2 = keep.tile([P, S // 16], U16, name="list2")
         v_scale_rows = held([P, T], U8, "v_scale_rows")
         v2_scale_rows = held([P, T], U8, "v2_scale_rows")
-        w1_scale_rows = placed([P, H], U8, "w1_scale_rows", DEALT + H - 256)
+        w1_scale_rows = placed([P, PASS], U8, "w1_scale_rows", W1_ROWS)
         w3_scale = held([P, N], U8, "w3_scale")
-        plane1 = held([P, S + H], U8, "plane1")
+        v_plane = held([P, 2 * S], U8, "v_plane")
+        w1_plane = held([P, 2 * H], U8, "w1_plane")
         nc.gpsimd.memset(v_scale_rows[:].bitcast(I32), 0)
-        for tile in (v2_scale_rows, w1_scale_rows, plane1, w3_scale):
+        for tile in (v2_scale_rows, w1_scale_rows, v_plane, w1_plane, w3_scale):
             nc.vector.memset(tile[:].bitcast(I32), 0)
-
-        def move_planes(a):
-            for r in range(1 - a, 4):
-                nc.sync.dma_start(planes[a][r:P:32, :].bitcast(I32), staged[8 * r + 4 * a : P : 32, :].bitcast(I32))
 
         nc.sync.dma_start(list1[:], offs)
         nc.sync.dma_start(list2[:], offs2)
@@ -134,31 +133,32 @@ def tile_list_wake_correction_kernel(
             queue = nc.scalar if r else nc.gpsimd
             queue.dma_start(v2_scale_rows[V2_ROW + r : P : 32, :].bitcast(I32), v2_rows[r].bitcast(I32))
         v2_words = load_table(tab2_words[0], "v2_words")
-        nc.sync.dma_start(w1_scale_rows[0:P:4, :].bitcast(I32), w1_scales.rearrange("a q c -> q a c").bitcast(I32))
-        w1_raw = [load_w1(0)]
+        w1_raw = [load_w1(0, held([P, 2, 2 * PASS], U8, "w1_raw0"))]
+        for a in range(2):
+            rows = w1_scales[a].rearrange("q (g c) -> (q g) c", g=GROUPS)
+            nc.sync.dma_start(w1_scale_rows[2 * a : P : 4, :].bitcast(I32), rows.bitcast(I32))
+
         v_words = [load_table(tab_words[0], "v_words0")]
-        w1_raw.append(load_w1(1))
+        move_rows(v_plane, pick_bytes(held([P, S], U8, "v_scale"), v_scale_rows, list1, 0), 4)
+        early_scale = pick_bytes(held([P, HALF], U8, "v2_scale0"), v2_scale_rows, list2, 0)
+        v2_scale = [early_scale[:, BLOCK * half : BLOCK * (half + 1)] for half in range(2)]
 
-        v_scale_picked = pick_bytes(v_scale_rows, list1, 0, S, "v_scale_picked")
-        v2_scale = [pick_bytes(v2_scale_rows, list2, 0, EARLY, "v2_scale0")]
-
-        w2_grouped = [placed([P, PACK, P, PACK], BF16, "w2_grouped0", S + H - 256), held([P, PACK, P, PACK], BF16, "w2_grouped1")]
+        w2_grouped = [held([P, PACK, P, PACK], BF16, "w2_grouped0"), placed([P, PACK, P, PACK], BF16, "w2_grouped1", GROUPED)]
         for chunk in range(2):
             round_w2(w2_raw[chunk], CHUNK * chunk, on_scalar)
         w2_mx = [quantise_w2(0)]
-        v2_codes = placed([P, S], U32, "v2_codes", S + H + 4 * S - 512)
-        pick_words(v2_codes, v2_words, list2, (0, UNIT))
-        staged = placed([P, S + H], U8, "staged", 0)
-        planes = [staged, plane1]
+        v2_codes = [held([P, BLOCK], U32, f"v2_codes{block}")[:] for block in range(2)]
+        for half in range(2):
+            pick_words(v2_codes[0][:, UNIT * half : UNIT * (half + 1)], v2_words, list2, UNIT * half)
+        pick_words(v2_codes[1], v2_words, list2, BLOCK)
+        w1_scale_dealt = held([P, PASS], U8, "w1_scale_dealt")
         nc.vector.tensor_copy(
-            staged[:, S : S + H].rearrange("p (g t m) -> p g t m", g=GROUPS, t=PACK),
-            w1_scale_rows[:].rearrange("p (g m t) -> p g t m", g=GROUPS, t=PACK),
+            w1_scale_dealt[:].rearrange("p (t m) -> p t m", t=PACK),
+            w1_scale_rows[:].rearrange("p (m t) -> p t m", t=PACK),
         )
-        nc.vector.tensor_copy(staged[:, 0:S].bitcast(I32), v_scale_picked[:].bitcast(I32))
-        pick_words(v2_codes, v2_words, list2, (UNIT, S // 2, S))
-        move_planes(0)
+        w1_raw.append(load_w1(1, held([P, 2, 2 * PASS], U8, "w1_raw1")))
+        move_rows(w1_plane, w1_scale_dealt, 2)
         v_words.append(load_table(tab_words[1], "v_words1"))
-        move_planes(1)
         w2_raw.extend(load_w2(first, CHUNK) for first in (PASS, PASS + CHUNK))
         w3_codes = held([P, GROUPS, N], U32, "w3_codes")
         nc.sync.dma_start(w3_codes[:].bitcast(I32), w3_words.rearrange("a p c i -> p a (c i)").bitcast(I32))
@@ -166,27 +166,33 @@ def tile_list_wake_correction_kernel(
             rows = slice(32 * d + W3_ROW, 32 * d + W3_ROW + 8)
             nc.sync.dma_start(w3_scale[rows, :].bitcast(I32), w3_scales[:, 4 * d : 4 * d + 4, :].bitcast(I32))
 
-        w1_codes = {(g, a): deal_w1_codes(g, a) for g in range(GROUPS) for a in range(2)}
-        v2_scale.append(pick_bytes(v2_scale_rows, list2, EARLY, S - EARLY, "v2_scale1", "v2_words"))
+        w1_codes = {}
+        deal_w1_codes(0, 0, nc.scalar.copy, held([P, 2 * PASS], U8, "w1_codes0_0"))
+        deal_w1_codes(0, 1, nc.gpsimd.tensor_copy, placed([P, 2 * PASS], U8, "w1_codes0_1", W1_ROWS + 64 + BLOCK))
+        for a in range(2):
+            deal_w1_codes(1, a, nc.gpsimd.tensor_copy, held([P, 2 * PASS], U8, f"w1_codes1_{a}"))
+        late_scale = placed([P, 2 * BLOCK], U8, "v2_scale2", W1_ROWS + 64 - 2 * BLOCK)
+        pick_bytes(late_scale, v2_scale_rows, list2, 2 * BLOCK)
+        v2_scale.extend(late_scale[:, BLOCK * half : BLOCK * (half + 1)] for half in range(2))
 
         def mast_pass(acc, g, t, first, width):
             codes, scale = w2_mx[g]
             cols = slice(P * t, P * (t + 1))
-            part, at = divmod(first, EARLY)
+            block, at = divmod(first, BLOCK)
             nc.tensor.matmul_mx(
                 out=acc,
                 lhsT=codes[:, cols].bitcast(FP8X4),
                 lhsT_scale=scale[:, cols],
-                rhs=v2_codes[:, first : first + width].bitcast(FP8X4),
-                rhs_scale=v2_scale[part][V2_ROW:P, at : at + width],
+                rhs=v2_codes[block][:, at : at + width].bitcast(FP8X4),
+                rhs_scale=v2_scale[block][V2_ROW:P, at : at + width],
                 start=True,
                 stop=True,
             )
 
-        def square(step, pair, number):
+        def square(step, pair, number, tag=""):
             g, block = divmod(step, BLOCKS)
             if pair == 0:
-                step_squares[step] = held([P, 2, BLOCK, 2], F32, f"squares{step}")
+                step_squares[step] = held([P, 2, BLOCK, 2], F32, f"squares{step}", tag)
             b = bank([P, 2, BLOCK], "b", number)
             for u in range(2):
                 mast_pass(b[:, u, :], g, 2 * pair + u, BLOCK * block, BLOCK)
@@ -213,21 +219,22 @@ def tile_list_wake_correction_kernel(
 
         def rotor_pass(unit, a, start, stop):
             g, first = unit // 8, UNIT * (unit % 8)
+            block, at = divmod(first, BLOCK)
             for t in range(PACK):
                 nc.tensor.matmul_mx(
                     out=rotor[unit][:, t, :],
                     lhsT=w1_codes[g, a][:, 2 * P * t : 2 * P * (t + 1)].bitcast(FP4X4),
-                    lhsT_scale=planes[a][:, S + PASS * g + P * t : S + PASS * g + P * (t + 1)],
-                    rhs=v_codes[a][:, first : first + UNIT].bitcast(FP8X4),
-                    rhs_scale=planes[a][:, first : first + UNIT],
+                    lhsT_scale=w1_plane[:, PASS * (2 * g + a) + P * t : PASS * (2 * g + a) + P * (t + 1)],
+                    rhs=v_codes[a, block][:, at : at + UNIT].bitcast(FP8X4),
+                    rhs_scale=v_plane[:, S * a + first : S * a + first + UNIT],
                     start=(start and t == 0),
                     stop=(stop and t == PACK - 1),
                 )
 
         def rotor_unit(unit, number):
             rotor[unit] = bank([P, PACK, UNIT], "a", number)
-            rotor_pass(unit, 1, True, False)
-            rotor_pass(unit, 0, False, True)
+            rotor_pass(unit, 0, True, False)
+            rotor_pass(unit, 1, False, True)
 
         def correct(unit):
             nc.vector.scalar_tensor_tensor(
@@ -276,104 +283,128 @@ def tile_list_wake_correction_kernel(
                     out_pass(acc[:, u, :], 2 * pair + u, g, BLOCK * block, BLOCK, g + u == 0, g + u == 2)
             return acc
 
-        shares, rotor, step_squares, unit_squares = {}, {}, {}, {}
+        def pick_v2_block(block, tag):
+            v2_codes.append(held([P, BLOCK], U32, f"v2_codes{block}", tag)[:])
+            pick_words(v2_codes[block], v2_words, list2, BLOCK * block)
+
+        def pick_v_block(a, block, tile):
+            v_codes[a, block] = tile
+            pick_words(tile, v_words[a], list1, BLOCK * block)
+
+        def h_tile(first, count, tag="", offset=None):
+            shape = [P, count, UNIT, PACK]
+            tile = held(shape, BF16, f"h{first}", tag) if offset is None else placed(shape, BF16, f"h{first}", offset)
+            for u in range(count):
+                minus_h[first + u] = tile[:, u, :, :]
+            return tile[:]
+
+        shares, rotor, step_squares, unit_squares, minus_h, v_codes = {}, {}, {}, {}, {}, {}
         h_codes = [held([P, S], U32, f"h_codes{g}") for g in range(GROUPS)]
-        h_first = held([P, 1, UNIT, PACK], BF16, "h_first")
-        h_rest = held([P, 2 * BLOCKS - 1, UNIT, PACK], BF16, "h_rest", f"w2_raw{PASS + CHUNK}")
-        h_second = [held([P, 2, UNIT, PACK], BF16, f"h_second{block}") for block in range(BLOCKS - 1)]
-        minus_h = [h_first[:, 0, :, :]] + [h_rest[:, u, :, :] for u in range(2 * BLOCKS - 1)]
-        minus_h.extend(h_second[u // 2][:, u % 2, :, :] for u in range(2 * BLOCKS - 2))
         square_unit(0, 0)
         square_unit(1, 1)
         exponential_unit(0)
         square(1, 0, 2)
         exponential_unit(1)
         square(1, 1, 3)
+        pick_v2_block(2, "squares_unit0")
+        early = [held([P, 2 * BLOCK], U32, f"v_codes{a}") for a in range(2)]
+        pick_words(early[0][:], v_words[0], list1, 0)
+        for block in range(2):
+            v_codes[0, block] = early[0][:, BLOCK * block : BLOCK * (block + 1)]
+        pick_v2_block(3, "squares_unit1")
         square(2, 0, 0)
         exponential(1)
-        h_scale = [held([P, S], U8, f"h_scale{g}", ("share1", "")[g]) for g in range(GROUPS)]
         square(2, 1, 1)
-        square(3, 0, 2)
-        square(3, 1, 3)
-        round_w2(w2_raw[2], PASS, on_scalar)
-        exponential(2, f"w2_raw{PASS}")
-        exponential(3)
-        v_codes = [pick_words(held([P, S], U32, "v_codes0"), v_words[0], list1, (0, S // 2, S))]
         for unit in range(AHEAD):
             rotor[unit] = bank([P, PACK, UNIT], "a", 4 + unit)
             rotor_pass(unit, 0, True, False)
-        v_codes.append(pick_words(held([P, S], U32, "v_codes1"), v_words[1], list1, (0, BLOCK, S // 2, S)))
+        square(3, 0, 2)
+        exponential(2)
+        square(3, 1, 3)
+        for block in range(2):
+            pick_v_block(1, block, early[1][:, BLOCK * block : BLOCK * (block + 1)])
         for unit in range(AHEAD):
             rotor_pass(unit, 1, False, True)
-        rotor_unit(4, 0)
-        rotor_unit(5, 1)
+        exponential(3)
+        rotor_unit(8, 0)
+        rotor_unit(9, 1)
+        h_scale = [held([P, S], U8, f"h_scale{g}", ("share1", "")[g]) for g in range(GROUPS)]
+        h0 = h_tile(0, 2, f"w2_raw{PASS + CHUNK}")
+        for chunk in (2, 3):
+            round_w2(w2_raw[chunk], CHUNK * chunk, nc.vector.tensor_copy)
         correct(0)
-        round_w2(w2_raw[3], PASS + CHUNK, nc.vector.tensor_copy)
-        correct(1)
         w2_mx.append(quantise_w2(1))
+        correct(1)
         square_unit(8, 2)
         square_unit(9, 3)
-        exponential_unit(8)
-        square(5, 0, 2)
-        exponential_unit(9)
-        square(5, 1, 3)
-        square(6, 0, 2)
-        exponential(5)
-        square(6, 1, 3)
-        square_unit(14, 2)
-        exponential(6)
-        square_unit(15, 3)
-        rotor_unit(8, 4)
-        rotor_unit(9, 5)
+        rotor_unit(10, 4)
+        rotor_unit(11, 5)
+        h2 = h_tile(2, 2, offset=GROUPED + 8 * BLOCK)
         correct(2)
         correct(3)
-        rotor_unit(6, 6)
-        rotor_unit(7, 7)
-        quantise_h(h_first[:], 0, 1)
-        correct(4)
-        quantise_h(h_rest[:, 0:3, :, :], 1, 3)
-        correct(5)
-        rotor_unit(10, 0)
-        rotor_unit(11, 1)
+        for a in range(2):
+            pick_v_block(a, 2, placed([P, BLOCK], U32, f"v_codes{a}_2", GROUPED + 4 * BLOCK * a)[:])
+        exponential_unit(8)
+        square(5, 0, 6)
+        exponential_unit(9)
+        square(5, 1, 7)
+        rotor_unit(4, 2)
+        rotor_unit(5, 3)
+        square(6, 0, 6)
+        exponential(5)
+        square(6, 1, 7)
+        quantise_h(h0, 0, 2)
+        quantise_h(h2, 2, 2)
+        h8, h4, h10, h12, h6 = (h_tile(first, 2) for first in (8, 4, 10, 12, 6))
         correct(8)
-        quantise_h(h_rest[:, 3:5, :, :], 4, 2)
         correct(9)
-        correct(6)
-        quantise_h(h_second[0][:], 8, 2)
-        rotor_unit(12, 6)
-        first_block = [multiply_out(0, pair, 4 + pair) for pair in range(2)]
+        correct(4)
+        quantise_h(h8, 8, 2)
+        correct(5)
+        accs = [multiply_out(0, pair, pair) for pair in range(2)]
+        square_unit(14, 6)
+        for pair in range(2):
+            store(accs[pair], pair, 0, BLOCK, False)
+        exponential(6)
+        square_unit(15, 7)
         exponential_unit(14)
-        store(first_block[1], 1, 0, BLOCK, False)
         exponential_unit(15)
+        for a in range(2):
+            pick_v_block(a, 3, held([P, BLOCK], U32, f"v_codes{a}_3", f"share_unit{8 + a}")[:])
+        quantise_h(h4, 4, 2)
+        rotor_unit(6, 2)
+        rotor_unit(7, 3)
         correct(10)
-        rotor_unit(13, 0)
         correct(11)
-        store(first_block[0], 0, 0, BLOCK, True)
-        quantise_h(h_second[1][:], 10, 2)
-        second_block = [multiply_out(1, pair, (1, 4)[pair]) for pair in range(2)]
-        store(second_block[1], 1, BLOCK, BLOCK, False)
-        correct(12)
-        rotor_unit(14, 6)
-        store(second_block[0], 0, BLOCK, BLOCK, True)
-        correct(13)
-        rotor_unit(15, 0)
+        rotor_unit(12, 0)
+        rotor_unit(13, 1)
+        correct(6)
+        quantise_h(h10, 10, 2)
+        accs = [multiply_out(1, pair, 4 + pair) for pair in range(2)]
+        for pair in range(2):
+            store(accs[pair], pair, BLOCK, BLOCK, False)
         correct(7)
-        quantise_h(h_second[2][:], 12, 2)
-        accs = [multiply_out(2, pair, (2, 3)[pair]) for pair in range(2)]
-        quantise_h(h_rest[:, 5:7, :, :], 6, 2)
-        for unit in (14, 15):
-            last = held([P, 1, UNIT, PACK], BF16, f"h_last{unit}", "h_last")
-            minus_h.append(last[:, 0, :, :])
-            correct(unit)
-            quantise_h(last[:], unit, 1)
+        rotor_unit(14, 6)
+        rotor_unit(15, 7)
+        correct(12)
+        quantise_h(h6, 6, 2)
+        correct(13)
+        last = [h_tile(14, 1, "h_last")]
+        correct(14)
+        quantise_h(h12, 12, 2)
+        accs = [multiply_out(2, pair, 2 + pair) for pair in range(2)]
         for pair in range(2):
             store(accs[pair], pair, 2 * BLOCK, BLOCK, False)
+        quantise_h(last[0], 14, 1)
+        last.append(h_tile(15, 1, "h_last"))
+        correct(15)
+        quantise_h(last[1], 15, 1)
         for half in range(2):
             first = S - BLOCK + UNIT * half
-            accs = [bank([P, 2, UNIT], "out_tail", ((5, 7), (1, 4))[half][pair]) for pair in range(2)]
+            accs = [bank([P, 2, UNIT], "out_tail", ((4, 5), (0, 1))[half][pair]) for pair in range(2)]
             for g in range(GROUPS):
                 for pair in range(2):
                     for u in range(2):
                         out_pass(accs[pair][:, u, :], 2 * pair + u, g, first, UNIT, g + u == 0, g + u == 2)
             for pair in range(2):
-                store(accs[pair], pair, first, UNIT, pair == 0)
+                store(accs[pair], pair, first, UNIT, pair == 0 and half == 1)

@@ -90,6 +90,18 @@ def tile_list_wake_correction_kernel(
                 raw[:].rearrange("p j (m t) -> p m j t", t=PACK),
             )
 
+        def round_w2_on_gpsimd(raw, first):
+            g, at = divmod(first, PASS)
+            rows = slice(at // PACK, (at + raw.shape[2]) // PACK)
+            nc.gpsimd.tensor_scalar(
+                out=w2_grouped[g][:, :, rows, :],
+                in0=raw[:].rearrange("p j (m t) -> p t m j", t=PACK),
+                scalar1=1.0,
+                scalar2=0.0,
+                op0=ALU.mult,
+                op1=ALU.add,
+            )
+
         def quantise(values, codes, name):
             scale = held(list(codes.shape), U8, f"{name}_scale")
             nc.vector.quantize_mx(out=codes[:].bitcast(FP8X4), scales=scale[:], in_=values)
@@ -246,23 +258,28 @@ def tile_list_wake_correction_kernel(
                 op1=ALU.mult,
             )
 
-        def quantise_h(tile, first, count):
+        def quantise_h(tile, first, count, tag="", offset=None):
             g, at = divmod(first, 2 * BLOCKS)
             cols = slice(UNIT * at, UNIT * (at + count))
+            shape, name = [P, UNIT * count], f"h_scale{first}"
+            scale = held(shape, U8, name, tag) if offset is None else placed(shape, U8, name, offset)
+            for u in range(count):
+                h_scale[first + u] = (scale, UNIT * u)
             nc.vector.quantize_mx(
                 out=h_codes[g][:, cols].bitcast(FP8X4),
-                scales=h_scale[g][:, cols],
+                scales=scale[:],
                 in_=tile.rearrange("p u n t -> p (u n t)"),
             )
 
         def out_pass(acc, row_tile, g, first, width, start, stop):
             cols = slice(P * row_tile, P * (row_tile + 1))
+            scale, at = h_scale[2 * BLOCKS * g + first // UNIT]
             nc.tensor.matmul_mx(
                 out=acc,
                 lhsT=w3_codes[:, g, cols].bitcast(FP8X4),
                 lhsT_scale=w3_scale[W3_ROW + 4 * g : P, cols],
                 rhs=h_codes[g][:, first : first + width].bitcast(FP8X4),
-                rhs_scale=h_scale[g][:, first : first + width],
+                rhs_scale=scale[:, at : at + width],
                 start=start,
                 stop=stop,
             )
@@ -298,7 +315,7 @@ def tile_list_wake_correction_kernel(
                 minus_h[first + u] = tile[:, u, :, :]
             return tile[:]
 
-        shares, rotor, step_squares, unit_squares, minus_h, v_codes = {}, {}, {}, {}, {}, {}
+        shares, rotor, step_squares, unit_squares, minus_h, v_codes, h_scale = {}, {}, {}, {}, {}, {}, {}
         h_codes = [held([P, S], U32, f"h_codes{g}") for g in range(GROUPS)]
         square_unit(0, 0)
         square_unit(1, 1)
@@ -328,20 +345,16 @@ def tile_list_wake_correction_kernel(
         exponential(3)
         rotor_unit(8, 0)
         rotor_unit(9, 1)
-        h_scale = [held([P, S], U8, f"h_scale{g}", ("share1", "")[g]) for g in range(GROUPS)]
-        h0 = h_tile(0, 2, f"w2_raw{PASS + CHUNK}")
+        h0 = h_tile(0, 4)
         for chunk in (2, 3):
-            round_w2(w2_raw[chunk], CHUNK * chunk, nc.vector.tensor_copy)
-        correct(0)
+            round_w2_on_gpsimd(w2_raw[chunk], CHUNK * chunk)
+        for unit in range(4):
+            correct(unit)
         w2_mx.append(quantise_w2(1))
-        correct(1)
         square_unit(8, 2)
         square_unit(9, 3)
         rotor_unit(10, 4)
         rotor_unit(11, 5)
-        h2 = h_tile(2, 2, offset=GROUPED + 8 * BLOCK)
-        correct(2)
-        correct(3)
         for a in range(2):
             pick_v_block(a, 2, placed([P, BLOCK], U32, f"v_codes{a}_2", GROUPED + 4 * BLOCK * a)[:])
         exponential_unit(8)
@@ -353,52 +366,51 @@ def tile_list_wake_correction_kernel(
         square(6, 0, 6)
         exponential(5)
         square(6, 1, 7)
-        quantise_h(h0, 0, 2)
-        quantise_h(h2, 2, 2)
-        h8, h4, h10, h12, h6 = (h_tile(first, 2) for first in (8, 4, 10, 12, 6))
+        quantise_h(h0, 0, 4, offset=GROUPED + 8 * BLOCK)
+        h8, h10, h12, h6 = (h_tile(first, 2) for first in (8, 10, 12, 6))
+        h4 = h_tile(4, 2, "squares_unit9")
         correct(8)
+        pick_v_block(0, 3, held([P, BLOCK], U32, "v_codes0_3", "squares_unit8")[:])
         correct(9)
         correct(4)
         quantise_h(h8, 8, 2)
         correct(5)
-        accs = [multiply_out(0, pair, pair) for pair in range(2)]
+        pick_v_block(1, 3, held([P, BLOCK], U32, "v_codes1_3", "share_unit9")[:])
+        quantise_h(h4, 4, 2)
+        rotor_unit(12, 2)
+        rotor_unit(13, 3)
         square_unit(14, 6)
+        accs = [multiply_out(0, pair, pair) for pair in range(2)]
         for pair in range(2):
             store(accs[pair], pair, 0, BLOCK, False)
         exponential(6)
         square_unit(15, 7)
         exponential_unit(14)
         exponential_unit(15)
-        for a in range(2):
-            pick_v_block(a, 3, held([P, BLOCK], U32, f"v_codes{a}_3", f"share_unit{8 + a}")[:])
-        quantise_h(h4, 4, 2)
-        rotor_unit(6, 2)
-        rotor_unit(7, 3)
         correct(10)
         correct(11)
-        rotor_unit(12, 0)
-        rotor_unit(13, 1)
+        rotor_unit(6, 4)
+        rotor_unit(7, 5)
         correct(6)
         quantise_h(h10, 10, 2)
-        accs = [multiply_out(1, pair, 4 + pair) for pair in range(2)]
+        accs = [multiply_out(1, pair, pair) for pair in range(2)]
         for pair in range(2):
             store(accs[pair], pair, BLOCK, BLOCK, False)
-        correct(7)
         rotor_unit(14, 6)
         rotor_unit(15, 7)
+        correct(7)
         correct(12)
-        quantise_h(h6, 6, 2)
+        quantise_h(h6, 6, 2, "squares6")
         correct(13)
-        last = [h_tile(14, 1, "h_last")]
+        last = [h_tile(unit, 1) for unit in (14, 15)]
         correct(14)
-        quantise_h(h12, 12, 2)
+        quantise_h(h12, 12, 2, "squares_unit14")
         accs = [multiply_out(2, pair, 2 + pair) for pair in range(2)]
-        for pair in range(2):
-            store(accs[pair], pair, 2 * BLOCK, BLOCK, False)
         quantise_h(last[0], 14, 1)
-        last.append(h_tile(15, 1, "h_last"))
         correct(15)
         quantise_h(last[1], 15, 1)
+        for pair in range(2):
+            store(accs[pair], pair, 2 * BLOCK, BLOCK, False)
         for half in range(2):
             first = S - BLOCK + UNIT * half
             accs = [bank([P, 2, UNIT], "out_tail", ((4, 5), (0, 1))[half][pair]) for pair in range(2)]
@@ -407,4 +419,4 @@ def tile_list_wake_correction_kernel(
                     for u in range(2):
                         out_pass(accs[pair][:, u, :], 2 * pair + u, g, first, UNIT, g + u == 0, g + u == 2)
             for pair in range(2):
-                store(accs[pair], pair, first, UNIT, pair == 0 and half == 1)
+                store(accs[pair], pair, first, UNIT, pair == 0)

@@ -27,8 +27,13 @@ UNIT = 128
 CHUNK = 256
 AHEAD = 4
 V2_ROW = 8
-W1_ROWS = 1024
 GROUPED = 4096
+SQUARES6 = 8192
+PLACES = {
+    "w1_raw0_0": 512, "v2_scale2": 64, "v2_codes2": 576,
+    "squares6": SQUARES6, "h_scale6": SQUARES6, "share_unit14": SQUARES6 + 256,
+}
+AFTER = {"share6": "h_scale8", "squares_unit15": "h_codes8", "h0": "w2_raw768"}
 W3_ROW = 4
 
 
@@ -43,7 +48,9 @@ def tile_list_wake_correction_kernel(
         psum = ctx.enter_context(tc.psum_pool(name="psum", bufs=1))
 
         def held(shape, dtype, name, tag=""):
-            return keep.tile(shape, dtype, name=name, tag=tag or name, align_bytes=256)
+            if name in PLACES:
+                return placed(shape, dtype, name, PLACES[name])
+            return keep.tile(shape, dtype, name=name, tag=tag or AFTER.get(name, name), align_bytes=256)
 
         def placed(shape, dtype, name, offset):
             return head.tile(shape, dtype, name=name, tag=name, align_bytes=64, offset=offset)
@@ -65,10 +72,12 @@ def tile_list_wake_correction_kernel(
             queue.dma_start(raw[:], w2.rearrange("(p j) c -> p j c", j=PACK)[:, :, first : first + width])
             return raw
 
-        def load_w1(g, raw):
-            columns = w1_words.rearrange("a p c -> p a c")[:, :, 2 * PASS * g : 2 * PASS * (g + 1)]
+        def load_w1(g, first, count):
+            raw = held([P, count, 2 * PASS], U8, f"w1_raw{g}_{first}")
+            columns = w1_words.rearrange("a p c -> p a c")[:, first : first + count, 2 * PASS * g : 2 * PASS * (g + 1)]
             nc.sync.dma_start(raw[:].bitcast(I32), columns.bitcast(I32))
-            return raw
+            for a in range(count):
+                w1_raw[g, first + a] = raw[:, a, :]
 
         def pick_bytes(picked, window, offsets, first):
             count = picked.shape[1]
@@ -90,18 +99,6 @@ def tile_list_wake_correction_kernel(
                 raw[:].rearrange("p j (m t) -> p m j t", t=PACK),
             )
 
-        def round_w2_on_gpsimd(raw, first):
-            g, at = divmod(first, PASS)
-            rows = slice(at // PACK, (at + raw.shape[2]) // PACK)
-            nc.gpsimd.tensor_scalar(
-                out=w2_grouped[g][:, :, rows, :],
-                in0=raw[:].rearrange("p j (m t) -> p t m j", t=PACK),
-                scalar1=1.0,
-                scalar2=0.0,
-                op0=ALU.mult,
-                op1=ALU.add,
-            )
-
         def quantise(values, codes, name):
             scale = held(list(codes.shape), U8, f"{name}_scale")
             nc.vector.quantize_mx(out=codes[:].bitcast(FP8X4), scales=scale[:], in_=values)
@@ -114,7 +111,7 @@ def tile_list_wake_correction_kernel(
         def deal_w1_codes(g, a, copy, codes):
             copy(
                 codes[:].bitcast(U16).rearrange("p (t m) -> p t m", t=PACK),
-                w1_raw[g][:, a, :].bitcast(U16).rearrange("p (m t) -> p t m", t=PACK),
+                w1_raw[g, a].bitcast(U16).rearrange("p (m t) -> p t m", t=PACK),
             )
             w1_codes[g, a] = codes
 
@@ -128,10 +125,10 @@ def tile_list_wake_correction_kernel(
         list2 = keep.tile([P, S // 16], U16, name="list2")
         v_scale_rows = held([P, T], U8, "v_scale_rows")
         v2_scale_rows = held([P, T], U8, "v2_scale_rows")
-        w1_scale_rows = placed([P, PASS], U8, "w1_scale_rows", W1_ROWS)
-        w3_scale = held([P, N], U8, "w3_scale")
+        w1_scale_rows = held([P, PASS], U8, "w1_scale_rows")
         v_plane = held([P, 2 * S], U8, "v_plane")
         w1_plane = held([P, 2 * H], U8, "w1_plane")
+        w3_scale = held([P, N], U8, "w3_scale")
         nc.gpsimd.memset(v_scale_rows[:].bitcast(I32), 0)
         for tile in (v2_scale_rows, w1_scale_rows, v_plane, w1_plane, w3_scale):
             nc.vector.memset(tile[:].bitcast(I32), 0)
@@ -144,16 +141,32 @@ def tile_list_wake_correction_kernel(
         for r in range(4):
             queue = nc.scalar if r else nc.gpsimd
             queue.dma_start(v2_scale_rows[V2_ROW + r : P : 32, :].bitcast(I32), v2_rows[r].bitcast(I32))
-        v2_words = load_table(tab2_words[0], "v2_words")
-        w1_raw = [load_w1(0, held([P, 2, 2 * PASS], U8, "w1_raw0"))]
         for a in range(2):
             rows = w1_scales[a].rearrange("q (g c) -> (q g) c", g=GROUPS)
             nc.sync.dma_start(w1_scale_rows[2 * a : P : 4, :].bitcast(I32), rows.bitcast(I32))
+        v2_words = load_table(tab2_words[0], "v2_words")
+        w1_raw = {}
+        for a in range(2):
+            load_w1(0, a, 1)
 
-        v_words = [load_table(tab_words[0], "v_words0")]
         move_rows(v_plane, pick_bytes(held([P, S], U8, "v_scale"), v_scale_rows, list1, 0), 4)
+        v_words = [load_table(tab_words[0], "v_words0")]
+        w1_scale_dealt = held([P, PASS], U8, "w1_scale_dealt")
+        nc.vector.tensor_copy(
+            w1_scale_dealt[:].rearrange("p (t m) -> p t m", t=PACK),
+            w1_scale_rows[:].rearrange("p (m t) -> p t m", t=PACK),
+        )
+        move_rows(w1_plane, w1_scale_dealt, 2)
         early_scale = pick_bytes(held([P, HALF], U8, "v2_scale0"), v2_scale_rows, list2, 0)
         v2_scale = [early_scale[:, BLOCK * half : BLOCK * (half + 1)] for half in range(2)]
+        load_w1(1, 0, 2)
+        v_words.append(load_table(tab_words[1], "v_words1"))
+        w2_raw.extend(load_w2(first, CHUNK) for first in (PASS, PASS + CHUNK))
+        w3_codes = held([P, GROUPS, N], U32, "w3_codes")
+        nc.sync.dma_start(w3_codes[:].bitcast(I32), w3_words.rearrange("a p c i -> p a (c i)").bitcast(I32))
+        for d in range(4):
+            rows = slice(32 * d + W3_ROW, 32 * d + W3_ROW + 8)
+            nc.sync.dma_start(w3_scale[rows, :].bitcast(I32), w3_scales[:, 4 * d : 4 * d + 4, :].bitcast(I32))
 
         w2_grouped = [held([P, PACK, P, PACK], BF16, "w2_grouped0"), placed([P, PACK, P, PACK], BF16, "w2_grouped1", GROUPED)]
         for chunk in range(2):
@@ -163,29 +176,12 @@ def tile_list_wake_correction_kernel(
         for half in range(2):
             pick_words(v2_codes[0][:, UNIT * half : UNIT * (half + 1)], v2_words, list2, UNIT * half)
         pick_words(v2_codes[1], v2_words, list2, BLOCK)
-        w1_scale_dealt = held([P, PASS], U8, "w1_scale_dealt")
-        nc.vector.tensor_copy(
-            w1_scale_dealt[:].rearrange("p (t m) -> p t m", t=PACK),
-            w1_scale_rows[:].rearrange("p (m t) -> p t m", t=PACK),
-        )
-        w1_raw.append(load_w1(1, held([P, 2, 2 * PASS], U8, "w1_raw1")))
-        move_rows(w1_plane, w1_scale_dealt, 2)
-        v_words.append(load_table(tab_words[1], "v_words1"))
-        w2_raw.extend(load_w2(first, CHUNK) for first in (PASS, PASS + CHUNK))
-        w3_codes = held([P, GROUPS, N], U32, "w3_codes")
-        nc.sync.dma_start(w3_codes[:].bitcast(I32), w3_words.rearrange("a p c i -> p a (c i)").bitcast(I32))
-        for d in range(4):
-            rows = slice(32 * d + W3_ROW, 32 * d + W3_ROW + 8)
-            nc.sync.dma_start(w3_scale[rows, :].bitcast(I32), w3_scales[:, 4 * d : 4 * d + 4, :].bitcast(I32))
 
         w1_codes = {}
         deal_w1_codes(0, 0, nc.scalar.copy, held([P, 2 * PASS], U8, "w1_codes0_0"))
-        deal_w1_codes(0, 1, nc.gpsimd.tensor_copy, placed([P, 2 * PASS], U8, "w1_codes0_1", W1_ROWS + 64 + BLOCK))
+        deal_w1_codes(0, 1, nc.gpsimd.tensor_copy, held([P, 2 * PASS], U8, "w1_codes0_1"))
         for a in range(2):
             deal_w1_codes(1, a, nc.gpsimd.tensor_copy, held([P, 2 * PASS], U8, f"w1_codes1_{a}"))
-        late_scale = placed([P, 2 * BLOCK], U8, "v2_scale2", W1_ROWS + 64 - 2 * BLOCK)
-        pick_bytes(late_scale, v2_scale_rows, list2, 2 * BLOCK)
-        v2_scale.extend(late_scale[:, BLOCK * half : BLOCK * (half + 1)] for half in range(2))
 
         def mast_pass(acc, g, t, first, width):
             codes, scale = w2_mx[g]
@@ -259,26 +255,25 @@ def tile_list_wake_correction_kernel(
             )
 
         def quantise_h(tile, first, count, tag="", offset=None):
-            g, at = divmod(first, 2 * BLOCKS)
-            cols = slice(UNIT * at, UNIT * (at + count))
             shape, name = [P, UNIT * count], f"h_scale{first}"
             scale = held(shape, U8, name, tag) if offset is None else placed(shape, U8, name, offset)
+            codes = held(shape, U32, f"h_codes{first}")
             for u in range(count):
-                h_scale[first + u] = (scale, UNIT * u)
+                h_mx[first + u] = (codes, scale, UNIT * u)
             nc.vector.quantize_mx(
-                out=h_codes[g][:, cols].bitcast(FP8X4),
+                out=codes[:].bitcast(FP8X4),
                 scales=scale[:],
                 in_=tile.rearrange("p u n t -> p (u n t)"),
             )
 
         def out_pass(acc, row_tile, g, first, width, start, stop):
             cols = slice(P * row_tile, P * (row_tile + 1))
-            scale, at = h_scale[2 * BLOCKS * g + first // UNIT]
+            codes, scale, at = h_mx[2 * BLOCKS * g + first // UNIT]
             nc.tensor.matmul_mx(
                 out=acc,
                 lhsT=w3_codes[:, g, cols].bitcast(FP8X4),
                 lhsT_scale=w3_scale[W3_ROW + 4 * g : P, cols],
-                rhs=h_codes[g][:, first : first + width].bitcast(FP8X4),
+                rhs=codes[:, at : at + width].bitcast(FP8X4),
                 rhs_scale=scale[:, at : at + width],
                 start=start,
                 stop=stop,
@@ -300,10 +295,6 @@ def tile_list_wake_correction_kernel(
                     out_pass(acc[:, u, :], 2 * pair + u, g, BLOCK * block, BLOCK, g + u == 0, g + u == 2)
             return acc
 
-        def pick_v2_block(block, tag):
-            v2_codes.append(held([P, BLOCK], U32, f"v2_codes{block}", tag)[:])
-            pick_words(v2_codes[block], v2_words, list2, BLOCK * block)
-
         def pick_v_block(a, block, tile):
             v_codes[a, block] = tile
             pick_words(tile, v_words[a], list1, BLOCK * block)
@@ -315,60 +306,66 @@ def tile_list_wake_correction_kernel(
                 minus_h[first + u] = tile[:, u, :, :]
             return tile[:]
 
-        shares, rotor, step_squares, unit_squares, minus_h, v_codes, h_scale = {}, {}, {}, {}, {}, {}, {}
-        h_codes = [held([P, S], U32, f"h_codes{g}") for g in range(GROUPS)]
+        shares, rotor, step_squares, unit_squares, minus_h, v_codes, h_mx = {}, {}, {}, {}, {}, {}, {}
         square_unit(0, 0)
         square_unit(1, 1)
         exponential_unit(0)
         square(1, 0, 2)
         exponential_unit(1)
         square(1, 1, 3)
-        pick_v2_block(2, "squares_unit0")
-        early = [held([P, 2 * BLOCK], U32, f"v_codes{a}") for a in range(2)]
+        late_scale = pick_bytes(held([P, HALF], U8, "v2_scale2"), v2_scale_rows, list2, HALF)
+        v2_scale.extend(late_scale[:, BLOCK * half : BLOCK * (half + 1)] for half in range(2))
+        late_codes = held([P, HALF], U32, "v2_codes2")
+        pick_words(late_codes[:], v2_words, list2, HALF)
+        v2_codes.extend(late_codes[:, BLOCK * half : BLOCK * (half + 1)] for half in range(2))
+        early = [held([P, HALF], U32, "v_codes0")]
         pick_words(early[0][:], v_words[0], list1, 0)
         for block in range(2):
             v_codes[0, block] = early[0][:, BLOCK * block : BLOCK * (block + 1)]
-        pick_v2_block(3, "squares_unit1")
-        square(2, 0, 0)
+        square(2, 0, 4)
         exponential(1)
-        square(2, 1, 1)
+        square(2, 1, 5)
         for unit in range(AHEAD):
-            rotor[unit] = bank([P, PACK, UNIT], "a", 4 + unit)
+            rotor[unit] = bank([P, PACK, UNIT], "a", unit)
             rotor_pass(unit, 0, True, False)
-        square(3, 0, 2)
+        early.append(held([P, HALF], U32, "v_codes1"))
+        pick_v_block(1, 0, early[1][:, 0:BLOCK])
+        pick_v_block(1, 1, early[1][:, BLOCK:HALF])
+        square(3, 0, 6)
         exponential(2)
-        square(3, 1, 3)
-        for block in range(2):
-            pick_v_block(1, block, early[1][:, BLOCK * block : BLOCK * (block + 1)])
+        square(3, 1, 7)
         for unit in range(AHEAD):
             rotor_pass(unit, 1, False, True)
         exponential(3)
-        rotor_unit(8, 0)
-        rotor_unit(9, 1)
-        h0 = h_tile(0, 4)
+        rotor_unit(8, 4)
+        rotor_unit(9, 5)
+        h0, h2 = h_tile(0, 2), h_tile(2, 2, offset=GROUPED + 8 * BLOCK)
         for chunk in (2, 3):
-            round_w2_on_gpsimd(w2_raw[chunk], CHUNK * chunk)
-        for unit in range(4):
-            correct(unit)
+            round_w2(w2_raw[chunk], CHUNK * chunk, nc.vector.tensor_copy)
+        correct(0)
         w2_mx.append(quantise_w2(1))
-        square_unit(8, 2)
-        square_unit(9, 3)
-        rotor_unit(10, 4)
-        rotor_unit(11, 5)
+        correct(1)
+        square_unit(8, 0)
+        square_unit(9, 1)
+        correct(2)
+        correct(3)
         for a in range(2):
             pick_v_block(a, 2, placed([P, BLOCK], U32, f"v_codes{a}_2", GROUPED + 4 * BLOCK * a)[:])
         exponential_unit(8)
-        square(5, 0, 6)
+        square(5, 0, 2)
         exponential_unit(9)
-        square(5, 1, 7)
-        rotor_unit(4, 2)
-        rotor_unit(5, 3)
-        square(6, 0, 6)
+        square(5, 1, 3)
+        rotor_unit(10, 0)
+        rotor_unit(11, 1)
+        rotor_unit(4, 6)
+        rotor_unit(5, 7)
+        square(6, 0, 2)
         exponential(5)
-        square(6, 1, 7)
-        quantise_h(h0, 0, 4, offset=GROUPED + 8 * BLOCK)
+        square(6, 1, 3)
+        quantise_h(h0, 0, 2, "share1")
+        quantise_h(h2, 2, 2)
         h8, h10, h12, h6 = (h_tile(first, 2) for first in (8, 10, 12, 6))
-        h4 = h_tile(4, 2, "squares_unit9")
+        h4 = h_tile(4, 2)
         correct(8)
         pick_v_block(0, 3, held([P, BLOCK], U32, "v_codes0_3", "squares_unit8")[:])
         correct(9)
@@ -377,35 +374,35 @@ def tile_list_wake_correction_kernel(
         correct(5)
         pick_v_block(1, 3, held([P, BLOCK], U32, "v_codes1_3", "share_unit9")[:])
         quantise_h(h4, 4, 2)
-        rotor_unit(12, 2)
-        rotor_unit(13, 3)
-        square_unit(14, 6)
-        accs = [multiply_out(0, pair, pair) for pair in range(2)]
+        square_unit(14, 2)
+        accs = [multiply_out(0, pair, 4 + pair) for pair in range(2)]
         for pair in range(2):
             store(accs[pair], pair, 0, BLOCK, False)
+        rotor_unit(12, 4)
+        rotor_unit(13, 5)
         exponential(6)
-        square_unit(15, 7)
+        square_unit(15, 3)
         exponential_unit(14)
         exponential_unit(15)
         correct(10)
         correct(11)
-        rotor_unit(6, 4)
-        rotor_unit(7, 5)
+        rotor_unit(6, 0)
+        rotor_unit(7, 1)
         correct(6)
         quantise_h(h10, 10, 2)
-        accs = [multiply_out(1, pair, pair) for pair in range(2)]
+        accs = [multiply_out(1, pair, 6 + pair) for pair in range(2)]
         for pair in range(2):
             store(accs[pair], pair, BLOCK, BLOCK, False)
-        rotor_unit(14, 6)
-        rotor_unit(15, 7)
+        rotor_unit(14, 2)
+        rotor_unit(15, 3)
         correct(7)
         correct(12)
-        quantise_h(h6, 6, 2, "squares6")
+        quantise_h(h6, 6, 2)
         correct(13)
         last = [h_tile(unit, 1) for unit in (14, 15)]
         correct(14)
         quantise_h(h12, 12, 2, "squares_unit14")
-        accs = [multiply_out(2, pair, 2 + pair) for pair in range(2)]
+        accs = [multiply_out(2, pair, 4 + pair) for pair in range(2)]
         quantise_h(last[0], 14, 1)
         correct(15)
         quantise_h(last[1], 15, 1)
@@ -413,7 +410,7 @@ def tile_list_wake_correction_kernel(
             store(accs[pair], pair, 2 * BLOCK, BLOCK, False)
         for half in range(2):
             first = S - BLOCK + UNIT * half
-            accs = [bank([P, 2, UNIT], "out_tail", ((4, 5), (0, 1))[half][pair]) for pair in range(2)]
+            accs = [bank([P, 2, UNIT], "out_tail", ((0, 1), (6, 7))[half][pair]) for pair in range(2)]
             for g in range(GROUPS):
                 for pair in range(2):
                     for u in range(2):

@@ -33,7 +33,7 @@ PLACES = {
     "w1_raw0_0": 512, "v2_scale2": 64, "v2_codes2": 576,
     "squares6": SQUARES6, "h_scale6": SQUARES6, "share_unit14": SQUARES6 + 256,
 }
-AFTER = {"share6": "h_scale8", "squares_unit15": "h_codes8", "h0": "w2_raw768"}
+AFTER = {"squares_unit15": "h_codes8", "h0": "w2_raw768"}
 W3_ROW = 4
 
 
@@ -295,9 +295,10 @@ def tile_list_wake_correction_kernel(
                     out_pass(acc[:, u, :], 2 * pair + u, g, BLOCK * block, BLOCK, g + u == 0, g + u == 2)
             return acc
 
-        def pick_v_block(a, block, tile):
-            v_codes[a, block] = tile
-            pick_words(tile, v_words[a], list1, BLOCK * block)
+        def pick_v_half(a, half, tile):
+            pick_words(tile[:], v_words[a], list1, HALF * half)
+            for block in range(2):
+                v_codes[a, 2 * half + block] = tile[:, BLOCK * block : BLOCK * (block + 1)]
 
         def h_tile(first, count, tag="", offset=None):
             shape = [P, count, UNIT, PACK]
@@ -318,19 +319,14 @@ def tile_list_wake_correction_kernel(
         late_codes = held([P, HALF], U32, "v2_codes2")
         pick_words(late_codes[:], v2_words, list2, HALF)
         v2_codes.extend(late_codes[:, BLOCK * half : BLOCK * (half + 1)] for half in range(2))
-        early = [held([P, HALF], U32, "v_codes0")]
-        pick_words(early[0][:], v_words[0], list1, 0)
-        for block in range(2):
-            v_codes[0, block] = early[0][:, BLOCK * block : BLOCK * (block + 1)]
+        pick_v_half(0, 0, held([P, HALF], U32, "v_codes0_0"))
         square(2, 0, 4)
         exponential(1)
         square(2, 1, 5)
         for unit in range(AHEAD):
             rotor[unit] = bank([P, PACK, UNIT], "a", unit)
             rotor_pass(unit, 0, True, False)
-        early.append(held([P, HALF], U32, "v_codes1"))
-        pick_v_block(1, 0, early[1][:, 0:BLOCK])
-        pick_v_block(1, 1, early[1][:, BLOCK:HALF])
+        pick_v_half(1, 0, held([P, HALF], U32, "v_codes1_0"))
         square(3, 0, 6)
         exponential(2)
         square(3, 1, 7)
@@ -339,7 +335,7 @@ def tile_list_wake_correction_kernel(
         exponential(3)
         rotor_unit(8, 4)
         rotor_unit(9, 5)
-        h0, h2 = h_tile(0, 2), h_tile(2, 2, offset=GROUPED + 8 * BLOCK)
+        h0 = h_tile(0, 4)
         for chunk in (2, 3):
             round_w2(w2_raw[chunk], CHUNK * chunk, nc.vector.tensor_copy)
         correct(0)
@@ -350,7 +346,7 @@ def tile_list_wake_correction_kernel(
         correct(2)
         correct(3)
         for a in range(2):
-            pick_v_block(a, 2, placed([P, BLOCK], U32, f"v_codes{a}_2", GROUPED + 4 * BLOCK * a)[:])
+            pick_v_half(a, 1, placed([P, HALF], U32, f"v_codes{a}_1", GROUPED + 4 * HALF * a))
         exponential_unit(8)
         square(5, 0, 2)
         exponential_unit(9)
@@ -362,20 +358,18 @@ def tile_list_wake_correction_kernel(
         square(6, 0, 2)
         exponential(5)
         square(6, 1, 3)
-        quantise_h(h0, 0, 2, "share1")
-        quantise_h(h2, 2, 2)
         h8, h10, h12, h6 = (h_tile(first, 2) for first in (8, 10, 12, 6))
-        h4 = h_tile(4, 2)
         correct(8)
-        pick_v_block(0, 3, held([P, BLOCK], U32, "v_codes0_3", "squares_unit8")[:])
         correct(9)
-        correct(4)
+        quantise_h(h0, 0, 4, "squares_unit9")
         quantise_h(h8, 8, 2)
+        h4 = h_tile(4, 2, "w2_raw768")
+        correct(4)
         correct(5)
-        pick_v_block(1, 3, held([P, BLOCK], U32, "v_codes1_3", "share_unit9")[:])
-        quantise_h(h4, 4, 2)
-        square_unit(14, 2)
         accs = [multiply_out(0, pair, 4 + pair) for pair in range(2)]
+        square_unit(14, 2)
+        rotor_unit(6, 6)
+        rotor_unit(7, 7)
         for pair in range(2):
             store(accs[pair], pair, 0, BLOCK, False)
         rotor_unit(12, 4)
@@ -385,12 +379,11 @@ def tile_list_wake_correction_kernel(
         exponential_unit(14)
         exponential_unit(15)
         correct(10)
+        quantise_h(h4, 4, 2, "squares5")
         correct(11)
-        rotor_unit(6, 0)
-        rotor_unit(7, 1)
         correct(6)
         quantise_h(h10, 10, 2)
-        accs = [multiply_out(1, pair, 6 + pair) for pair in range(2)]
+        accs = [multiply_out(1, pair, pair) for pair in range(2)]
         for pair in range(2):
             store(accs[pair], pair, BLOCK, BLOCK, False)
         rotor_unit(14, 2)
@@ -410,7 +403,7 @@ def tile_list_wake_correction_kernel(
             store(accs[pair], pair, 2 * BLOCK, BLOCK, False)
         for half in range(2):
             first = S - BLOCK + UNIT * half
-            accs = [bank([P, 2, UNIT], "out_tail", ((0, 1), (6, 7))[half][pair]) for pair in range(2)]
+            accs = [bank([P, 2, UNIT], "out_tail", ((6, 7), (0, 1))[half][pair]) for pair in range(2)]
             for g in range(GROUPS):
                 for pair in range(2):
                     for u in range(2):

@@ -30,10 +30,10 @@ V2_ROW = 8
 GROUPED = 4096
 SQUARES6 = 8192
 PLACES = {
-    "w1_raw0_0": 512, "v2_scale2": 64, "v2_codes2": 576,
-    "squares6": SQUARES6, "h_scale6": SQUARES6, "share_unit14": SQUARES6 + 256,
+    "w1_raw0_0": 512, "v2_scale2": 64, "v2_scale1": 576, "v2_codes2": 832,
+    "squares6": SQUARES6, "h_scale6": SQUARES6,
 }
-AFTER = {"squares_unit15": "h_codes8", "h0": "w2_raw768"}
+AFTER = {"share_unit14": "h_scale10", "share_unit15": "h_codes10", "squares_unit15": "h_codes8", "h0": "w2_raw768"}
 W3_ROW = 4
 
 
@@ -72,12 +72,12 @@ def tile_list_wake_correction_kernel(
             queue.dma_start(raw[:], w2.rearrange("(p j) c -> p j c", j=PACK)[:, :, first : first + width])
             return raw
 
-        def load_w1(g, first, count):
-            raw = held([P, count, 2 * PASS], U8, f"w1_raw{g}_{first}")
-            columns = w1_words.rearrange("a p c -> p a c")[:, first : first + count, 2 * PASS * g : 2 * PASS * (g + 1)]
+        def load_w1(a, first, count):
+            raw = held([P, count, 2 * PASS], U8, f"w1_raw{first}_{a}")
+            columns = w1_words[a].rearrange("p (g c) -> p g c", g=GROUPS)[:, first : first + count, :]
             nc.sync.dma_start(raw[:].bitcast(I32), columns.bitcast(I32))
-            for a in range(count):
-                w1_raw[g, first + a] = raw[:, a, :]
+            for g in range(count):
+                w1_raw[first + g, a] = raw[:, g, :]
 
         def pick_bytes(picked, window, offsets, first):
             count = picked.shape[1]
@@ -146,8 +146,8 @@ def tile_list_wake_correction_kernel(
             nc.sync.dma_start(w1_scale_rows[2 * a : P : 4, :].bitcast(I32), rows.bitcast(I32))
         v2_words = load_table(tab2_words[0], "v2_words")
         w1_raw = {}
-        for a in range(2):
-            load_w1(0, a, 1)
+        load_w1(0, 0, 1)
+        load_w1(1, 0, 2)
 
         move_rows(v_plane, pick_bytes(held([P, S], U8, "v_scale"), v_scale_rows, list1, 0), 4)
         v_words = [load_table(tab_words[0], "v_words0")]
@@ -157,9 +157,8 @@ def tile_list_wake_correction_kernel(
             w1_scale_rows[:].rearrange("p (m t) -> p t m", t=PACK),
         )
         move_rows(w1_plane, w1_scale_dealt, 2)
-        early_scale = pick_bytes(held([P, HALF], U8, "v2_scale0"), v2_scale_rows, list2, 0)
-        v2_scale = [early_scale[:, BLOCK * half : BLOCK * (half + 1)] for half in range(2)]
-        load_w1(1, 0, 2)
+        v2_scale = [pick_bytes(held([P, BLOCK], U8, "v2_scale0"), v2_scale_rows, list2, 0)[:]]
+        load_w1(0, 1, 1)
         v_words.append(load_table(tab_words[1], "v_words1"))
         w2_raw.extend(load_w2(first, CHUNK) for first in (PASS, PASS + CHUNK))
         w3_codes = held([P, GROUPS, N], U32, "w3_codes")
@@ -180,7 +179,7 @@ def tile_list_wake_correction_kernel(
         w1_codes = {}
         deal_w1_codes(0, 0, nc.scalar.copy, held([P, 2 * PASS], U8, "w1_codes0_0"))
         deal_w1_codes(0, 1, nc.gpsimd.tensor_copy, held([P, 2 * PASS], U8, "w1_codes0_1"))
-        for a in range(2):
+        for a in (1, 0):
             deal_w1_codes(1, a, nc.gpsimd.tensor_copy, held([P, 2 * PASS], U8, f"w1_codes1_{a}"))
 
         def mast_pass(acc, g, t, first, width):
@@ -308,6 +307,7 @@ def tile_list_wake_correction_kernel(
             return tile[:]
 
         shares, rotor, step_squares, unit_squares, minus_h, v_codes, h_mx = {}, {}, {}, {}, {}, {}, {}
+        v2_scale.append(pick_bytes(held([P, BLOCK], U8, "v2_scale1"), v2_scale_rows, list2, BLOCK)[:])
         square_unit(0, 0)
         square_unit(1, 1)
         exponential_unit(0)
@@ -376,8 +376,6 @@ def tile_list_wake_correction_kernel(
         rotor_unit(13, 5)
         exponential(6)
         square_unit(15, 3)
-        exponential_unit(14)
-        exponential_unit(15)
         correct(10)
         quantise_h(h4, 4, 2, "squares5")
         correct(11)
@@ -386,18 +384,19 @@ def tile_list_wake_correction_kernel(
         accs = [multiply_out(1, pair, pair) for pair in range(2)]
         for pair in range(2):
             store(accs[pair], pair, BLOCK, BLOCK, False)
+            exponential_unit(14 + pair)
         rotor_unit(14, 2)
         rotor_unit(15, 3)
         correct(7)
         correct(12)
-        quantise_h(h6, 6, 2)
         correct(13)
+        quantise_h(h6, 6, 2)
+        quantise_h(h12, 12, 2)
+        accs = [multiply_out(2, pair, 4 + pair) for pair in range(2)]
         last = [h_tile(unit, 1) for unit in (14, 15)]
         correct(14)
-        quantise_h(h12, 12, 2, "squares_unit14")
-        accs = [multiply_out(2, pair, 4 + pair) for pair in range(2)]
-        quantise_h(last[0], 14, 1)
         correct(15)
+        quantise_h(last[0], 14, 1)
         quantise_h(last[1], 15, 1)
         for pair in range(2):
             store(accs[pair], pair, 2 * BLOCK, BLOCK, False)

@@ -30,7 +30,7 @@ V2_ROW = 8
 GROUPED = 4096
 SQUARES6 = 8192
 PLACES = {
-    "w1_raw0_0": 512, "v2_scale2": 64, "v2_scale1": 576, "v2_codes2": 832,
+    "w1_raw0_0": 512, "v2_scale2": 256, "v2_scale1": 768, "v2_codes2": 1024,
     "squares6": SQUARES6, "h_scale6": SQUARES6,
 }
 AFTER = {"share_unit14": "h_scale10", "share_unit15": "h_codes10", "squares_unit15": "h_codes8", "h0": "w2_raw768"}
@@ -53,7 +53,7 @@ def tile_list_wake_correction_kernel(
             return keep.tile(shape, dtype, name=name, tag=tag or AFTER.get(name, name), align_bytes=256)
 
         def placed(shape, dtype, name, offset):
-            return head.tile(shape, dtype, name=name, tag=name, align_bytes=64, offset=offset)
+            return head.tile(shape, dtype, name=name, tag=name, align_bytes=256, offset=offset)
 
         def bank(shape, name, number):
             return psum.tile(shape, F32, name=name, tag=f"bank{number}")

from contextlib import ExitStack

import concourse.mybir as mybir

K, K2, H, N, T, S = 1024, 512, 1024, 512, 2048, 1024
FLOPS = 2 * S * (K * H + K2 * H + H * N)

F32 = mybir.dt.float32
BF16 = mybir.dt.bfloat16
I32 = mybir.dt.int32
U32 = mybir.dt.uint32
U16 = mybir.dt.uint16
U8 = mybir.dt.uint8
FP8X4 = mybir.dt.float8_e4m3fn_x4
FP4X4 = mybir.dt.float4_e2m1fn_x4
ACT = mybir.ActivationFunctionType
ALU = mybir.AluOpType

P = 128
PACK = 4
PASS = P * PACK
GROUPS = H // PASS
BLOCK = 256
BLOCKS = S // BLOCK
HALF = S // 2
UNIT = 128
CHUNK = 256
AHEAD = 4
V2_ROW = 8
GROUPED = 4096
SQUARES6 = 8192
PLACES = {
    "w1_raw0_0": 512, "v2_scale2": 256, "v2_scale1": 768, "v2_codes2": 1024,
    "squares6": SQUARES6, "h_scale6": SQUARES6,
}
AFTER = {"share_unit14": "h_scale10", "share_unit15": "h_codes10", "squares_unit15": "h_codes8", "h0": "w2_raw768"}
W3_ROW = 4


def tile_list_wake_correction_kernel(
    tc, tab_words, tab_scales, offs, tab2_words, tab2_scales, offs2,
    w1_words, w1_scales, w2, w3_words, w3_scales, out,
):
    nc = tc.nc
    with ExitStack() as ctx:
        keep = ctx.enter_context(tc.tile_pool(name="keep", bufs=1))
        head = ctx.enter_context(tc.tile_pool(name="head", bufs=1))
        psum = ctx.enter_context(tc.psum_pool(name="psum", bufs=1))

        def held(shape, dtype, name, tag=""):
            if name in PLACES:
                return placed(shape, dtype, name, PLACES[name])
            return keep.tile(shape, dtype, name=name, tag=tag or AFTER.get(name, name), align_bytes=256)

        def placed(shape, dtype, name, offset):
            return head.tile(shape, dtype, name=name, tag=name, align_bytes=256, offset=offset)

        def bank(shape, name, number):
            return psum.tile(shape, F32, name=name, tag=f"bank{number}")

        def entries(offsets, first, count):
            return offsets[:, first // 16 : (first + count) // 16]

        def load_table(words, name):
            window = held([P, T], I32, name)
            nc.sync.dma_start(window[:], words.rearrange("p t i -> p (t i)").bitcast(I32))
            return window

        def load_w2(first, width):
            raw = held([P, PACK, width], F32, f"w2_raw{first}")
            queue = nc.sync if first else nc.scalar
            queue.dma_start(raw[:], w2.rearrange("(p j) c -> p j c", j=PACK)[:, :, first : first + width])
            return raw

        def load_w1(a, first, count):
            raw = held([P, count, 2 * PASS], U8, f"w1_raw{first}_{a}")
            columns = w1_words[a].rearrange("p (g c) -> p g c", g=GROUPS)[:, first : first + count, :]
            nc.sync.dma_start(raw[:].bitcast(I32), columns.bitcast(I32))
            for g in range(count):
                w1_raw[first + g, a] = raw[:, g, :]

        def pick_bytes(picked, window, offsets, first):
            count = picked.shape[1]
            nc.vector.tensor_copy(picked[:], window[:].indirect(entries(offsets, first, count)))
            return picked

        def pick_words(picked, window, offsets, first):
            looked_up = window[:].bitcast(U32).indirect(entries(offsets, first, picked.shape[1]))
            nc.vector.tensor_copy(picked, looked_up)

        def on_scalar(dst, src):
            nc.scalar.activation(dst, src, ACT.Copy)

        def round_w2(raw, first, copy):
            g, at = divmod(first, PASS)
            rows = slice(at // PACK, (at + raw.shape[2]) // PACK)
            copy(
                w2_grouped[g][:, :, rows, :].rearrange("p t m j -> p m j t"),
                raw[:].rearrange("p j (m t) -> p m j t", t=PACK),
            )

        def quantise(values, codes, name):
            scale = held(list(codes.shape), U8, f"{name}_scale")
            nc.vector.quantize_mx(out=codes[:].bitcast(FP8X4), scales=scale[:], in_=values)
            return codes, scale

        def quantise_w2(g):
            codes = held([P, PASS], U32, f"w2_codes{g}")
            return quantise(w2_grouped[g][:].rearrange("p t m j -> p (t m j)"), codes, f"w2_{g}")

        def deal_w1_codes(g, a, copy, codes):
            copy(
                codes[:].bitcast(U16).rearrange("p (t m) -> p t m", t=PACK),
                w1_raw[g, a].bitcast(U16).rearrange("p (m t) -> p t m", t=PACK),
            )
            w1_codes[g, a] = codes

        def move_rows(plane, rows, step):
            for d in range(4):
                source = rows[32 * d : 32 * (d + 1) : step, :].bitcast(I32)
                target = plane[32 * d : 32 * d + 4, :].bitcast(I32).rearrange("p (x c) -> p x c", x=8 // step)
                nc.sync.dma_start(target, source)

        list1 = keep.tile([P, S // 16], U16, name="list1")
        list2 = keep.tile([P, S // 16], U16, name="list2")
        v_scale_rows = held([P, T], U8, "v_scale_rows")
        v2_scale_rows = held([P, T], U8, "v2_scale_rows")
        w1_scale_rows = held([P, PASS], U8, "w1_scale_rows")
        v_plane = held([P, 2 * S], U8, "v_plane")
        w1_plane = held([P, 2 * H], U8, "w1_plane")
        w3_scale = held([P, N], U8, "w3_scale")
        nc.gpsimd.memset(v_scale_rows[:].bitcast(I32), 0)
        for tile in (v2_scale_rows, w1_scale_rows, v_plane, w1_plane, w3_scale):
            nc.vector.memset(tile[:].bitcast(I32), 0)

        nc.sync.dma_start(list1[:], offs)
        nc.sync.dma_start(list2[:], offs2)
        nc.sync.dma_start(v_scale_rows[0:P:4, :].bitcast(I32), tab_scales.rearrange("a q t -> q a t").bitcast(I32))
        w2_raw = [load_w2(first, CHUNK) for first in (0, CHUNK)]
        v2_rows = tab2_scales[0].rearrange("(d r) t -> r d t", r=4)
        for r in range(4):
            queue = nc.scalar if r else nc.gpsimd
            queue.dma_start(v2_scale_rows[V2_ROW + r : P : 32, :].bitcast(I32), v2_rows[r].bitcast(I32))
        for a in range(2):
            rows = w1_scales[a].rearrange("q (g c) -> (q g) c", g=GROUPS)
            nc.sync.dma_start(w1_scale_rows[2 * a : P : 4, :].bitcast(I32), rows.bitcast(I32))
        v2_words = load_table(tab2_words[0], "v2_words")
        w1_raw = {}
        load_w1(0, 0, 1)
        load_w1(1, 0, 2)

        move_rows(v_plane, pick_bytes(held([P, S], U8, "v_scale"), v_scale_rows, list1, 0), 4)
        v_words = [load_table(tab_words[0], "v_words0")]
        w1_scale_dealt = held([P, PASS], U8, "w1_scale_dealt")
        nc.vector.tensor_copy(
            w1_scale_dealt[:].rearrange("p (t m) -> p t m", t=PACK),
            w1_scale_rows[:].rearrange("p (m t) -> p t m", t=PACK),
        )
        move_rows(w1_plane, w1_scale_dealt, 2)
        v2_scale = [pick_bytes(held([P, BLOCK], U8, "v2_scale0"), v2_scale_rows, list2, 0)[:]]
        load_w1(0, 1, 1)
        v_words.append(load_table(tab_words[1], "v_words1"))
        w2_raw.extend(load_w2(first, CHUNK) for first in (PASS, PASS + CHUNK))
        w3_codes = held([P, GROUPS, N], U32, "w3_codes")
        nc.sync.dma_start(w3_codes[:].bitcast(I32), w3_words.rearrange("a p c i -> p a (c i)").bitcast(I32))
        for d in range(4):
            rows = slice(32 * d + W3_ROW, 32 * d + W3_ROW + 8)
            nc.sync.dma_start(w3_scale[rows, :].bitcast(I32), w3_scales[:, 4 * d : 4 * d + 4, :].bitcast(I32))

        w2_grouped = [held([P, PACK, P, PACK], BF16, "w2_grouped0"), placed([P, PACK, P, PACK], BF16, "w2_grouped1", GROUPED)]
        for chunk in range(2):
            round_w2(w2_raw[chunk], CHUNK * chunk, on_scalar)
        w2_mx = [quantise_w2(0)]
        v2_codes = [held([P, BLOCK], U32, f"v2_codes{block}")[:] for block in range(2)]
        for half in range(2):
            pick_words(v2_codes[0][:, UNIT * half : UNIT * (half + 1)], v2_words, list2, UNIT * half)
        pick_words(v2_codes[1], v2_words, list2, BLOCK)

        w1_codes = {}
        deal_w1_codes(0, 0, nc.scalar.copy, held([P, 2 * PASS], U8, "w1_codes0_0"))
        deal_w1_codes(0, 1, nc.gpsimd.tensor_copy, held([P, 2 * PASS], U8, "w1_codes0_1"))
        for a in (1, 0):
            deal_w1_codes(1, a, nc.gpsimd.tensor_copy, held([P, 2 * PASS], U8, f"w1_codes1_{a}"))

        def mast_pass(acc, g, t, first, width):
            codes, scale = w2_mx[g]
            cols = slice(P * t, P * (t + 1))
            block, at = divmod(first, BLOCK)
            nc.tensor.matmul_mx(
                out=acc,
                lhsT=codes[:, cols].bitcast(FP8X4),
                lhsT_scale=scale[:, cols],
                rhs=v2_codes[block][:, at : at + width].bitcast(FP8X4),
                rhs_scale=v2_scale[block][V2_ROW:P, at : at + width],
                start=True,
                stop=True,
            )

        def square(step, pair, number, tag=""):
            g, block = divmod(step, BLOCKS)
            if pair == 0:
                step_squares[step] = held([P, 2, BLOCK, 2], F32, f"squares{step}", tag)
            b = bank([P, 2, BLOCK], "b", number)
            for u in range(2):
                mast_pass(b[:, u, :], g, 2 * pair + u, BLOCK * block, BLOCK)
            nc.scalar.activation(step_squares[step][:, pair, :, :], b[:].rearrange("p u n -> p n u"), ACT.Square)

        def exponential(step, tag=""):
            share = held([P, BLOCK, 2, 2], F32, f"share{step}", tag)
            nc.scalar.activation(share[:], step_squares[step][:].rearrange("p h n u -> p n h u"), ACT.Exp, scale=-1.0)
            for half in range(2):
                shares[2 * step + half] = share[:, UNIT * half : UNIT * (half + 1), :, :].rearrange("p n h u -> p n (h u)")

        def square_unit(unit, number):
            g, at = divmod(unit, 2 * BLOCKS)
            b = bank([P, PACK, UNIT], "b", number)
            for t in range(PACK):
                mast_pass(b[:, t, :], g, t, UNIT * at, UNIT)
            unit_squares[unit] = held([P, UNIT, PACK], F32, f"squares_unit{unit}")
            nc.scalar.activation(unit_squares[unit][:], b[:].rearrange("p t n -> p n t"), ACT.Square)

        def exponential_unit(unit):
            share = held([P, UNIT, PACK], F32, f"share_unit{unit}")
            nc.scalar.activation(share[:], unit_squares[unit][:], ACT.Exp, scale=-1.0)
            shares[unit] = share[:]

        def rotor_pass(unit, a, start, stop):
            g, first = unit // 8, UNIT * (unit % 8)
            block, at = divmod(first, BLOCK)
            for t in range(PACK):
                nc.tensor.matmul_mx(
                    out=rotor[unit][:, t, :],
                    lhsT=w1_codes[g, a][:, 2 * P * t : 2 * P * (t + 1)].bitcast(FP4X4),
                    lhsT_scale=w1_plane[:, PASS * (2 * g + a) + P * t : PASS * (2 * g + a) + P * (t + 1)],
                    rhs=v_codes[a, block][:, at : at + UNIT].bitcast(FP8X4),
                    rhs_scale=v_plane[:, S * a + first : S * a + first + UNIT],
                    start=(start and t == 0),
                    stop=(stop and t == PACK - 1),
                )

        def rotor_unit(unit, number):
            rotor[unit] = bank([P, PACK, UNIT], "a", number)
            rotor_pass(unit, 0, True, False)
            rotor_pass(unit, 1, False, True)

        def correct(unit):
            nc.vector.scalar_tensor_tensor(
                out=minus_h[unit],
                in0=shares[unit],
                scalar=1.0,
                in1=rotor[unit][:].rearrange("p t n -> p n t"),
                op0=ALU.subtract,
                op1=ALU.mult,
            )

        def quantise_h(tile, first, count, tag="", offset=None):
            shape, name = [P, UNIT * count], f"h_scale{first}"
            scale = held(shape, U8, name, tag) if offset is None else placed(shape, U8, name, offset)
            codes = held(shape, U32, f"h_codes{first}")
            for u in range(count):
                h_mx[first + u] = (codes, scale, UNIT * u)
            nc.vector.quantize_mx(
                out=codes[:].bitcast(FP8X4),
                scales=scale[:],
                in_=tile.rearrange("p u n t -> p (u n t)"),
            )

        def out_pass(acc, row_tile, g, first, width, start, stop):
            cols = slice(P * row_tile, P * (row_tile + 1))
            codes, scale, at = h_mx[2 * BLOCKS * g + first // UNIT]
            nc.tensor.matmul_mx(
                out=acc,
                lhsT=w3_codes[:, g, cols].bitcast(FP8X4),
                lhsT_scale=w3_scale[W3_ROW + 4 * g : P, cols],
                rhs=codes[:, at : at + width].bitcast(FP8X4),
                rhs_scale=scale[:, at : at + width],
                start=start,
                stop=stop,
            )

        def store(acc, pair, first, width, on_vector):
            result = held([P, 2, width], F32, f"result{first}_{pair}")
            if on_vector:
                nc.vector.tensor_scalar_mul(result[:], acc[:], -1.0)
            else:
                nc.scalar.activation(result[:], acc[:], ACT.Copy, scale=-1.0)
            rows = out[2 * P * pair : 2 * P * (pair + 1), first : first + width]
            nc.sync.dma_start(rows.rearrange("(u p) c -> p u c", p=P), result[:])

        def multiply_out(block, pair, number):
            acc = bank([P, 2, BLOCK], "out", number)
            for g in range(GROUPS):
                for u in range(2):
                    out_pass(acc[:, u, :], 2 * pair + u, g, BLOCK * block, BLOCK, g + u == 0, g + u == 2)
            return acc

        def pick_v_half(a, half, tile):
            pick_words(tile[:], v_words[a], list1, HALF * half)
            for block in range(2):
                v_codes[a, 2 * half + block] = tile[:, BLOCK * block : BLOCK * (block + 1)]

        def h_tile(first, count, tag="", offset=None):
            shape = [P, count, UNIT, PACK]
            tile = held(shape, BF16, f"h{first}", tag) if offset is None else placed(shape, BF16, f"h{first}", offset)
            for u in range(count):
                minus_h[first + u] = tile[:, u, :, :]
            return tile[:]

        shares, rotor, step_squares, unit_squares, minus_h, v_codes, h_mx = {}, {}, {}, {}, {}, {}, {}
        v2_scale.append(pick_bytes(held([P, BLOCK], U8, "v2_scale1"), v2_scale_rows, list2, BLOCK)[:])
        square_unit(0, 0)
        square_unit(1, 1)
        exponential_unit(0)
        square(1, 0, 2)
        exponential_unit(1)
        square(1, 1, 3)
        late_scale = pick_bytes(held([P, HALF], U8, "v2_scale2"), v2_scale_rows, list2, HALF)
        v2_scale.extend(late_scale[:, BLOCK * half : BLOCK * (half + 1)] for half in range(2))
        late_codes = held([P, HALF], U32, "v2_codes2")
        pick_words(late_codes[:], v2_words, list2, HALF)
        v2_codes.extend(late_codes[:, BLOCK * half : BLOCK * (half + 1)] for half in range(2))
        pick_v_half(0, 0, held([P, HALF], U32, "v_codes0_0"))
        square(2, 0, 4)
        exponential(1)
        square(2, 1, 5)
        for unit in range(AHEAD):
            rotor[unit] = bank([P, PACK, UNIT], "a", unit)
            rotor_pass(unit, 0, True, False)
        pick_v_half(1, 0, held([P, HALF], U32, "v_codes1_0"))
        square(3, 0, 6)
        exponential(2)
        square(3, 1, 7)
        for unit in range(AHEAD):
            rotor_pass(unit, 1, False, True)
        exponential(3)
        rotor_unit(8, 4)
        rotor_unit(9, 5)
        h0 = h_tile(0, 4)
        for chunk in (2, 3):
            round_w2(w2_raw[chunk], CHUNK * chunk, nc.vector.tensor_copy)
        correct(0)
        w2_mx.append(quantise_w2(1))
        correct(1)
        square_unit(8, 0)
        square_unit(9, 1)
        correct(2)
        correct(3)
        for a in range(2):
            pick_v_half(a, 1, placed([P, HALF], U32, f"v_codes{a}_1", GROUPED + 4 * HALF * a))
        exponential_unit(8)
        square(5, 0, 2)
        exponential_unit(9)
        square(5, 1, 3)
        rotor_unit(10, 0)
        rotor_unit(11, 1)
        rotor_unit(4, 6)
        rotor_unit(5, 7)
        square(6, 0, 2)
        exponential(5)
        square(6, 1, 3)
        h8, h10, h12, h6 = (h_tile(first, 2) for first in (8, 10, 12, 6))
        correct(8)
        correct(9)
        quantise_h(h0, 0, 4, "squares_unit9")
        quantise_h(h8, 8, 2)
        h4 = h_tile(4, 2, "w2_raw768")
        correct(4)
        correct(5)
        accs = [multiply_out(0, pair, 4 + pair) for pair in range(2)]
        square_unit(14, 2)
        rotor_unit(6, 6)
        rotor_unit(7, 7)
        for pair in range(2):
            store(accs[pair], pair, 0, BLOCK, False)
        rotor_unit(12, 4)
        rotor_unit(13, 5)
        exponential(6)
        square_unit(15, 3)
        correct(10)
        quantise_h(h4, 4, 2, "squares5")
        correct(11)
        correct(6)
        quantise_h(h10, 10, 2)
        accs = [multiply_out(1, pair, pair) for pair in range(2)]
        for pair in range(2):
            store(accs[pair], pair, BLOCK, BLOCK, False)
            exponential_unit(14 + pair)
        rotor_unit(14, 2)
        rotor_unit(15, 3)
        correct(7)
        correct(12)
        correct(13)
        quantise_h(h6, 6, 2)
        quantise_h(h12, 12, 2)
        accs = [multiply_out(2, pair, 4 + pair) for pair in range(2)]
        last = [h_tile(unit, 1) for unit in (14, 15)]
        correct(14)
        correct(15)
        quantise_h(last[0], 14, 1)
        quantise_h(last[1], 15, 1)
        for pair in range(2):
            store(accs[pair], pair, 2 * BLOCK, BLOCK, False)
        for half in range(2):
            first = S - BLOCK + UNIT * half
            accs = [bank([P, 2, UNIT], "out_tail", ((6, 7), (0, 1))[half][pair]) for pair in range(2)]
            for g in range(GROUPS):
                for pair in range(2):
                    for u in range(2):
                        out_pass(accs[pair][:, u, :], 2 * pair + u, g, first, UNIT, g + u == 0, g + u == 2)
            for pair in range(2):
                store(accs[pair], pair, first, UNIT, pair == 0)
